import numpy as np
import ml_dtypes


def mxq(x, axis, fmt="e4m3"):
    dtype, down = {"e4m3": (ml_dtypes.float8_e4m3fn, 7), "e5m2": (ml_dtypes.float8_e5m2, 14)}[fmt]
    v = np.moveaxis(np.asarray(x, np.float32).astype(ml_dtypes.bfloat16).astype(np.float64), axis, -1)
    blocks = v.reshape(v.shape[:-1] + (-1, 32))
    amax = np.abs(blocks).max(-1, keepdims=True)
    byte = np.maximum(np.where(amax > 0, np.frexp(amax)[1] - 1 + 127, 0) - down, 1)
    scale = np.exp2(byte - 127.0)
    codes = (blocks / scale).astype(np.float32).astype(dtype).astype(np.float64)
    return np.moveaxis((codes * scale).reshape(v.shape), -1, axis)


WIDE = False


def mx_kscale(k):
    if not WIDE:
        return np.ones(k)
    levels = np.array([10, -10, 5, -5, 0])
    if k % 512:
        return np.exp2(np.random.permutation(np.resize(levels, k // 32))).repeat(32)
    a = np.empty((k // 512, 16))
    for p in range(k // 512):
        a[p, :8] = np.random.permutation(np.resize(levels, 8))
        for g in range(8):
            far = levels[np.abs(levels - a[p, g]) >= 10]
            a[p, g + 8] = far[np.random.randint(len(far))]
    return np.exp2(a.ravel()).repeat(32)


def f64(x):
    return np.asarray(x).astype(np.float64)


def striped(idx):
    return np.tile(idx.reshape(-1, 16).T, (8, 1)).astype(np.uint16)


def unstriped(offs):
    return offs[:16].T.reshape(-1).astype(np.int64)


E2M1 = np.array([0.0, 0.5, 1.0, 1.5, 2.0, 3.0, 4.0, 6.0, -0.0, -0.5, -1.0, -1.5, -2.0, -3.0, -4.0, -6.0])


def pack_weight(w, fmt):
    k, n = w.shape
    w = f64(np.asarray(w, np.float32).astype(ml_dtypes.bfloat16)).reshape(k // 32, 32, n)
    amax = np.abs(w).max(1)
    if fmt == "e4m3":
        byte = np.frexp(amax)[1] - 1 + 127 - 7
    else:
        mant, ex = np.frexp(amax / 6.0)
        byte = np.where(mant > 0.5, ex, ex - 1) + 127
    byte = np.clip(np.where(amax > 0, byte, 1), 1, 254)
    scaled = (w * np.exp2(127.0 - byte)[:, None, :]).reshape(k, n).astype(np.float32)
    by_word = np.ascontiguousarray(scaled.reshape(k // 512, 128, 4, n).transpose(0, 1, 3, 2))
    if fmt == "e4m3":
        words = by_word.astype(ml_dtypes.float8_e4m3fn).view(np.uint8)
    else:
        c = by_word.astype(ml_dtypes.float4_e2m1fn).view(np.uint8) & 0xF
        words = (c[..., 0::2] | (c[..., 1::2] << 4)).reshape(k // 512, 128, 2 * n)
    return np.ascontiguousarray(words), np.ascontiguousarray(byte.astype(np.uint8).reshape(k // 512, 16, n))


def unpack_weight(words, scales, fmt):
    g, _, n = scales.shape
    words = np.ascontiguousarray(words).reshape(g, 128, n, -1)
    if fmt == "e4m3":
        vals = words.view(ml_dtypes.float8_e4m3fn).astype(np.float64)
    else:
        nib = np.empty((g, 128, n, 4), np.uint8)
        nib[..., 0::2] = words & 0xF
        nib[..., 1::2] = words >> 4
        vals = E2M1[nib]
    vals = vals * np.repeat(np.exp2(scales.astype(np.float64) - 127.0), 8, axis=1)[..., None]
    return vals.transpose(0, 1, 3, 2).reshape(g * 512, n)


def gelu(v):
    return 0.5 * v * (1.0 + np.tanh(np.sqrt(2.0 / np.pi) * (v + 0.044715 * v**3)))


K, H, T, S, T2, T3, S2, P = 512, 1024, 4096, 1024, 2048, 2048, 512, 1024

def setup_inputs():
    n = np.random.standard_normal
    s = mx_kscale(K)[:, None]
    u = mx_kscale(H)[:, None]
    tab_words, tab_scales = pack_weight(n((K, T)) * s, "e4m3")
    tab2_words, tab2_scales = pack_weight(n((H, T3)) / np.sqrt(H) / u, "e4m3")
    w4_words, w4_scales = pack_weight(n((K, H)) / np.sqrt(2 * K) / s * u.T, "e2m1")
    return {
        "tab_words": tab_words, "tab_scales": tab_scales,
        "tab2_words": tab2_words, "tab2_scales": tab2_scales,
        "w4_words": w4_words, "w4_scales": w4_scales,
        "w1": (n((K, H)) / np.sqrt(2 * K) / s * u.T).astype(np.float32),
        "c2": (0.4 * n(H) / u[:, 0]).astype(np.float32),
        "c3": (0.1 * np.exp(0.3 * n(H)) / u[:, 0] ** 2).astype(np.float32),
        "page0": (n((H, T2)) * u).astype(np.float32),
        "wgs": np.exp(0.3 * n((128, S))).astype(np.float32),
        "gain": (0.7 * np.exp(0.3 * n(S2))).astype(np.float32),
        "offs": striped(np.random.permutation(T)[:S]),
        "offs2": striped(np.random.permutation(T3)[:S2]),
        "offs3": striped(np.random.permutation(T2)[:S]),
        "offs4": striped(np.random.permutation(T2)[:P]),
    }

def reference(tab_words, tab_scales, tab2_words, tab2_scales, w4_words, w4_scales, w1, c2, c3, page0, wgs, gain, offs, offs2, offs3, offs4):
    v = unpack_weight(tab_words, tab_scales, "e4m3")[:, unstriped(offs)]
    v2 = unpack_weight(tab2_words, tab2_scales, "e4m3")[:, unstriped(offs2)]
    w4 = unpack_weight(w4_words, w4_scales, "e2m1")
    lin = w4.T @ v + mxq(f64(w1), 0, "e4m3").T @ v
    h = lin + np.square(lin) * (f64(c3)[:, None] * lin + f64(c2)[:, None])
    page = f64(page0).copy()
    page[:, unstriped(offs3)] = np.tile(f64(wgs), (H // 128, 1)) * h
    e = v2.T @ mxq(page, 0, "e4m3")
    x = e[:, unstriped(offs4)]
    return np.tanh(f64(gain)[:, None] * x)

@@ -1,0 +1,353 @@
+from contextlib import ExitStack
+
+import concourse.mybir as mybir
+
+K, H, T, S, T2, S2, PQ = 512, 1024, 4096, 1024, 2048, 512, 1024
+FLOPS = 2 * (2 * K * H * S) + 2 * H * S2 * T2
+
+F32 = mybir.dt.float32
+BF16 = mybir.dt.bfloat16
+I32 = mybir.dt.int32
+U32 = mybir.dt.uint32
+U16 = mybir.dt.uint16
+U8 = mybir.dt.uint8
+FP8X4 = mybir.dt.float8_e4m3fn_x4
+FP4X4 = mybir.dt.float4_e2m1fn_x4
+ACT = mybir.ActivationFunctionType
+MULT = mybir.AluOpType.mult
+ADD = mybir.AluOpType.add
+
+P = 128
+N = 512
+VECTOR_EVAC = ((0, 0), (0, 1))
+
+
+def tile_list_checkers_endgame_retrieval_kernel(
+    tc, tab_words, tab_scales, tab2_words, tab2_scales, w4_words, w4_scales, w1, c2, c3, page0, wgs, gain,
+    offs, offs2, offs3, offs4, out,
+):
+    nc = tc.nc
+    with ExitStack() as ctx:
+        lists = ctx.enter_context(tc.tile_pool(name="lists", bufs=1))
+        keep = ctx.enter_context(tc.tile_pool(name="keep", bufs=1))
+        big = ctx.enter_context(tc.tile_pool(name="big", bufs=1))
+        rows = ctx.enter_context(tc.tile_pool(name="rows", bufs=8))
+        poly = ctx.enter_context(tc.tile_pool(name="poly", bufs=3))
+        psum = ctx.enter_context(tc.psum_pool(name="psum", bufs=1))
+
+        idx = lists.tile([P, S // 16], U16, name="idx")
+        idx2 = lists.tile([P, S2 // 16], U16, name="idx2")
+        idx3 = lists.tile([P, S // 16], U16, name="idx3")
+        idx4 = lists.tile([P, PQ // 16], U16, name="idx4")
+
+        tab_s = keep.tile([P, T], U8, name="tab_s", align_bytes=64)
+        w4_s_raw = keep.tile([P, H], U8, name="w4_s_raw", tag="woven1", align_bytes=64)
+        tab2_s = keep.tile([P, T2], U8, name="tab2_s", align_bytes=64)
+        warm = keep.tile([P, 8], F32, name="warm")
+        nc.vector.memset(tab_s[:].bitcast(I32), 0)
+        nc.gpsimd.memset(w4_s_raw[:].bitcast(I32), 0)
+        nc.gpsimd.memset(tab2_s[:].bitcast(I32), 0)
+        nc.vector.memset(warm[:], 0.0)
+        nc.scalar.activation(warm[:, 0:1], warm[:, 1:2], ACT.Tanh)
+
+        w4_raw = keep.tile([P, 2 * H], U8, name="w4_raw", tag="woven0", align_bytes=64)
+        c2_t = keep.tile([P, 8], F32, name="c2_t", tag="woven_a", align_bytes=64)
+        c3_t = keep.tile([P, 8], F32, name="c3_t", tag="woven_b", align_bytes=64)
+        gain_t = keep.tile([P, 4], F32, name="gain_t")
+        w1_raw = [
+            big.tile([P, 4, N], F32, name="w1_raw0", tag="big2", align_bytes=64),
+            keep.tile([P, 4, N], F32, name="w1_raw1", tag="page_c1", align_bytes=64),
+        ]
+        tab_w = big.tile([P, T], I32, name="tab_w", tag="big0", align_bytes=64)
+        wg = [keep.tile([P, 2, S], F32, name="wg%d" % u) for u in range(2)]
+        pages = {}
+
+        def load_w1(a):
+            nc.sync.dma_start(w1_raw[a][:], w1[:, N * a : N * (a + 1)].rearrange("(p j) c -> p j c", j=4))
+
+        def load_wg(u):
+            src = wgs.rearrange("(q t) j -> q t j", t=4)[:, 2 * u : 2 * u + 2, :]
+            for g in (0, 2, 1, 3):
+                nc.sync.dma_start(wg[u][32 * g : 32 * (g + 1), :, :], src)
+
+        def load_page(i):
+            a, t = divmod(i, 4)
+            pages[i] = rows.tile([P, T2], F32, name="page%d" % i, tag="row")
+            nc.sync.dma_start(pages[i][:], page0[N * a : N * (a + 1), :].rearrange("(p t) c -> t p c", t=4)[t])
+
+        nc.sync.dma_start(idx[:], offs)
+        nc.sync.dma_start(w4_raw[:].bitcast(I32), w4_words[0].bitcast(I32))
+        load_w1(0)
+        nc.sync.dma_start(tab_w[:], tab_words[0].rearrange("p t i -> p (t i)").bitcast(I32))
+        for q in range(4):
+            nc.gpsimd.dma_start(w4_s_raw[32 * q : 32 * q + 4, :].bitcast(I32), w4_scales[0, 4 * q : 4 * q + 4, :].bitcast(I32))
+        for q in range(4):
+            nc.gpsimd.dma_start(tab_s[32 * q : 32 * q + 4, :].bitcast(I32), tab_scales[0, 4 * q : 4 * q + 4, :].bitcast(I32))
+        nc.sync.dma_start(c2_t[:].rearrange("p (a t) -> p a t", t=4), c2.rearrange("(a p t) -> p a t", a=2, t=4))
+        nc.sync.dma_start(c3_t[:].rearrange("p (a t) -> p a t", t=4), c3.rearrange("(a p t) -> p a t", a=2, t=4))
+        nc.sync.dma_start(idx3[:], offs3)
+        load_page(0)
+        load_wg(0)
+        load_page(1)
+        nc.sync.dma_start(idx2[:], offs2)
+        for q in range(4):
+            nc.sync.dma_start(tab2_s[32 * q : 32 * q + 8, :].bitcast(I32), tab2_scales[:, 4 * q : 4 * q + 4, :].bitcast(I32))
+        tab2_w = big.tile([P, 2 * T2], I32, name="tab2_w", tag="big1", align_bytes=64)
+        for a in range(2):
+            nc.sync.dma_start(tab2_w[:, T2 * a : T2 * (a + 1)], tab2_words[a].rearrange("p t i -> p (t i)").bitcast(I32))
+        load_w1(1)
+        load_wg(1)
+        for i in range(2, 8):
+            load_page(i)
+        nc.sync.dma_start(idx4[:], offs4)
+        with nc.allow_non_contiguous_dma(reason="512 gains, one to a partition"):
+            nc.sync.dma_start(gain_t[:], gain.rearrange("(c p) -> p c", p=P))
+
+        w4_c = keep.tile([P, 2 * H], U8, name="w4_c", align_bytes=64)
+        w4_s = keep.tile([P, H], U8, name="w4_s", align_bytes=64)
+        nc.vector.tensor_copy(
+            w4_c[:].bitcast(U16).rearrange("p (a t m) -> p a t m", a=2, t=4),
+            w4_raw[:].bitcast(U16).rearrange("p (a m t) -> p a t m", a=2, t=4),
+        )
+        nc.vector.tensor_copy(
+            w4_s[:].rearrange("p (a t m) -> p a t m", a=2, t=4),
+            w4_s_raw[:].rearrange("p (a m t) -> p a t m", a=2, t=4),
+        )
+        w1_c = [keep.tile([P, N], U32, name="w1_c%d" % a, align_bytes=64) for a in range(2)]
+        w1_s = [keep.tile([P, N], U8, name="w1_s%d" % a, align_bytes=64) for a in range(2)]
+
+        def quantize_w1(a):
+            grouped = keep.tile([P, 4 * N], BF16, name="w1_g", tag="w1_g", align_bytes=64)
+            nc.scalar.copy(
+                grouped[:].rearrange("p (t m j) -> p m j t", t=4, j=4),
+                w1_raw[a][:].rearrange("p j (m t) -> p m j t", t=4),
+            )
+            nc.vector.quantize_mx(out=w1_c[a][:].bitcast(FP8X4), scales=w1_s[a][:], in_=grouped[:])
+
+        quantize_w1(0)
+
+        v_s = [keep.tile([P, N], U8, name="v_s%d" % h, align_bytes=64) for h in range(2)]
+        v_w = [keep.tile([P, N], U32, name="v_w%d" % h, align_bytes=64) for h in range(2)]
+        for h in range(2):
+            nc.vector.tensor_copy(v_s[h][:], tab_s[:].indirect(idx[:, 32 * h : 32 * (h + 1)]))
+            nc.vector.tensor_copy(v_w[h][:], tab_w[:].bitcast(U32).indirect(idx[:, 32 * h : 32 * (h + 1)]))
+
+        v2 = {}
+        v2_s = keep.tile([P, S2], U8, name="v2_s", align_bytes=64)
+
+        def gather_tab2():
+            v2_w = keep.tile([P, 2 * S2], U32, name="v2_w", tag="v2_w", align_bytes=64)
+            v2["w"] = v2_w
+            nc.vector.tensor_copy(v2_s[:], tab2_s[:].indirect(idx2[:]))
+            for a in range(2):
+                nc.vector.tensor_copy(v2_w[:, S2 * a : S2 * (a + 1)], tab2_w[:, T2 * a : T2 * (a + 1)].bitcast(U32).indirect(idx2[:]))
+
+        steps = [((2 * pair, h), (2 * pair + 1, h)) for pair in range(3) for h in range(2)]
+        steps.extend([((6, 0), (6, 1)), ((7, 0), (7, 1))])
+        held = {}
+
+        def first_product(d):
+            if d == 3:
+                sq = keep.tile([P, 2, N], F32, name="sq3", tag="w1_g", align_bytes=64)
+            else:
+                sq = poly.tile([P, 2, N], F32, name="sq")
+            if d == 6:
+                af = keep.tile([P, 2, N], F32, name="af6", tag="page_c01", align_bytes=64)
+            elif d == 0:
+                af = keep.tile([P, 2, N], F32, name="af0", tag="v2_w", align_bytes=64)
+            else:
+                af = poly.tile([P, 2, N], F32, name="af")
+            plain = []
+            for e, (i, h) in enumerate(steps[d]):
+                a, t = divmod(i, 4)
+                lin = psum.tile([P, N], F32, name="lin", tag="bank%d" % (2 * (d % 3) + e))
+                nc.tensor.matmul_mx(
+                    out=lin[:], lhsT=w4_c[:, 256 * i : 256 * (i + 1)].bitcast(FP4X4), lhsT_scale=w4_s[:, P * i : P * (i + 1)],
+                    rhs=v_w[h][:].bitcast(FP8X4), rhs_scale=v_s[h][:], start=True, stop=False,
+                )
+                nc.tensor.matmul_mx(
+                    out=lin[:], lhsT=w1_c[a][:, P * t : P * (t + 1)].bitcast(FP8X4), lhsT_scale=w1_s[a][:, P * t : P * (t + 1)],
+                    rhs=v_w[h][:].bitcast(FP8X4), rhs_scale=v_s[h][:], start=False, stop=True,
+                )
+                nc.scalar.activation(sq[:, e, :], lin[:], ACT.Square)
+                nc.scalar.activation(af[:, e, :], lin[:], ACT.Identity, bias=c2_t[:, i : i + 1], scale=c3_t[:, i : i + 1])
+                if e == 0 or d == 0:
+                    plain.append(lin)
+                else:
+                    ln = poly.tile([P, N], F32, name="ln", bufs=2)
+                    nc.scalar.copy(ln[:], lin[:])
+                    plain.append(ln)
+            held[d] = (sq, af, plain)
+
+        def factors(d):
+            (i0, h0), (i1, h1) = steps[d]
+            both = wg[i0 % 4 // 2]
+            if i0 == i1:
+                return both[:, i0 % 2, :].rearrange("p (e c) -> p e c", e=2)
+            return both[:, :, N * h0 : N * (h0 + 1)]
+
+        weighted = {}
+
+        cubics = {}
+
+        def cubic(d):
+            sq, af, plain = held[d]
+            hh = poly.tile([P, 2, N], F32, name="hh", bufs=2)
+            nc.gpsimd.tensor_tensor(hh[:], sq[:], af[:], MULT)
+            nc.vector.tensor_tensor(hh[:, 0, :], hh[:, 0, :], plain[0][:], ADD)
+            nc.gpsimd.tensor_tensor(hh[:, 1, :], hh[:, 1, :], plain[1][:], ADD)
+            cubics[d] = hh
+
+        def weigh(d):
+            if d < 7:
+                weighted[d] = held[d + 1][1]
+            else:
+                weighted[d] = keep.tile([P, 2, N], F32, name="last", tag="page_c00", align_bytes=64)
+            nc.gpsimd.tensor_tensor(weighted[d][:], cubics[d][:], factors(d), MULT)
+
+        def first_step():
+            sq, af, plain = held[0]
+            weighted[0] = af
+            for e, (i, h) in enumerate(steps[0]):
+                nc.vector.tensor_tensor(sq[:, e, :], sq[:, e, :], af[:, e, :], MULT)
+                nc.vector.tensor_tensor(sq[:, e, :], sq[:, e, :], plain[e][:], ADD)
+                nc.vector.tensor_tensor(af[:, e, :], sq[:, e, :], factors(0)[:, e, :], MULT)
+                nc.vector.tensor_copy(pages[i][:].indirect(idx3[:, 32 * h : 32 * (h + 1)]), af[:, e, :])
+
+        def scatter(d):
+            for e, (i, h) in enumerate(steps[d]):
+                nc.vector.tensor_copy(pages[i][:].indirect(idx3[:, 32 * h : 32 * (h + 1)]), weighted[d][:, e, :])
+
+        woven = {}
+        page_c = {}
+        page_s = {}
+
+        def woven_tile(a, c):
+            if (a, c) not in woven:
+                if a == 1 and c < 2:
+                    woven[a, c] = keep.tile([P, N, 4], BF16, name="woven", tag="woven%d" % c, align_bytes=64)[:]
+                else:
+                    if a == 1:
+                        both = big.tile([P, 2 * N, 4], BF16, name="woven3", tag="big2", align_bytes=64)
+                    else:
+                        both = keep.tile([P, 2 * N, 4], BF16, name="woven2", tag="woven_a" if c > 1 else "woven_b", align_bytes=64)
+                    woven[a, c // 2, "both"] = both[:]
+                    for e in range(2):
+                        woven[a, c - c % 2 + e] = both[:, N * e : N * (e + 1), :]
+            return woven[a, c]
+
+        stage = {}
+
+        def stage_page(i):
+            a, t = divmod(i, 4)
+            for half in range(2):
+                if t == 0:
+                    stage[a, half] = big.tile([P, 4, 2 * N], F32, name="stage", tag="big%d" % (1 + half - 2 * a * half), align_bytes=64)
+                nc.sync.dma_start(stage[a, half][:, t, :], pages[i][:, 2 * N * half : 2 * N * (half + 1)])
+
+        def weave(a, c, t0, t1, on_vector):
+            src = stage[a, c // 2][:, t0:t1, N * (c % 2) : N * (c % 2 + 1)].rearrange("p t (g i) -> p g t i", i=4)
+            dst = woven_tile(a, c)[:, :, t0:t1].rearrange("p (g i) t -> p g t i", i=4)
+            if on_vector:
+                nc.vector.tensor_copy(dst, src)
+            else:
+                nc.scalar.copy(dst, src)
+
+        def weave_half(a, half, t1):
+            woven_tile(a, 2 * half)
+            nc.scalar.copy(
+                woven[a, half, "both"][:, :, 0:t1].rearrange("p (g i) t -> p g t i", i=4),
+                stage[a, half][:, 0:t1, :].rearrange("p t (g i) -> p g t i", i=4),
+            )
+
+        def quantize_page(a, c):
+            if (a, c) not in page_c:
+                if a == 0:
+                    codes = keep.tile([P, 2 * N], U32, name="page_c", tag="page_c0%d" % (c // 2), align_bytes=64)
+                    for e in range(2):
+                        page_c[a, c - c % 2 + e] = codes[:, N * e : N * (e + 1)]
+                else:
+                    codes = keep.tile([P, 4 * N], U32, name="page_c1", tag="page_c1", align_bytes=64)
+                    for e in range(4):
+                        page_c[a, e] = codes[:, N * e : N * (e + 1)]
+            page_s[a, c] = keep.tile([P, N], U8, name="page_s%d%d" % (a, c), align_bytes=64)
+            nc.vector.quantize_mx(
+                out=page_c[a, c].bitcast(FP8X4), scales=page_s[a, c][:], in_=woven[a, c].rearrange("p c t -> p (c t)")
+            )
+
+        score = {}
+
+        def second_product(n, a, c):
+            if a == 0:
+                score[n, c] = psum.tile([P, N], F32, name="score", tag="bank%d" % (4 * (1 - n % 2) + c))
+            nc.tensor.matmul_mx(
+                out=score[n, c][:],
+                lhsT=v2["w"][:, S2 * a + P * n : S2 * a + P * (n + 1)].bitcast(FP8X4),
+                lhsT_scale=v2_s[4 * a : P, P * n : P * (n + 1)],
+                rhs=page_c[a, c].bitcast(FP8X4), rhs_scale=page_s[a, c][:], start=(a == 0), stop=(a == 1),
+            )
+
+        first_product(0)
+        first_product(1)
+        first_step()
+        cubic(1)
+        first_product(2)
+        quantize_w1(1)
+        gather_tab2()
+        for d in range(1, 8):
+            if d + 2 < 8:
+                first_product(d + 2)
+            if d + 1 < 8:
+                cubic(d + 1)
+            if d == 5:
+                weave_half(0, 1, 4)
+                weave_half(0, 0, 4)
+            weigh(d)
+            scatter(d)
+            for i, h in steps[d]:
+                if h == 1 and i < 7:
+                    stage_page(i)
+            if d == 5:
+                for c in (2, 3):
+                    quantize_page(0, c)
+                weave_half(1, 1, 2)
+            if d == 6:
+                for c in (0, 1):
+                    weave(1, c, 0, 3, False)
+
+        clock = keep.tile([P, 8], F32, name="clock")
+        nc.gpsimd.tensor_copy(clock[:, 0:1], pages[7][:, 0:1])
+        for n in range(2):
+            for c in (2, 3):
+                second_product(n, 0, c)
+        for c in (0, 1):
+            quantize_page(0, c)
+            for n in range(2):
+                second_product(n, 0, c)
+        nc.vector.tensor_copy(stage[1, 1][:, 3, :], pages[7][:, 2 * N : 4 * N])
+        for c in (0, 1):
+            nc.scalar.copy(woven[1, c][:, :, 3], pages[7][:, N * c : N * (c + 1)])
+        for c in (2, 3):
+            weave(1, c, 2, 4, True)
+        for c in (2, 3, 0, 1):
+            quantize_page(1, c)
+            for n in range(2):
+                second_product(n, 1, c)
+        e_sb = {}
+        for n in range(4):
+            e_sb[n] = rows.tile([P, T2], F32, name="e%d" % n, tag="row")
+            for c in (2, 3, 0, 1):
+                if (n, c) in VECTOR_EVAC:
+                    nc.vector.tensor_copy(e_sb[n][:, N * c : N * (c + 1)], score[n, c][:])
+                else:
+                    nc.scalar.copy(e_sb[n][:, N * c : N * (c + 1)], score[n, c][:])
+                if n + 2 < 4:
+                    second_product(n + 2, 0, c)
+                    second_product(n + 2, 1, c)
+        for n in range(4):
+            x = poly.tile([P, 2, N], F32, name="x", tag="af")
+            y = poly.tile([P, 2, N], F32, name="y", tag="sq")
+            for h in range(2):
+                nc.vector.tensor_copy(x[:, h, :], e_sb[n][:].indirect(idx4[:, 32 * h : 32 * (h + 1)]))
+                nc.scalar.activation(y[:, h, :], x[:, h, :], ACT.Tanh, scale=gain_t[:, n : n + 1])
+                nc.sync.dma_start(out[P * n : P * (n + 1), N * h : N * (h + 1)], y[:, h, :])

@@ -91,7 +91,7 @@ def tile_list_checkers_endgame_retrieval_kernel(
         load_page(1)
         nc.sync.dma_start(idx2[:], offs2)
         for q in range(4):
-            nc.sync.dma_start(tab2_s[32 * q : 32 * q + 8, :].bitcast(I32), tab2_scales[:, 4 * q : 4 * q + 4, :].bitcast(I32))
+            nc.gpsimd.dma_start(tab2_s[32 * q : 32 * q + 8, :].bitcast(I32), tab2_scales[:, 4 * q : 4 * q + 4, :].bitcast(I32))
         tab2_w = big.tile([P, 2 * T2], I32, name="tab2_w", tag="big1", align_bytes=64)
         for a in range(2):
             nc.sync.dma_start(tab2_w[:, T2 * a : T2 * (a + 1)], tab2_words[a].rearrange("p t i -> p (t i)").bitcast(I32))
@@ -194,8 +194,8 @@ def tile_list_checkers_endgame_retrieval_kernel(
             sq, af, plain = held[d]
             hh = poly.tile([P, 2, N], F32, name="hh", bufs=2)
             nc.gpsimd.tensor_tensor(hh[:], sq[:], af[:], MULT)
-            nc.vector.tensor_tensor(hh[:, 0, :], hh[:, 0, :], plain[0][:], ADD)
             nc.gpsimd.tensor_tensor(hh[:, 1, :], hh[:, 1, :], plain[1][:], ADD)
+            nc.vector.tensor_tensor(hh[:, 0, :], hh[:, 0, :], plain[0][:], ADD)
             cubics[d] = hh
 
         def weigh(d):
@@ -311,12 +311,11 @@ def tile_list_checkers_endgame_retrieval_kernel(
                 for c in (2, 3):
                     quantize_page(0, c)
                 weave_half(1, 1, 2)
-            if d == 6:
                 for c in (0, 1):
-                    weave(1, c, 0, 3, False)
+                    weave(1, c, 0, 2, False)
 
-        clock = keep.tile([P, 8], F32, name="clock")
-        nc.gpsimd.tensor_copy(clock[:, 0:1], pages[7][:, 0:1])
+        for half in range(2):
+            nc.vector.tensor_copy(stage[1, half][:, 3, :], pages[7][:, 2 * N * half : 2 * N * (half + 1)])
         for n in range(2):
             for c in (2, 3):
                 second_product(n, 0, c)
@@ -324,11 +323,8 @@ def tile_list_checkers_endgame_retrieval_kernel(
             quantize_page(0, c)
             for n in range(2):
                 second_product(n, 0, c)
-        nc.vector.tensor_copy(stage[1, 1][:, 3, :], pages[7][:, 2 * N : 4 * N])
-        for c in (0, 1):
-            nc.scalar.copy(woven[1, c][:, :, 3], pages[7][:, N * c : N * (c + 1)])
-        for c in (2, 3):
-            weave(1, c, 2, 4, True)
+        for c in range(4):
+            weave(1, c, 2, 4, c > 1)
         for c in (2, 3, 0, 1):
             quantize_page(1, c)
             for n in range(2):

@@ -42,11 +42,9 @@ def tile_list_checkers_endgame_retrieval_kernel(
 
         tab_s = keep.tile([P, T], U8, name="tab_s", align_bytes=64)
         w4_s_raw = keep.tile([P, H], U8, name="w4_s_raw", tag="woven1", align_bytes=64)
-        tab2_s = keep.tile([P, T2], U8, name="tab2_s", align_bytes=64)
         warm = keep.tile([P, 8], F32, name="warm")
         nc.vector.memset(tab_s[:].bitcast(I32), 0)
         nc.gpsimd.memset(w4_s_raw[:].bitcast(I32), 0)
-        nc.gpsimd.memset(tab2_s[:].bitcast(I32), 0)
         nc.vector.memset(warm[:], 0.0)
         nc.scalar.activation(warm[:, 0:1], warm[:, 1:2], ACT.Tanh)
 
@@ -89,13 +87,11 @@ def tile_list_checkers_endgame_retrieval_kernel(
         load_page(0)
         load_wg(0)
         load_page(1)
+        load_w1(1)
         nc.sync.dma_start(idx2[:], offs2)
-        for q in range(4):
-            nc.gpsimd.dma_start(tab2_s[32 * q : 32 * q + 8, :].bitcast(I32), tab2_scales[:, 4 * q : 4 * q + 4, :].bitcast(I32))
         tab2_w = big.tile([P, 2 * T2], I32, name="tab2_w", tag="big1", align_bytes=64)
         for a in range(2):
             nc.sync.dma_start(tab2_w[:, T2 * a : T2 * (a + 1)], tab2_words[a].rearrange("p t i -> p (t i)").bitcast(I32))
-        load_w1(1)
         load_wg(1)
         for i in range(2, 8):
             load_page(i)
@@ -113,6 +109,10 @@ def tile_list_checkers_endgame_retrieval_kernel(
             w4_s[:].rearrange("p (a t m) -> p a t m", a=2, t=4),
             w4_s_raw[:].rearrange("p (a m t) -> p a t m", a=2, t=4),
         )
+        tab2_s = keep.tile([P, T2], U8, name="tab2_s", tag="woven1", align_bytes=64)
+        nc.vector.memset(tab2_s[:].bitcast(I32), 0)
+        for q in range(4):
+            nc.gpsimd.dma_start(tab2_s[32 * q : 32 * q + 8, :].bitcast(I32), tab2_scales[:, 4 * q : 4 * q + 4, :].bitcast(I32))
         w1_c = [keep.tile([P, N], U32, name="w1_c%d" % a, align_bytes=64) for a in range(2)]
         w1_s = [keep.tile([P, N], U8, name="w1_s%d" % a, align_bytes=64) for a in range(2)]
 
@@ -133,11 +133,12 @@ def tile_list_checkers_endgame_retrieval_kernel(
             nc.vector.tensor_copy(v_w[h][:], tab_w[:].bitcast(U32).indirect(idx[:, 32 * h : 32 * (h + 1)]))
 
         v2 = {}
-        v2_s = keep.tile([P, S2], U8, name="v2_s", align_bytes=64)
 
         def gather_tab2():
             v2_w = keep.tile([P, 2 * S2], U32, name="v2_w", tag="v2_w", align_bytes=64)
+            v2_s = keep.tile([P, S2], U8, name="v2_s", tag="v2_s", align_bytes=64)
             v2["w"] = v2_w
+            v2["s"] = v2_s
             nc.vector.tensor_copy(v2_s[:], tab2_s[:].indirect(idx2[:]))
             for a in range(2):
                 nc.vector.tensor_copy(v2_w[:, S2 * a : S2 * (a + 1)], tab2_w[:, T2 * a : T2 * (a + 1)].bitcast(U32).indirect(idx2[:]))
@@ -147,14 +148,9 @@ def tile_list_checkers_endgame_retrieval_kernel(
         held = {}
 
         def first_product(d):
-            if d == 3:
-                sq = keep.tile([P, 2, N], F32, name="sq3", tag="w1_g", align_bytes=64)
-            else:
-                sq = poly.tile([P, 2, N], F32, name="sq")
+            sq = poly.tile([P, 2, N], F32, name="sq")
             if d == 6:
                 af = keep.tile([P, 2, N], F32, name="af6", tag="page_c01", align_bytes=64)
-            elif d == 0:
-                af = keep.tile([P, 2, N], F32, name="af0", tag="v2_w", align_bytes=64)
             else:
                 af = poly.tile([P, 2, N], F32, name="af")
             plain = []
@@ -174,7 +170,10 @@ def tile_list_checkers_endgame_retrieval_kernel(
                 if e == 0 or d == 0:
                     plain.append(lin)
                 else:
-                    ln = poly.tile([P, N], F32, name="ln", bufs=2)
+                    if d < 3:
+                        ln = keep.tile([P, N], F32, name="ln_early", tag=("v2_s", "v2_w")[d - 1], align_bytes=64)
+                    else:
+                        ln = poly.tile([P, N], F32, name="ln", bufs=2)
                     nc.scalar.copy(ln[:], lin[:])
                     plain.append(ln)
             held[d] = (sq, af, plain)
@@ -199,7 +198,9 @@ def tile_list_checkers_endgame_retrieval_kernel(
             cubics[d] = hh
 
         def weigh(d):
-            if d < 7:
+            if d == 1:
+                weighted[d] = keep.tile([P, 2, N], F32, name="second", tag="w1_g", align_bytes=64)
+            elif d < 7:
                 weighted[d] = held[d + 1][1]
             else:
                 weighted[d] = keep.tile([P, 2, N], F32, name="last", tag="page_c00", align_bytes=64)
@@ -283,7 +284,7 @@ def tile_list_checkers_endgame_retrieval_kernel(
             nc.tensor.matmul_mx(
                 out=score[n, c][:],
                 lhsT=v2["w"][:, S2 * a + P * n : S2 * a + P * (n + 1)].bitcast(FP8X4),
-                lhsT_scale=v2_s[4 * a : P, P * n : P * (n + 1)],
+                lhsT_scale=v2["s"][4 * a : P, P * n : P * (n + 1)],
                 rhs=page_c[a, c].bitcast(FP8X4), rhs_scale=page_s[a, c][:], start=(a == 0), stop=(a == 1),
             )
 
@@ -293,7 +294,6 @@ def tile_list_checkers_endgame_retrieval_kernel(
         cubic(1)
         first_product(2)
         quantize_w1(1)
-        gather_tab2()
         for d in range(1, 8):
             if d + 2 < 8:
                 first_product(d + 2)
@@ -303,6 +303,8 @@ def tile_list_checkers_endgame_retrieval_kernel(
                 weave_half(0, 1, 4)
                 weave_half(0, 0, 4)
             weigh(d)
+            if d == 1:
+                gather_tab2()
             scatter(d)
             for i, h in steps[d]:
                 if h == 1 and i < 7:

@@ -19,7 +19,13 @@ ADD = mybir.AluOpType.add
 
 P = 128
 N = 512
-VECTOR_EVAC = ((0, 0), (0, 1))
+LIST_HALF = N // 16
+ROW_TILES = H // P
+STEPS = ROW_TILES
+LAST = STEPS - 1
+STAGED_STEP = 5
+CHUNK_ORDER = (2, 3, 0, 1)
+VECTOR_EMPTIES = ((0, 0), (0, 1))
 
 
 def tile_list_checkers_endgame_retrieval_kernel(
@@ -31,7 +37,7 @@ def tile_list_checkers_endgame_retrieval_kernel(
         lists = ctx.enter_context(tc.tile_pool(name="lists", bufs=1))
         keep = ctx.enter_context(tc.tile_pool(name="keep", bufs=1))
         big = ctx.enter_context(tc.tile_pool(name="big", bufs=1))
-        rows = ctx.enter_context(tc.tile_pool(name="rows", bufs=8))
+        rows = ctx.enter_context(tc.tile_pool(name="rows", bufs=ROW_TILES))
         poly = ctx.enter_context(tc.tile_pool(name="poly", bufs=3))
         psum = ctx.enter_context(tc.psum_pool(name="psum", bufs=1))
 
@@ -40,188 +46,197 @@ def tile_list_checkers_endgame_retrieval_kernel(
         idx3 = lists.tile([P, S // 16], U16, name="idx3")
         idx4 = lists.tile([P, PQ // 16], U16, name="idx4")
 
-        tab_s = keep.tile([P, T], U8, name="tab_s", align_bytes=64)
-        w4_s_raw = keep.tile([P, H], U8, name="w4_s_raw", tag="woven1", align_bytes=64)
-        warm = keep.tile([P, 8], F32, name="warm")
-        nc.vector.memset(tab_s[:].bitcast(I32), 0)
-        nc.gpsimd.memset(w4_s_raw[:].bitcast(I32), 0)
-        nc.vector.memset(warm[:], 0.0)
-        nc.scalar.activation(warm[:, 0:1], warm[:, 1:2], ACT.Tanh)
+        def list_half(tile, h):
+            return tile[:, LIST_HALF * h : LIST_HALF * (h + 1)]
+
+        def scale_rows(tile, q, count=4):
+            return tile[32 * q : 32 * q + count, :].bitcast(I32)
+
+        tab_plane = keep.tile([P, T], U8, name="tab_plane", align_bytes=64)
+        w4_plane_raw = keep.tile([P, H], U8, name="w4_plane_raw", tag="woven1", align_bytes=64)
+        nc.vector.memset(tab_plane[:].bitcast(I32), 0)
+        nc.gpsimd.memset(w4_plane_raw[:].bitcast(I32), 0)
 
         w4_raw = keep.tile([P, 2 * H], U8, name="w4_raw", tag="woven0", align_bytes=64)
-        c2_t = keep.tile([P, 8], F32, name="c2_t", tag="woven_a", align_bytes=64)
-        c3_t = keep.tile([P, 8], F32, name="c3_t", tag="woven_b", align_bytes=64)
-        gain_t = keep.tile([P, 4], F32, name="gain_t")
+        c2_t = keep.tile([P, ROW_TILES], F32, name="c2_t", tag="woven_a", align_bytes=64)
+        c3_t = keep.tile([P, ROW_TILES], F32, name="c3_t", tag="woven_b", align_bytes=64)
+        gain_t = keep.tile([P, S2 // P], F32, name="gain_t")
         w1_raw = [
             big.tile([P, 4, N], F32, name="w1_raw0", tag="big2", align_bytes=64),
-            keep.tile([P, 4, N], F32, name="w1_raw1", tag="page_c1", align_bytes=64),
+            keep.tile([P, 4, N], F32, name="w1_raw1", tag="page_codes1", align_bytes=64),
         ]
         tab_w = big.tile([P, T], I32, name="tab_w", tag="big0", align_bytes=64)
-        wg = [keep.tile([P, 2, S], F32, name="wg%d" % u) for u in range(2)]
+        factor = [keep.tile([P, 2, S], F32, name="factor%d" % u) for u in range(2)]
         pages = {}
 
         def load_w1(a):
             nc.sync.dma_start(w1_raw[a][:], w1[:, N * a : N * (a + 1)].rearrange("(p j) c -> p j c", j=4))
 
-        def load_wg(u):
+        def load_factors(u):
             src = wgs.rearrange("(q t) j -> q t j", t=4)[:, 2 * u : 2 * u + 2, :]
             for g in (0, 2, 1, 3):
-                nc.sync.dma_start(wg[u][32 * g : 32 * (g + 1), :, :], src)
+                nc.sync.dma_start(factor[u][32 * g : 32 * (g + 1), :, :], src)
 
         def load_page(i):
             a, t = divmod(i, 4)
             pages[i] = rows.tile([P, T2], F32, name="page%d" % i, tag="row")
             nc.sync.dma_start(pages[i][:], page0[N * a : N * (a + 1), :].rearrange("(p t) c -> t p c", t=4)[t])
 
-        nc.sync.dma_start(idx[:], offs)
-        nc.sync.dma_start(w4_raw[:].bitcast(I32), w4_words[0].bitcast(I32))
+        tab_rows = keep.tile([P, T], U8, name="tab_rows", tag="page_codes00", align_bytes=64)
         load_w1(0)
+        nc.sync.dma_start(idx[:], offs)
+        for q in range(4):
+            nc.sync.dma_start(scale_rows(tab_rows, q), tab_scales[0, 4 * q : 4 * q + 4, :].bitcast(I32))
+        nc.sync.dma_start(w4_raw[:].bitcast(I32), w4_words[0].bitcast(I32))
+        w4_rows = keep.tile([P, H], U8, name="w4_rows", tag="page_codes01", align_bytes=64)
+        for q in range(4):
+            nc.sync.dma_start(scale_rows(w4_rows, q), w4_scales[0, 4 * q : 4 * q + 4, :].bitcast(I32))
         nc.sync.dma_start(tab_w[:], tab_words[0].rearrange("p t i -> p (t i)").bitcast(I32))
         for q in range(4):
-            nc.gpsimd.dma_start(w4_s_raw[32 * q : 32 * q + 4, :].bitcast(I32), w4_scales[0, 4 * q : 4 * q + 4, :].bitcast(I32))
-        for q in range(4):
-            nc.gpsimd.dma_start(tab_s[32 * q : 32 * q + 4, :].bitcast(I32), tab_scales[0, 4 * q : 4 * q + 4, :].bitcast(I32))
+            nc.vector.tensor_copy(scale_rows(tab_plane, q), scale_rows(tab_rows, q))
         nc.sync.dma_start(c2_t[:].rearrange("p (a t) -> p a t", t=4), c2.rearrange("(a p t) -> p a t", a=2, t=4))
         nc.sync.dma_start(c3_t[:].rearrange("p (a t) -> p a t", t=4), c3.rearrange("(a p t) -> p a t", a=2, t=4))
         nc.sync.dma_start(idx3[:], offs3)
         load_page(0)
-        load_wg(0)
+        load_factors(0)
         load_page(1)
         load_w1(1)
         nc.sync.dma_start(idx2[:], offs2)
         tab2_w = big.tile([P, 2 * T2], I32, name="tab2_w", tag="big1", align_bytes=64)
         for a in range(2):
             nc.sync.dma_start(tab2_w[:, T2 * a : T2 * (a + 1)], tab2_words[a].rearrange("p t i -> p (t i)").bitcast(I32))
-        load_wg(1)
-        for i in range(2, 8):
+        load_factors(1)
+        for i in range(2, ROW_TILES):
             load_page(i)
         nc.sync.dma_start(idx4[:], offs4)
         with nc.allow_non_contiguous_dma(reason="512 gains, one to a partition"):
             nc.sync.dma_start(gain_t[:], gain.rearrange("(c p) -> p c", p=P))
 
-        w4_c = keep.tile([P, 2 * H], U8, name="w4_c", align_bytes=64)
-        w4_s = keep.tile([P, H], U8, name="w4_s", align_bytes=64)
+        w4_codes = keep.tile([P, 2 * H], U8, name="w4_codes", align_bytes=64)
+        w4_plane = keep.tile([P, H], U8, name="w4_plane", align_bytes=64)
         nc.vector.tensor_copy(
-            w4_c[:].bitcast(U16).rearrange("p (a t m) -> p a t m", a=2, t=4),
+            w4_codes[:].bitcast(U16).rearrange("p (a t m) -> p a t m", a=2, t=4),
             w4_raw[:].bitcast(U16).rearrange("p (a m t) -> p a t m", a=2, t=4),
         )
-        nc.vector.tensor_copy(
-            w4_s[:].rearrange("p (a t m) -> p a t m", a=2, t=4),
-            w4_s_raw[:].rearrange("p (a m t) -> p a t m", a=2, t=4),
-        )
-        tab2_s = keep.tile([P, T2], U8, name="tab2_s", tag="woven1", align_bytes=64)
-        nc.vector.memset(tab2_s[:].bitcast(I32), 0)
         for q in range(4):
-            nc.gpsimd.dma_start(tab2_s[32 * q : 32 * q + 8, :].bitcast(I32), tab2_scales[:, 4 * q : 4 * q + 4, :].bitcast(I32))
-        w1_c = [keep.tile([P, N], U32, name="w1_c%d" % a, align_bytes=64) for a in range(2)]
-        w1_s = [keep.tile([P, N], U8, name="w1_s%d" % a, align_bytes=64) for a in range(2)]
+            nc.vector.tensor_copy(scale_rows(w4_plane_raw, q), scale_rows(w4_rows, q))
+        nc.vector.tensor_copy(
+            w4_plane[:].rearrange("p (a t m) -> p a t m", a=2, t=4),
+            w4_plane_raw[:].rearrange("p (a m t) -> p a t m", a=2, t=4),
+        )
+        tab2_plane = keep.tile([P, T2], U8, name="tab2_plane", tag="woven1", align_bytes=64)
+        nc.vector.memset(tab2_plane[:].bitcast(I32), 0)
+        for q in range(4):
+            nc.gpsimd.dma_start(scale_rows(tab2_plane, q, 8), tab2_scales[:, 4 * q : 4 * q + 4, :].bitcast(I32))
+        w1_codes = [keep.tile([P, N], U32, name="w1_codes%d" % a, align_bytes=64) for a in range(2)]
+        w1_plane = [keep.tile([P, N], U8, name="w1_plane%d" % a, align_bytes=64) for a in range(2)]
 
         def quantize_w1(a):
-            grouped = keep.tile([P, 4 * N], BF16, name="w1_g", tag="w1_g", align_bytes=64)
+            grouped = keep.tile([P, 4 * N], BF16, name="w1_grouped", tag="w1_grouped", align_bytes=64)
             nc.scalar.copy(
                 grouped[:].rearrange("p (t m j) -> p m j t", t=4, j=4),
                 w1_raw[a][:].rearrange("p j (m t) -> p m j t", t=4),
             )
-            nc.vector.quantize_mx(out=w1_c[a][:].bitcast(FP8X4), scales=w1_s[a][:], in_=grouped[:])
+            nc.vector.quantize_mx(out=w1_codes[a][:].bitcast(FP8X4), scales=w1_plane[a][:], in_=grouped[:])
 
         quantize_w1(0)
 
-        v_s = [keep.tile([P, N], U8, name="v_s%d" % h, align_bytes=64) for h in range(2)]
-        v_w = [keep.tile([P, N], U32, name="v_w%d" % h, align_bytes=64) for h in range(2)]
+        v_plane = [keep.tile([P, N], U8, name="v_plane%d" % h, align_bytes=64) for h in range(2)]
+        v_codes = [keep.tile([P, N], U32, name="v_codes%d" % h, align_bytes=64) for h in range(2)]
         for h in range(2):
-            nc.vector.tensor_copy(v_s[h][:], tab_s[:].indirect(idx[:, 32 * h : 32 * (h + 1)]))
-            nc.vector.tensor_copy(v_w[h][:], tab_w[:].bitcast(U32).indirect(idx[:, 32 * h : 32 * (h + 1)]))
+            nc.vector.tensor_copy(v_plane[h][:], tab_plane[:].indirect(list_half(idx, h)))
+            nc.vector.tensor_copy(v_codes[h][:], tab_w[:].bitcast(U32).indirect(list_half(idx, h)))
 
         v2 = {}
 
         def gather_tab2():
-            v2_w = keep.tile([P, 2 * S2], U32, name="v2_w", tag="v2_w", align_bytes=64)
-            v2_s = keep.tile([P, S2], U8, name="v2_s", tag="v2_s", align_bytes=64)
-            v2["w"] = v2_w
-            v2["s"] = v2_s
-            nc.vector.tensor_copy(v2_s[:], tab2_s[:].indirect(idx2[:]))
+            codes = keep.tile([P, 2 * S2], U32, name="v2_codes", tag="v2_codes", align_bytes=64)
+            plane = keep.tile([P, S2], U8, name="v2_plane", tag="v2_plane", align_bytes=64)
+            v2["codes"] = codes
+            v2["plane"] = plane
+            nc.vector.tensor_copy(plane[:], tab2_plane[:].indirect(idx2[:]))
             for a in range(2):
-                nc.vector.tensor_copy(v2_w[:, S2 * a : S2 * (a + 1)], tab2_w[:, T2 * a : T2 * (a + 1)].bitcast(U32).indirect(idx2[:]))
+                nc.vector.tensor_copy(codes[:, S2 * a : S2 * (a + 1)], tab2_w[:, T2 * a : T2 * (a + 1)].bitcast(U32).indirect(idx2[:]))
 
         steps = [((2 * pair, h), (2 * pair + 1, h)) for pair in range(3) for h in range(2)]
-        steps.extend([((6, 0), (6, 1)), ((7, 0), (7, 1))])
-        held = {}
+        steps.extend([((i, 0), (i, 1)) for i in (ROW_TILES - 2, ROW_TILES - 1)])
+        terms = {}
 
         def first_product(d):
-            sq = poly.tile([P, 2, N], F32, name="sq")
-            if d == 6:
-                af = keep.tile([P, 2, N], F32, name="af6", tag="page_c01", align_bytes=64)
+            square = poly.tile([P, 2, N], F32, name="square")
+            if d == STAGED_STEP + 1:
+                affine = keep.tile([P, 2, N], F32, name="affine_staged", tag="page_codes01", align_bytes=64)
             else:
-                af = poly.tile([P, 2, N], F32, name="af")
-            plain = []
+                affine = poly.tile([P, 2, N], F32, name="affine")
+            linear = []
             for e, (i, h) in enumerate(steps[d]):
                 a, t = divmod(i, 4)
                 lin = psum.tile([P, N], F32, name="lin", tag="bank%d" % (2 * (d % 3) + e))
                 nc.tensor.matmul_mx(
-                    out=lin[:], lhsT=w4_c[:, 256 * i : 256 * (i + 1)].bitcast(FP4X4), lhsT_scale=w4_s[:, P * i : P * (i + 1)],
-                    rhs=v_w[h][:].bitcast(FP8X4), rhs_scale=v_s[h][:], start=True, stop=False,
+                    out=lin[:], lhsT=w1_codes[a][:, P * t : P * (t + 1)].bitcast(FP8X4), lhsT_scale=w1_plane[a][:, P * t : P * (t + 1)],
+                    rhs=v_codes[h][:].bitcast(FP8X4), rhs_scale=v_plane[h][:], start=True, stop=False,
                 )
                 nc.tensor.matmul_mx(
-                    out=lin[:], lhsT=w1_c[a][:, P * t : P * (t + 1)].bitcast(FP8X4), lhsT_scale=w1_s[a][:, P * t : P * (t + 1)],
-                    rhs=v_w[h][:].bitcast(FP8X4), rhs_scale=v_s[h][:], start=False, stop=True,
+                    out=lin[:], lhsT=w4_codes[:, 2 * P * i : 2 * P * (i + 1)].bitcast(FP4X4), lhsT_scale=w4_plane[:, P * i : P * (i + 1)],
+                    rhs=v_codes[h][:].bitcast(FP8X4), rhs_scale=v_plane[h][:], start=False, stop=True,
                 )
-                nc.scalar.activation(sq[:, e, :], lin[:], ACT.Square)
-                nc.scalar.activation(af[:, e, :], lin[:], ACT.Identity, bias=c2_t[:, i : i + 1], scale=c3_t[:, i : i + 1])
+                nc.scalar.activation(square[:, e, :], lin[:], ACT.Square)
+                nc.scalar.activation(affine[:, e, :], lin[:], ACT.Identity, bias=c2_t[:, i : i + 1], scale=c3_t[:, i : i + 1])
                 if e == 0 or d == 0:
-                    plain.append(lin)
+                    linear.append(lin)
                 else:
-                    if d < 3:
-                        ln = keep.tile([P, N], F32, name="ln_early", tag=("v2_s", "v2_w")[d - 1], align_bytes=64)
+                    if d <= 2:
+                        lin_sb = keep.tile([P, N], F32, name="lin_early", tag=("v2_plane", "v2_codes")[d - 1], align_bytes=64)
                     else:
-                        ln = poly.tile([P, N], F32, name="ln", bufs=2)
-                    nc.scalar.copy(ln[:], lin[:])
-                    plain.append(ln)
-            held[d] = (sq, af, plain)
+                        lin_sb = poly.tile([P, N], F32, name="lin_sb", bufs=2)
+                    nc.scalar.copy(lin_sb[:], lin[:])
+                    linear.append(lin_sb)
+            terms[d] = (square, affine, linear)
 
         def factors(d):
-            (i0, h0), (i1, h1) = steps[d]
-            both = wg[i0 % 4 // 2]
-            if i0 == i1:
+            (i0, h0), second = steps[d]
+            both = factor[i0 % 4 // 2]
+            if i0 == second[0]:
                 return both[:, i0 % 2, :].rearrange("p (e c) -> p e c", e=2)
             return both[:, :, N * h0 : N * (h0 + 1)]
 
         weighted = {}
-
         cubics = {}
 
         def cubic(d):
-            sq, af, plain = held[d]
-            hh = poly.tile([P, 2, N], F32, name="hh", bufs=2)
-            nc.gpsimd.tensor_tensor(hh[:], sq[:], af[:], MULT)
-            nc.gpsimd.tensor_tensor(hh[:, 1, :], hh[:, 1, :], plain[1][:], ADD)
-            nc.vector.tensor_tensor(hh[:, 0, :], hh[:, 0, :], plain[0][:], ADD)
-            cubics[d] = hh
+            square, affine, linear = terms[d]
+            h_tile = poly.tile([P, 2, N], F32, name="h_tile", bufs=2)
+            nc.gpsimd.tensor_tensor(h_tile[:], square[:], affine[:], MULT)
+            nc.gpsimd.tensor_tensor(h_tile[:, 1, :], h_tile[:, 1, :], linear[1][:], ADD)
+            nc.vector.tensor_tensor(h_tile[:, 0, :], h_tile[:, 0, :], linear[0][:], ADD)
+            cubics[d] = h_tile
 
         def weigh(d):
             if d == 1:
-                weighted[d] = keep.tile([P, 2, N], F32, name="second", tag="w1_g", align_bytes=64)
-            elif d < 7:
-                weighted[d] = held[d + 1][1]
+                weighted[d] = keep.tile([P, 2, N], F32, name="weighted_second", tag="w1_grouped", align_bytes=64)
+            elif d < LAST:
+                weighted[d] = terms[d + 1][1]
             else:
-                weighted[d] = keep.tile([P, 2, N], F32, name="last", tag="page_c00", align_bytes=64)
+                weighted[d] = keep.tile([P, 2, N], F32, name="weighted_last", tag="page_codes00", align_bytes=64)
             nc.gpsimd.tensor_tensor(weighted[d][:], cubics[d][:], factors(d), MULT)
 
         def first_step():
-            sq, af, plain = held[0]
-            weighted[0] = af
+            square, affine, linear = terms[0]
             for e, (i, h) in enumerate(steps[0]):
-                nc.vector.tensor_tensor(sq[:, e, :], sq[:, e, :], af[:, e, :], MULT)
-                nc.vector.tensor_tensor(sq[:, e, :], sq[:, e, :], plain[e][:], ADD)
-                nc.vector.tensor_tensor(af[:, e, :], sq[:, e, :], factors(0)[:, e, :], MULT)
-                nc.vector.tensor_copy(pages[i][:].indirect(idx3[:, 32 * h : 32 * (h + 1)]), af[:, e, :])
+                nc.vector.tensor_tensor(square[:, e, :], square[:, e, :], affine[:, e, :], MULT)
+                nc.vector.tensor_tensor(square[:, e, :], square[:, e, :], linear[e][:], ADD)
+                nc.vector.tensor_tensor(affine[:, e, :], square[:, e, :], factors(0)[:, e, :], MULT)
+                nc.vector.tensor_copy(pages[i][:].indirect(list_half(idx3, h)), affine[:, e, :])
 
         def scatter(d):
             for e, (i, h) in enumerate(steps[d]):
-                nc.vector.tensor_copy(pages[i][:].indirect(idx3[:, 32 * h : 32 * (h + 1)]), weighted[d][:, e, :])
+                nc.vector.tensor_copy(pages[i][:].indirect(list_half(idx3, h)), weighted[d][:, e, :])
 
         woven = {}
-        page_c = {}
-        page_s = {}
+        woven_half = {}
+        page_codes = {}
+        page_plane = {}
+        stage = {}
 
         def woven_tile(a, c):
             if (a, c) not in woven:
@@ -229,21 +244,21 @@ def tile_list_checkers_endgame_retrieval_kernel(
                     woven[a, c] = keep.tile([P, N, 4], BF16, name="woven", tag="woven%d" % c, align_bytes=64)[:]
                 else:
                     if a == 1:
-                        both = big.tile([P, 2 * N, 4], BF16, name="woven3", tag="big2", align_bytes=64)
+                        both = big.tile([P, 2 * N, 4], BF16, name="woven_late", tag="big2", align_bytes=64)
                     else:
-                        both = keep.tile([P, 2 * N, 4], BF16, name="woven2", tag="woven_a" if c > 1 else "woven_b", align_bytes=64)
-                    woven[a, c // 2, "both"] = both[:]
+                        both = keep.tile([P, 2 * N, 4], BF16, name="woven_early", tag="woven_a" if c > 1 else "woven_b", align_bytes=64)
+                    woven_half[a, c // 2] = both[:]
                     for e in range(2):
                         woven[a, c - c % 2 + e] = both[:, N * e : N * (e + 1), :]
             return woven[a, c]
 
-        stage = {}
+        stage_buffer = {(0, 0): "big1", (0, 1): "big2", (1, 0): "big1", (1, 1): "big0"}
 
         def stage_page(i):
             a, t = divmod(i, 4)
             for half in range(2):
                 if t == 0:
-                    stage[a, half] = big.tile([P, 4, 2 * N], F32, name="stage", tag="big%d" % (1 + half - 2 * a * half), align_bytes=64)
+                    stage[a, half] = big.tile([P, 4, 2 * N], F32, name="stage", tag=stage_buffer[a, half], align_bytes=64)
                 nc.sync.dma_start(stage[a, half][:, t, :], pages[i][:, 2 * N * half : 2 * N * (half + 1)])
 
         def weave(a, c, t0, t1, on_vector):
@@ -257,23 +272,23 @@ def tile_list_checkers_endgame_retrieval_kernel(
         def weave_half(a, half, t1):
             woven_tile(a, 2 * half)
             nc.scalar.copy(
-                woven[a, half, "both"][:, :, 0:t1].rearrange("p (g i) t -> p g t i", i=4),
+                woven_half[a, half][:, :, 0:t1].rearrange("p (g i) t -> p g t i", i=4),
                 stage[a, half][:, 0:t1, :].rearrange("p t (g i) -> p g t i", i=4),
             )
 
         def quantize_page(a, c):
-            if (a, c) not in page_c:
+            if (a, c) not in page_codes:
                 if a == 0:
-                    codes = keep.tile([P, 2 * N], U32, name="page_c", tag="page_c0%d" % (c // 2), align_bytes=64)
+                    codes = keep.tile([P, 2 * N], U32, name="page_codes0", tag="page_codes0%d" % (c // 2), align_bytes=64)
                     for e in range(2):
-                        page_c[a, c - c % 2 + e] = codes[:, N * e : N * (e + 1)]
+                        page_codes[a, c - c % 2 + e] = codes[:, N * e : N * (e + 1)]
                 else:
-                    codes = keep.tile([P, 4 * N], U32, name="page_c1", tag="page_c1", align_bytes=64)
+                    codes = keep.tile([P, 4 * N], U32, name="page_codes1", tag="page_codes1", align_bytes=64)
                     for e in range(4):
-                        page_c[a, e] = codes[:, N * e : N * (e + 1)]
-            page_s[a, c] = keep.tile([P, N], U8, name="page_s%d%d" % (a, c), align_bytes=64)
+                        page_codes[a, e] = codes[:, N * e : N * (e + 1)]
+            page_plane[a, c] = keep.tile([P, N], U8, name="page_plane%d%d" % (a, c), align_bytes=64)
             nc.vector.quantize_mx(
-                out=page_c[a, c].bitcast(FP8X4), scales=page_s[a, c][:], in_=woven[a, c].rearrange("p c t -> p (c t)")
+                out=page_codes[a, c].bitcast(FP8X4), scales=page_plane[a, c][:], in_=woven[a, c].rearrange("p c t -> p (c t)")
             )
 
         score = {}
@@ -283,9 +298,9 @@ def tile_list_checkers_endgame_retrieval_kernel(
                 score[n, c] = psum.tile([P, N], F32, name="score", tag="bank%d" % (4 * (1 - n % 2) + c))
             nc.tensor.matmul_mx(
                 out=score[n, c][:],
-                lhsT=v2["w"][:, S2 * a + P * n : S2 * a + P * (n + 1)].bitcast(FP8X4),
-                lhsT_scale=v2["s"][4 * a : P, P * n : P * (n + 1)],
-                rhs=page_c[a, c].bitcast(FP8X4), rhs_scale=page_s[a, c][:], start=(a == 0), stop=(a == 1),
+                lhsT=v2["codes"][:, S2 * a + P * n : S2 * a + P * (n + 1)].bitcast(FP8X4),
+                lhsT_scale=v2["plane"][4 * a : P, P * n : P * (n + 1)],
+                rhs=page_codes[a, c].bitcast(FP8X4), rhs_scale=page_plane[a, c][:], start=(a == 0), stop=(a == 1),
             )
 
         first_product(0)
@@ -294,12 +309,12 @@ def tile_list_checkers_endgame_retrieval_kernel(
         cubic(1)
         first_product(2)
         quantize_w1(1)
-        for d in range(1, 8):
-            if d + 2 < 8:
+        for d in range(1, STEPS):
+            if d + 2 < STEPS:
                 first_product(d + 2)
-            if d + 1 < 8:
+            if d + 1 < STEPS:
                 cubic(d + 1)
-            if d == 5:
+            if d == STAGED_STEP:
                 weave_half(0, 1, 4)
                 weave_half(0, 0, 4)
             weigh(d)
@@ -307,9 +322,9 @@ def tile_list_checkers_endgame_retrieval_kernel(
                 gather_tab2()
             scatter(d)
             for i, h in steps[d]:
-                if h == 1 and i < 7:
+                if h == 1 and i < ROW_TILES - 1:
                     stage_page(i)
-            if d == 5:
+            if d == STAGED_STEP:
                 for c in (2, 3):
                     quantize_page(0, c)
                 weave_half(1, 1, 2)
@@ -317,7 +332,7 @@ def tile_list_checkers_endgame_retrieval_kernel(
                     weave(1, c, 0, 2, False)
 
         for half in range(2):
-            nc.vector.tensor_copy(stage[1, half][:, 3, :], pages[7][:, 2 * N * half : 2 * N * (half + 1)])
+            nc.vector.tensor_copy(stage[1, half][:, 3, :], pages[ROW_TILES - 1][:, 2 * N * half : 2 * N * (half + 1)])
         for n in range(2):
             for c in (2, 3):
                 second_product(n, 0, c)
@@ -327,25 +342,26 @@ def tile_list_checkers_endgame_retrieval_kernel(
                 second_product(n, 0, c)
         for c in range(4):
             weave(1, c, 2, 4, c > 1)
-        for c in (2, 3, 0, 1):
+        for c in CHUNK_ORDER:
             quantize_page(1, c)
             for n in range(2):
                 second_product(n, 1, c)
-        e_sb = {}
-        for n in range(4):
-            e_sb[n] = rows.tile([P, T2], F32, name="e%d" % n, tag="row")
-            for c in (2, 3, 0, 1):
-                if (n, c) in VECTOR_EVAC:
-                    nc.vector.tensor_copy(e_sb[n][:, N * c : N * (c + 1)], score[n, c][:])
+
+        score_sb = {}
+        for n in range(S2 // P):
+            score_sb[n] = rows.tile([P, T2], F32, name="score_sb%d" % n, tag="row")
+            for c in CHUNK_ORDER:
+                if (n, c) in VECTOR_EMPTIES:
+                    nc.vector.tensor_copy(score_sb[n][:, N * c : N * (c + 1)], score[n, c][:])
                 else:
-                    nc.scalar.copy(e_sb[n][:, N * c : N * (c + 1)], score[n, c][:])
-                if n + 2 < 4:
+                    nc.scalar.copy(score_sb[n][:, N * c : N * (c + 1)], score[n, c][:])
+                if n + 2 < S2 // P:
                     second_product(n + 2, 0, c)
                     second_product(n + 2, 1, c)
-        for n in range(4):
-            x = poly.tile([P, 2, N], F32, name="x", tag="af")
-            y = poly.tile([P, 2, N], F32, name="y", tag="sq")
+        for n in range(S2 // P):
+            picked = poly.tile([P, 2, N], F32, name="picked", tag="affine")
+            result = poly.tile([P, 2, N], F32, name="result", tag="square")
             for h in range(2):
-                nc.vector.tensor_copy(x[:, h, :], e_sb[n][:].indirect(idx4[:, 32 * h : 32 * (h + 1)]))
-                nc.scalar.activation(y[:, h, :], x[:, h, :], ACT.Tanh, scale=gain_t[:, n : n + 1])
-                nc.sync.dma_start(out[P * n : P * (n + 1), N * h : N * (h + 1)], y[:, h, :])
+                nc.vector.tensor_copy(picked[:, h, :], score_sb[n][:].indirect(list_half(idx4, h)))
+                nc.scalar.activation(result[:, h, :], picked[:, h, :], ACT.Tanh, scale=gain_t[:, n : n + 1])
+                nc.sync.dma_start(out[P * n : P * (n + 1), N * h : N * (h + 1)], result[:, h, :])

@@ -21,11 +21,20 @@ P = 128
 N = 512
 LIST_HALF = N // 16
 ROW_TILES = H // P
-STEPS = ROW_TILES
-LAST = STEPS - 1
-STAGED_STEP = 5
-CHUNK_ORDER = (2, 3, 0, 1)
-VECTOR_EMPTIES = ((0, 0), (0, 1))
+LAST = ROW_TILES - 1
+KIB = 1024
+SCALAR_COLUMNS = 1024
+
+PAGES = 0
+FACTOR = PAGES + 64 * KIB
+SQUARE = FACTOR + 16 * KIB
+CUBIC = SQUARE + 12 * KIB
+LINEAR = CUBIC + 8 * KIB
+AFFINE = LINEAR + 16 * KIB
+TAB2 = AFFINE + 21 * KIB
+STAGE0 = TAB2 + 16 * KIB
+STAGE1 = STAGE0 + 32 * KIB
+SMALL = STAGE1 + 24 * KIB
 
 
 def tile_list_checkers_endgame_retrieval_kernel(
@@ -36,10 +45,11 @@ def tile_list_checkers_endgame_retrieval_kernel(
     with ExitStack() as ctx:
         lists = ctx.enter_context(tc.tile_pool(name="lists", bufs=1))
         keep = ctx.enter_context(tc.tile_pool(name="keep", bufs=1))
-        big = ctx.enter_context(tc.tile_pool(name="big", bufs=1))
-        rows = ctx.enter_context(tc.tile_pool(name="rows", bufs=ROW_TILES))
-        poly = ctx.enter_context(tc.tile_pool(name="poly", bufs=3))
+        arena = ctx.enter_context(tc.tile_pool(name="arena", bufs=1))
         psum = ctx.enter_context(tc.psum_pool(name="psum", bufs=1))
+
+        def place(name, shape, dtype, offset):
+            return arena.tile(shape, dtype, name=name, offset=offset, align_bytes=64)
 
         idx = lists.tile([P, S // 16], U16, name="idx")
         idx2 = lists.tile([P, S2 // 16], U16, name="idx2")
@@ -52,87 +62,83 @@ def tile_list_checkers_endgame_retrieval_kernel(
         def scale_rows(tile, q, count=4):
             return tile[32 * q : 32 * q + count, :].bitcast(I32)
 
-        tab_plane = keep.tile([P, T], U8, name="tab_plane", align_bytes=64)
-        w4_plane_raw = keep.tile([P, H], U8, name="w4_plane_raw", tag="woven1", align_bytes=64)
-        nc.vector.memset(tab_plane[:].bitcast(I32), 0)
-        nc.gpsimd.memset(w4_plane_raw[:].bitcast(I32), 0)
-
-        w4_raw = keep.tile([P, 2 * H], U8, name="w4_raw", tag="woven0", align_bytes=64)
-        c2_t = keep.tile([P, ROW_TILES], F32, name="c2_t", tag="woven_a", align_bytes=64)
-        c3_t = keep.tile([P, ROW_TILES], F32, name="c3_t", tag="woven_b", align_bytes=64)
+        c2_t = keep.tile([P, ROW_TILES], F32, name="c2_t")
+        c3_t = keep.tile([P, ROW_TILES], F32, name="c3_t")
         gain_t = keep.tile([P, S2 // P], F32, name="gain_t")
-        w1_raw = [
-            big.tile([P, 4, N], F32, name="w1_raw0", tag="big2", align_bytes=64),
-            keep.tile([P, 4, N], F32, name="w1_raw1", tag="page_codes1", align_bytes=64),
-        ]
-        tab_w = big.tile([P, T], I32, name="tab_w", tag="big0", align_bytes=64)
-        factor = [keep.tile([P, 2, S], F32, name="factor%d" % u) for u in range(2)]
-        pages = {}
+        tab2_plane = keep.tile([P, T2], U8, name="tab2_plane", align_bytes=64)
+        w4_codes = keep.tile([P, 2 * H], U8, name="w4_codes", align_bytes=64)
+        w4_plane = keep.tile([P, H], U8, name="w4_plane", align_bytes=64)
+        w1_codes = [keep.tile([P, N], U32, name="w1_codes%d" % a, align_bytes=64) for a in range(2)]
+        w1_plane = [keep.tile([P, N], U8, name="w1_plane%d" % a, align_bytes=64) for a in range(2)]
+        v_plane = keep.tile([P, S], U8, name="v_plane", align_bytes=64)
+        v_codes = [keep.tile([P, N], U32, name="v_codes%d" % h, align_bytes=64) for h in range(2)]
+        page_plane = [keep.tile([P, T2], U8, name="page_plane%d" % a, align_bytes=64) for a in range(2)]
+
+        tab_w = place("tab_w", [P, T], I32, STAGE0)
+        w1_raw = [place("w1_raw0", [P, 4, N], F32, STAGE0 + 16 * KIB), place("w1_raw1", [P, 4, N], F32, STAGE1)]
+        tab_rows = place("tab_rows", [P, T], U8, STAGE0 + 24 * KIB)
+        tab_plane = place("tab_plane", [P, T], U8, STAGE0 + 28 * KIB)
+        w4_raw = place("w4_raw", [P, 2 * H], U8, STAGE1 + 8 * KIB)
+        w4_plane_raw = place("w4_plane_raw", [P, H], U8, STAGE1 + 10 * KIB)
+        tab2_w = place("tab2_w", [P, 2 * T2], I32, TAB2)
+        factor = [place("factor%d" % t, [P, S], F32, FACTOR + 4 * KIB * t) for t in range(4)]
+        pages = [place("page%d" % i, [P, T2], F32, PAGES + 8 * KIB * i) for i in range(ROW_TILES)]
+
+        nc.vector.memset(w4_plane_raw[:].bitcast(I32), 0)
+        nc.vector.memset(tab_plane[:].bitcast(I32), 0)
+        nc.gpsimd.memset(tab2_plane[:].bitcast(I32), 0)
 
         def load_w1(a):
             nc.sync.dma_start(w1_raw[a][:], w1[:, N * a : N * (a + 1)].rearrange("(p j) c -> p j c", j=4))
 
-        def load_factors(u):
-            src = wgs.rearrange("(q t) j -> q t j", t=4)[:, 2 * u : 2 * u + 2, :]
+        def load_factor(t):
+            src = wgs.rearrange("(q t) j -> t q j", t=4)[t]
             for g in (0, 2, 1, 3):
-                nc.sync.dma_start(factor[u][32 * g : 32 * (g + 1), :, :], src)
+                nc.sync.dma_start(factor[t][32 * g : 32 * (g + 1), :], src)
 
         def load_page(i):
             a, t = divmod(i, 4)
-            pages[i] = rows.tile([P, T2], F32, name="page%d" % i, tag="row")
             nc.sync.dma_start(pages[i][:], page0[N * a : N * (a + 1), :].rearrange("(p t) c -> t p c", t=4)[t])
 
-        tab_rows = keep.tile([P, T], U8, name="tab_rows", tag="page_codes00", align_bytes=64)
-        load_w1(0)
-        nc.sync.dma_start(idx[:], offs)
         for q in range(4):
             nc.sync.dma_start(scale_rows(tab_rows, q), tab_scales[0, 4 * q : 4 * q + 4, :].bitcast(I32))
+        nc.sync.dma_start(idx[:], offs)
         nc.sync.dma_start(w4_raw[:].bitcast(I32), w4_words[0].bitcast(I32))
-        w4_rows = keep.tile([P, H], U8, name="w4_rows", tag="page_codes01", align_bytes=64)
-        for q in range(4):
-            nc.sync.dma_start(scale_rows(w4_rows, q), w4_scales[0, 4 * q : 4 * q + 4, :].bitcast(I32))
+        load_w1(0)
         nc.sync.dma_start(tab_w[:], tab_words[0].rearrange("p t i -> p (t i)").bitcast(I32))
-        for q in range(4):
-            nc.vector.tensor_copy(scale_rows(tab_plane, q), scale_rows(tab_rows, q))
         nc.sync.dma_start(c2_t[:].rearrange("p (a t) -> p a t", t=4), c2.rearrange("(a p t) -> p a t", a=2, t=4))
         nc.sync.dma_start(c3_t[:].rearrange("p (a t) -> p a t", t=4), c3.rearrange("(a p t) -> p a t", a=2, t=4))
-        nc.sync.dma_start(idx3[:], offs3)
+        load_factor(0)
         load_page(0)
-        load_factors(0)
-        load_page(1)
+        nc.sync.dma_start(idx3[:], offs3)
+        load_factor(1)
         load_w1(1)
-        nc.sync.dma_start(idx2[:], offs2)
-        tab2_w = big.tile([P, 2 * T2], I32, name="tab2_w", tag="big1", align_bytes=64)
-        for a in range(2):
-            nc.sync.dma_start(tab2_w[:, T2 * a : T2 * (a + 1)], tab2_words[a].rearrange("p t i -> p (t i)").bitcast(I32))
-        load_factors(1)
+        load_factor(2)
+        load_page(1)
+        load_factor(3)
         for i in range(2, ROW_TILES):
             load_page(i)
+        nc.sync.dma_start(idx2[:], offs2)
+        for a in range(2):
+            nc.sync.dma_start(tab2_w[:, T2 * a : T2 * (a + 1)], tab2_words[a].rearrange("p t i -> p (t i)").bitcast(I32))
         nc.sync.dma_start(idx4[:], offs4)
         with nc.allow_non_contiguous_dma(reason="512 gains, one to a partition"):
             nc.sync.dma_start(gain_t[:], gain.rearrange("(c p) -> p c", p=P))
+        for q in range(4):
+            nc.scalar.dma_start(scale_rows(w4_plane_raw, q), w4_scales[0, 4 * q : 4 * q + 4, :].bitcast(I32))
+        for q in range(4):
+            nc.gpsimd.dma_start(scale_rows(tab2_plane, q, 8), tab2_scales[:, 4 * q : 4 * q + 4, :].bitcast(I32))
 
-        w4_codes = keep.tile([P, 2 * H], U8, name="w4_codes", align_bytes=64)
-        w4_plane = keep.tile([P, H], U8, name="w4_plane", align_bytes=64)
+        for q in range(4):
+            nc.vector.tensor_copy(scale_rows(tab_plane, q), scale_rows(tab_rows, q))
+        nc.vector.tensor_copy(v_plane[:], tab_plane[:].indirect(idx[:]))
         nc.vector.tensor_copy(
             w4_codes[:].bitcast(U16).rearrange("p (a t m) -> p a t m", a=2, t=4),
             w4_raw[:].bitcast(U16).rearrange("p (a m t) -> p a t m", a=2, t=4),
         )
-        for q in range(4):
-            nc.vector.tensor_copy(scale_rows(w4_plane_raw, q), scale_rows(w4_rows, q))
-        nc.vector.tensor_copy(
-            w4_plane[:].rearrange("p (a t m) -> p a t m", a=2, t=4),
-            w4_plane_raw[:].rearrange("p (a m t) -> p a t m", a=2, t=4),
-        )
-        tab2_plane = keep.tile([P, T2], U8, name="tab2_plane", tag="woven1", align_bytes=64)
-        nc.vector.memset(tab2_plane[:].bitcast(I32), 0)
-        for q in range(4):
-            nc.gpsimd.dma_start(scale_rows(tab2_plane, q, 8), tab2_scales[:, 4 * q : 4 * q + 4, :].bitcast(I32))
-        w1_codes = [keep.tile([P, N], U32, name="w1_codes%d" % a, align_bytes=64) for a in range(2)]
-        w1_plane = [keep.tile([P, N], U8, name="w1_plane%d" % a, align_bytes=64) for a in range(2)]
 
         def quantize_w1(a):
-            grouped = keep.tile([P, 4 * N], BF16, name="w1_grouped", tag="w1_grouped", align_bytes=64)
+            grouped = place("w1_grouped%d" % a, [P, 4 * N], BF16, STAGE1 + 12 * KIB + 4 * KIB * a)
             nc.scalar.copy(
                 grouped[:].rearrange("p (t m j) -> p m j t", t=4, j=4),
                 w1_raw[a][:].rearrange("p j (m t) -> p m j t", t=4),
@@ -140,218 +146,172 @@ def tile_list_checkers_endgame_retrieval_kernel(
             nc.vector.quantize_mx(out=w1_codes[a][:].bitcast(FP8X4), scales=w1_plane[a][:], in_=grouped[:])
 
         quantize_w1(0)
-
-        v_plane = [keep.tile([P, N], U8, name="v_plane%d" % h, align_bytes=64) for h in range(2)]
-        v_codes = [keep.tile([P, N], U32, name="v_codes%d" % h, align_bytes=64) for h in range(2)]
+        nc.vector.tensor_copy(
+            w4_plane[:].rearrange("p (a t m) -> p a t m", a=2, t=4),
+            w4_plane_raw[:].rearrange("p (a m t) -> p a t m", a=2, t=4),
+        )
         for h in range(2):
-            nc.vector.tensor_copy(v_plane[h][:], tab_plane[:].indirect(list_half(idx, h)))
             nc.vector.tensor_copy(v_codes[h][:], tab_w[:].bitcast(U32).indirect(list_half(idx, h)))
 
-        v2 = {}
-
-        def gather_tab2():
-            codes = keep.tile([P, 2 * S2], U32, name="v2_codes", tag="v2_codes", align_bytes=64)
-            plane = keep.tile([P, S2], U8, name="v2_plane", tag="v2_plane", align_bytes=64)
-            v2["codes"] = codes
-            v2["plane"] = plane
-            nc.vector.tensor_copy(plane[:], tab2_plane[:].indirect(idx2[:]))
-            for a in range(2):
-                nc.vector.tensor_copy(codes[:, S2 * a : S2 * (a + 1)], tab2_w[:, T2 * a : T2 * (a + 1)].bitcast(U32).indirect(idx2[:]))
-
-        steps = [((2 * pair, h), (2 * pair + 1, h)) for pair in range(3) for h in range(2)]
-        steps.extend([((i, 0), (i, 1)) for i in (ROW_TILES - 2, ROW_TILES - 1)])
+        lin = {}
         terms = {}
 
-        def first_product(d):
-            square = poly.tile([P, 2, N], F32, name="square")
-            if d == STAGED_STEP + 1:
-                affine = keep.tile([P, 2, N], F32, name="affine_staged", tag="page_codes01", align_bytes=64)
-            else:
-                affine = poly.tile([P, 2, N], F32, name="affine")
-            linear = []
-            for e, (i, h) in enumerate(steps[d]):
-                a, t = divmod(i, 4)
-                lin = psum.tile([P, N], F32, name="lin", tag="bank%d" % (2 * (d % 3) + e))
+        def first_product(i):
+            a, t = divmod(i, 4)
+            affine = place("affine%d" % i, [P, S], F32, AFFINE + 4 * KIB * ((i + 2) % 5))
+            square = linear = None
+            if i > 0:
+                square = place("square%d" % i, [P, S], F32, SQUARE + 4 * KIB * (i % 3))
+                linear = place("linear%d" % i, [P, S], F32, LINEAR + 4 * KIB * (i % 4))
+            for h in range(2):
+                cols = slice(N * h, N * (h + 1))
+                lin[i, h] = psum.tile([P, N], F32, name="lin", tag="bank%d" % (2 * (i % 3) + h))
                 nc.tensor.matmul_mx(
-                    out=lin[:], lhsT=w1_codes[a][:, P * t : P * (t + 1)].bitcast(FP8X4), lhsT_scale=w1_plane[a][:, P * t : P * (t + 1)],
-                    rhs=v_codes[h][:].bitcast(FP8X4), rhs_scale=v_plane[h][:], start=True, stop=False,
+                    out=lin[i, h][:], lhsT=w1_codes[a][:, P * t : P * (t + 1)].bitcast(FP8X4), lhsT_scale=w1_plane[a][:, P * t : P * (t + 1)],
+                    rhs=v_codes[h][:].bitcast(FP8X4), rhs_scale=v_plane[:, cols], start=True, stop=False,
                 )
                 nc.tensor.matmul_mx(
-                    out=lin[:], lhsT=w4_codes[:, 2 * P * i : 2 * P * (i + 1)].bitcast(FP4X4), lhsT_scale=w4_plane[:, P * i : P * (i + 1)],
-                    rhs=v_codes[h][:].bitcast(FP8X4), rhs_scale=v_plane[h][:], start=False, stop=True,
+                    out=lin[i, h][:], lhsT=w4_codes[:, 2 * P * i : 2 * P * (i + 1)].bitcast(FP4X4), lhsT_scale=w4_plane[:, P * i : P * (i + 1)],
+                    rhs=v_codes[h][:].bitcast(FP8X4), rhs_scale=v_plane[:, cols], start=False, stop=True,
                 )
-                nc.scalar.activation(square[:, e, :], lin[:], ACT.Square)
-                nc.scalar.activation(affine[:, e, :], lin[:], ACT.Identity, bias=c2_t[:, i : i + 1], scale=c3_t[:, i : i + 1])
-                if e == 0 or d == 0:
-                    linear.append(lin)
-                else:
-                    if d <= 2:
-                        lin_sb = keep.tile([P, N], F32, name="lin_early", tag=("v2_plane", "v2_codes")[d - 1], align_bytes=64)
-                    else:
-                        lin_sb = poly.tile([P, N], F32, name="lin_sb", bufs=2)
-                    nc.scalar.copy(lin_sb[:], lin[:])
-                    linear.append(lin_sb)
-            terms[d] = (square, affine, linear)
+                nc.scalar.activation(affine[:, cols], lin[i, h][:], ACT.Identity, bias=c2_t[:, i : i + 1], scale=c3_t[:, i : i + 1])
+                if i > 0:
+                    nc.scalar.activation(square[:, cols], lin[i, h][:], ACT.Square)
+            if i > 0:
+                for h in range(2):
+                    nc.scalar.copy(linear[:, N * h : N * (h + 1)], lin[i, h][:])
+            terms[i] = (square, affine, linear)
 
-        def factors(d):
-            (i0, h0), second = steps[d]
-            both = factor[i0 % 4 // 2]
-            if i0 == second[0]:
-                return both[:, i0 % 2, :].rearrange("p (e c) -> p e c", e=2)
-            return both[:, :, N * h0 : N * (h0 + 1)]
+        def first_tile():
+            affine = terms[0][1]
+            horner = place("horner", [P, S], F32, CUBIC + 4 * KIB)
+            halves = [slice(N * h, N * (h + 1)) for h in range(2)]
+            for h in range(2):
+                nc.vector.tensor_tensor(horner[:, halves[h]], affine[:, halves[h]], lin[0, h][:], MULT)
+            for h in range(2):
+                nc.vector.scalar_tensor_tensor(horner[:, halves[h]], horner[:, halves[h]], 1.0, lin[0, h][:], ADD, MULT)
+            nc.vector.tensor_tensor(affine[:], horner[:], factor[0][:], MULT)
 
-        weighted = {}
-        cubics = {}
+        cubic = {}
 
-        def cubic(d):
-            square, affine, linear = terms[d]
-            h_tile = poly.tile([P, 2, N], F32, name="h_tile", bufs=2)
-            nc.gpsimd.tensor_tensor(h_tile[:], square[:], affine[:], MULT)
-            nc.gpsimd.tensor_tensor(h_tile[:, 1, :], h_tile[:, 1, :], linear[1][:], ADD)
-            nc.vector.tensor_tensor(h_tile[:, 0, :], h_tile[:, 0, :], linear[0][:], ADD)
-            cubics[d] = h_tile
+        def high_terms(i):
+            square, affine, linear = terms[i]
+            cubic[i] = place("cubic%d" % i, [P, S], F32, CUBIC + 4 * KIB * (i % 2))
+            nc.gpsimd.tensor_tensor(cubic[i][:], square[:], affine[:], MULT)
 
-        def weigh(d):
-            if d == 1:
-                weighted[d] = keep.tile([P, 2, N], F32, name="weighted_second", tag="w1_grouped", align_bytes=64)
-            elif d < LAST:
-                weighted[d] = terms[d + 1][1]
-            else:
-                weighted[d] = keep.tile([P, 2, N], F32, name="weighted_last", tag="page_codes00", align_bytes=64)
-            nc.gpsimd.tensor_tensor(weighted[d][:], cubics[d][:], factors(d), MULT)
+        def polynomial(i):
+            square, affine, linear = terms[i]
+            nc.gpsimd.tensor_tensor(cubic[i][:], cubic[i][:], linear[:], ADD)
+            if i < LAST:
+                high_terms(i + 1)
+            nc.gpsimd.tensor_tensor(affine[:], cubic[i][:], factor[i % 4][:], MULT)
 
-        def first_step():
-            square, affine, linear = terms[0]
-            for e, (i, h) in enumerate(steps[0]):
-                nc.vector.tensor_tensor(square[:, e, :], square[:, e, :], affine[:, e, :], MULT)
-                nc.vector.tensor_tensor(square[:, e, :], square[:, e, :], linear[e][:], ADD)
-                nc.vector.tensor_tensor(affine[:, e, :], square[:, e, :], factors(0)[:, e, :], MULT)
-                nc.vector.tensor_copy(pages[i][:].indirect(list_half(idx3, h)), affine[:, e, :])
+        def scatter(i):
+            nc.vector.tensor_copy(pages[i][:].indirect(idx3[:]), terms[i][1][:])
 
-        def scatter(d):
-            for e, (i, h) in enumerate(steps[d]):
-                nc.vector.tensor_copy(pages[i][:].indirect(list_half(idx3, h)), weighted[d][:, e, :])
-
-        woven = {}
-        woven_half = {}
-        page_codes = {}
-        page_plane = {}
         stage = {}
-
-        def woven_tile(a, c):
-            if (a, c) not in woven:
-                if a == 1 and c < 2:
-                    woven[a, c] = keep.tile([P, N, 4], BF16, name="woven", tag="woven%d" % c, align_bytes=64)[:]
-                else:
-                    if a == 1:
-                        both = big.tile([P, 2 * N, 4], BF16, name="woven_late", tag="big2", align_bytes=64)
-                    else:
-                        both = keep.tile([P, 2 * N, 4], BF16, name="woven_early", tag="woven_a" if c > 1 else "woven_b", align_bytes=64)
-                    woven_half[a, c // 2] = both[:]
-                    for e in range(2):
-                        woven[a, c - c % 2 + e] = both[:, N * e : N * (e + 1), :]
-            return woven[a, c]
-
-        stage_buffer = {(0, 0): "big1", (0, 1): "big2", (1, 0): "big1", (1, 1): "big0"}
 
         def stage_page(i):
             a, t = divmod(i, 4)
             for half in range(2):
                 if t == 0:
-                    stage[a, half] = big.tile([P, 4, 2 * N], F32, name="stage", tag=stage_buffer[a, half], align_bytes=64)
+                    rows = 4 - a
+                    base = (STAGE0, STAGE1)[a] + rows * 4 * KIB * half
+                    stage[a, half] = place("stage%d%d" % (a, half), [P, rows, 2 * N], F32, base)
                 nc.sync.dma_start(stage[a, half][:, t, :], pages[i][:, 2 * N * half : 2 * N * (half + 1)])
 
-        def weave(a, c, t0, t1, on_vector):
-            src = stage[a, c // 2][:, t0:t1, N * (c % 2) : N * (c % 2 + 1)].rearrange("p t (g i) -> p g t i", i=4)
-            dst = woven_tile(a, c)[:, :, t0:t1].rearrange("p (g i) t -> p g t i", i=4)
-            if on_vector:
-                nc.vector.tensor_copy(dst, src)
-            else:
-                nc.scalar.copy(dst, src)
+        woven = {}
 
-        def weave_half(a, half, t1):
-            woven_tile(a, 2 * half)
-            nc.scalar.copy(
-                woven_half[a, half][:, :, 0:t1].rearrange("p (g i) t -> p g t i", i=4),
-                stage[a, half][:, 0:t1, :].rearrange("p t (g i) -> p g t i", i=4),
-            )
+        def weave(a, c, rows, on_scalar):
+            woven[a, c] = place("woven%d%d" % (a, c), [P, N, 4], BF16, (PAGES, STAGE0)[a] + 4 * KIB * c)
+            src = stage[a, c // 2][:, 0:rows, N * (c % 2) : N * (c % 2 + 1)].rearrange("p t (g i) -> p g t i", i=4)
+            dst = woven[a, c][:, :, 0:rows].rearrange("p (g i) t -> p g t i", i=4)
+            if on_scalar:
+                nc.scalar.copy(dst, src)
+            else:
+                nc.gpsimd.tensor_scalar(dst, src, 1.0, 0.0, MULT, ADD)
+
+        def weave_last(c, on_scalar):
+            src = pages[LAST][:, N * c : N * (c + 1)]
+            dst = woven[1, c][:, :, 3]
+            if on_scalar:
+                nc.scalar.copy(dst, src)
+            else:
+                nc.gpsimd.tensor_scalar(dst, src, 1.0, 0.0, MULT, ADD)
+
+        codes = {}
 
         def quantize_page(a, c):
-            if (a, c) not in page_codes:
-                if a == 0:
-                    codes = keep.tile([P, 2 * N], U32, name="page_codes0", tag="page_codes0%d" % (c // 2), align_bytes=64)
-                    for e in range(2):
-                        page_codes[a, c - c % 2 + e] = codes[:, N * e : N * (e + 1)]
-                else:
-                    codes = keep.tile([P, 4 * N], U32, name="page_codes1", tag="page_codes1", align_bytes=64)
-                    for e in range(4):
-                        page_codes[a, e] = codes[:, N * e : N * (e + 1)]
-            page_plane[a, c] = keep.tile([P, N], U8, name="page_plane%d%d" % (a, c), align_bytes=64)
             nc.vector.quantize_mx(
-                out=page_codes[a, c].bitcast(FP8X4), scales=page_plane[a, c][:], in_=woven[a, c].rearrange("p c t -> p (c t)")
+                out=codes[a][:, N * c : N * (c + 1)].bitcast(FP8X4), scales=page_plane[a][:, N * c : N * (c + 1)],
+                in_=woven[a, c][:].rearrange("p c t -> p (c t)"),
             )
+
+        first_product(0)
+        first_product(1)
+        first_tile()
+        first_product(2)
+        quantize_w1(1)
+        first_product(3)
+        high_terms(1)
+        polynomial(1)
+        scatter(0)
+        stage_page(0)
+        first_product(4)
+        for i in range(1, ROW_TILES):
+            if i + 1 < ROW_TILES:
+                polynomial(i + 1)
+            if i == LAST:
+                codes[0] = place("page_codes0", [P, T2], U32, AFFINE + 8 * KIB)
+                for c in range(4):
+                    quantize_page(0, c)
+            scatter(i)
+            if i < LAST:
+                stage_page(i)
+            if i + 4 < ROW_TILES:
+                first_product(i + 4)
+            if i == 5:
+                for c in range(4):
+                    weave(0, c, 4, True)
+        for c in range(4):
+            weave(1, c, 3, N * c < SCALAR_COLUMNS)
+
+        v2_plane = place("v2_plane", [P, S2], U8, AFFINE + 16 * KIB)
+        v2_codes = place("v2_codes", [P, 2 * S2], U32, AFFINE + 16 * KIB + S2)
+        nc.vector.tensor_copy(v2_plane[:], tab2_plane[:].indirect(idx2[:]))
+        for a in range(2):
+            nc.vector.tensor_copy(v2_codes[:, S2 * a : S2 * (a + 1)], tab2_w[:, T2 * a : T2 * (a + 1)].bitcast(U32).indirect(idx2[:]))
+        for c in range(4):
+            weave_last(c, N * c < SCALAR_COLUMNS)
 
         score = {}
 
         def second_product(n, a, c):
             if a == 0:
-                score[n, c] = psum.tile([P, N], F32, name="score", tag="bank%d" % (4 * (1 - n % 2) + c))
+                score[n, c] = psum.tile([P, N], F32, name="score", tag="bank%d" % (4 * (n % 2) + c))
             nc.tensor.matmul_mx(
                 out=score[n, c][:],
-                lhsT=v2["codes"][:, S2 * a + P * n : S2 * a + P * (n + 1)].bitcast(FP8X4),
-                lhsT_scale=v2["plane"][4 * a : P, P * n : P * (n + 1)],
-                rhs=page_codes[a, c].bitcast(FP8X4), rhs_scale=page_plane[a, c][:], start=(a == 0), stop=(a == 1),
+                lhsT=v2_codes[:, S2 * a + P * n : S2 * a + P * (n + 1)].bitcast(FP8X4),
+                lhsT_scale=v2_plane[4 * a : P, P * n : P * (n + 1)],
+                rhs=codes[a][:, N * c : N * (c + 1)].bitcast(FP8X4), rhs_scale=page_plane[a][:, N * c : N * (c + 1)],
+                start=(a == 0), stop=(a == 1),
             )
 
-        first_product(0)
-        first_product(1)
-        first_step()
-        cubic(1)
-        first_product(2)
-        quantize_w1(1)
-        for d in range(1, STEPS):
-            if d + 2 < STEPS:
-                first_product(d + 2)
-            if d + 1 < STEPS:
-                cubic(d + 1)
-            if d == STAGED_STEP:
-                weave_half(0, 1, 4)
-                weave_half(0, 0, 4)
-            weigh(d)
-            if d == 1:
-                gather_tab2()
-            scatter(d)
-            for i, h in steps[d]:
-                if h == 1 and i < ROW_TILES - 1:
-                    stage_page(i)
-            if d == STAGED_STEP:
-                for c in (2, 3):
-                    quantize_page(0, c)
-                weave_half(1, 1, 2)
-                for c in (0, 1):
-                    weave(1, c, 0, 2, False)
-
-        for half in range(2):
-            nc.vector.tensor_copy(stage[1, half][:, 3, :], pages[ROW_TILES - 1][:, 2 * N * half : 2 * N * (half + 1)])
+        order = (0, 2, 1, 3)
         for n in range(2):
-            for c in (2, 3):
+            for c in order:
                 second_product(n, 0, c)
-        for c in (0, 1):
-            quantize_page(0, c)
-            for n in range(2):
-                second_product(n, 0, c)
-        for c in range(4):
-            weave(1, c, 2, 4, c > 1)
-        for c in CHUNK_ORDER:
+        codes[1] = place("page_codes1", [P, T2], U32, STAGE0 + 16 * KIB)
+        for c in order:
             quantize_page(1, c)
             for n in range(2):
                 second_product(n, 1, c)
 
         score_sb = {}
         for n in range(S2 // P):
-            score_sb[n] = rows.tile([P, T2], F32, name="score_sb%d" % n, tag="row")
-            for c in CHUNK_ORDER:
-                if (n, c) in VECTOR_EMPTIES:
+            score_sb[n] = place("score_sb%d" % n, [P, T2], F32, PAGES + 8 * KIB * (2 + n))
+            for c in order:
+                if (n, c) == (0, 3):
                     nc.vector.tensor_copy(score_sb[n][:, N * c : N * (c + 1)], score[n, c][:])
                 else:
                     nc.scalar.copy(score_sb[n][:, N * c : N * (c + 1)], score[n, c][:])
@@ -359,9 +319,12 @@ def tile_list_checkers_endgame_retrieval_kernel(
                     second_product(n + 2, 0, c)
                     second_product(n + 2, 1, c)
         for n in range(S2 // P):
-            picked = poly.tile([P, 2, N], F32, name="picked", tag="affine")
-            result = poly.tile([P, 2, N], F32, name="result", tag="square")
-            for h in range(2):
-                nc.vector.tensor_copy(picked[:, h, :], score_sb[n][:].indirect(list_half(idx4, h)))
-                nc.scalar.activation(result[:, h, :], picked[:, h, :], ACT.Tanh, scale=gain_t[:, n : n + 1])
-                nc.sync.dma_start(out[P * n : P * (n + 1), N * h : N * (h + 1)], result[:, h, :])
+            picked = place("picked%d" % n, [P, PQ], F32, FACTOR + 4 * KIB * n)
+            result = place("result%d" % n, [P, PQ], F32, SQUARE + 4 * KIB * n)
+            pieces = 2 if n == S2 // P - 1 else 1
+            width = PQ // pieces
+            for u in range(pieces):
+                cols = slice(width * u, width * (u + 1))
+                nc.vector.tensor_copy(picked[:, cols], score_sb[n][:].indirect(idx4[:, width // 16 * u : width // 16 * (u + 1)]))
+                nc.scalar.activation(result[:, cols], picked[:, cols], ACT.Tanh, scale=gain_t[:, n : n + 1])
+                nc.sync.dma_start(out[P * n : P * (n + 1), cols], result[:, cols])

@@ -23,7 +23,8 @@ LIST_HALF = N // 16
 ROW_TILES = H // P
 LAST = ROW_TILES - 1
 KIB = 1024
-SCALAR_COLUMNS = 1024
+FIRST_PIECE = 256
+ON_VECTOR = 2
 
 PAGES = 0
 FACTOR = PAGES + 64 * KIB
@@ -81,7 +82,9 @@ def tile_list_checkers_endgame_retrieval_kernel(
         w4_raw = place("w4_raw", [P, 2 * H], U8, STAGE1 + 8 * KIB)
         w4_plane_raw = place("w4_plane_raw", [P, H], U8, STAGE1 + 10 * KIB)
         tab2_w = place("tab2_w", [P, 2 * T2], I32, TAB2)
-        factor = [place("factor%d" % t, [P, S], F32, FACTOR + 4 * KIB * t) for t in range(4)]
+        factor_first = place("factor_first", [P, 1, S], F32, FACTOR)
+        factor_rest = place("factor_rest", [P, 3, S], F32, FACTOR + 4 * KIB)
+        factor = [factor_first[:, 0, :]] + [factor_rest[:, u, :] for u in range(3)]
         pages = [place("page%d" % i, [P, T2], F32, PAGES + 8 * KIB * i) for i in range(ROW_TILES)]
 
         nc.vector.memset(w4_plane_raw[:].bitcast(I32), 0)
@@ -91,10 +94,10 @@ def tile_list_checkers_endgame_retrieval_kernel(
         def load_w1(a):
             nc.sync.dma_start(w1_raw[a][:], w1[:, N * a : N * (a + 1)].rearrange("(p j) c -> p j c", j=4))
 
-        def load_factor(t):
-            src = wgs.rearrange("(q t) j -> t q j", t=4)[t]
+        def load_factor(tile, t0, t1):
+            src = wgs.rearrange("(q t) j -> q t j", t=4)[:, t0:t1, :]
             for g in (0, 2, 1, 3):
-                nc.sync.dma_start(factor[t][32 * g : 32 * (g + 1), :], src)
+                nc.sync.dma_start(tile[32 * g : 32 * (g + 1), :, :], src)
 
         def load_page(i):
             a, t = divmod(i, 4)
@@ -108,15 +111,12 @@ def tile_list_checkers_endgame_retrieval_kernel(
         nc.sync.dma_start(tab_w[:], tab_words[0].rearrange("p t i -> p (t i)").bitcast(I32))
         nc.sync.dma_start(c2_t[:].rearrange("p (a t) -> p a t", t=4), c2.rearrange("(a p t) -> p a t", a=2, t=4))
         nc.sync.dma_start(c3_t[:].rearrange("p (a t) -> p a t", t=4), c3.rearrange("(a p t) -> p a t", a=2, t=4))
-        load_factor(0)
+        load_factor(factor_first, 0, 1)
+        load_w1(1)
         load_page(0)
         nc.sync.dma_start(idx3[:], offs3)
-        load_factor(1)
-        load_w1(1)
-        load_factor(2)
-        load_page(1)
-        load_factor(3)
-        for i in range(2, ROW_TILES):
+        load_factor(factor_rest, 1, 4)
+        for i in range(1, ROW_TILES):
             load_page(i)
         nc.sync.dma_start(idx2[:], offs2)
         for a in range(2):
@@ -160,7 +160,7 @@ def tile_list_checkers_endgame_retrieval_kernel(
             a, t = divmod(i, 4)
             affine = place("affine%d" % i, [P, S], F32, AFFINE + 4 * KIB * ((i + 2) % 5))
             square = linear = None
-            if i > 0:
+            if i >= ON_VECTOR:
                 square = place("square%d" % i, [P, S], F32, SQUARE + 4 * KIB * (i % 3))
                 linear = place("linear%d" % i, [P, S], F32, LINEAR + 4 * KIB * (i % 4))
             for h in range(2):
@@ -175,24 +175,26 @@ def tile_list_checkers_endgame_retrieval_kernel(
                     rhs=v_codes[h][:].bitcast(FP8X4), rhs_scale=v_plane[:, cols], start=False, stop=True,
                 )
                 nc.scalar.activation(affine[:, cols], lin[i, h][:], ACT.Identity, bias=c2_t[:, i : i + 1], scale=c3_t[:, i : i + 1])
-                if i > 0:
+                if i >= ON_VECTOR:
                     nc.scalar.activation(square[:, cols], lin[i, h][:], ACT.Square)
-            if i > 0:
+            if i >= ON_VECTOR:
                 for h in range(2):
                     nc.scalar.copy(linear[:, N * h : N * (h + 1)], lin[i, h][:])
             terms[i] = (square, affine, linear)
 
-        def first_tile():
-            affine = terms[0][1]
-            horner = place("horner", [P, S], F32, CUBIC + 4 * KIB)
+        cubic = {}
+
+        def horner(i):
+            affine = terms[i][1]
+            cubic[i] = place("cubic%d" % i, [P, S], F32, CUBIC + 4 * KIB * (i % 2))
             halves = [slice(N * h, N * (h + 1)) for h in range(2)]
             for h in range(2):
-                nc.vector.tensor_tensor(horner[:, halves[h]], affine[:, halves[h]], lin[0, h][:], MULT)
+                nc.vector.tensor_tensor(cubic[i][:, halves[h]], affine[:, halves[h]], lin[i, h][:], MULT)
             for h in range(2):
-                nc.vector.scalar_tensor_tensor(horner[:, halves[h]], horner[:, halves[h]], 1.0, lin[0, h][:], ADD, MULT)
-            nc.vector.tensor_tensor(affine[:], horner[:], factor[0][:], MULT)
+                nc.vector.scalar_tensor_tensor(cubic[i][:, halves[h]], cubic[i][:, halves[h]], 1.0, lin[i, h][:], ADD, MULT)
 
-        cubic = {}
+        def weigh(i, engine):
+            engine.tensor_tensor(terms[i][1][:], cubic[i][:], factor[i % 4], MULT)
 
         def high_terms(i):
             square, affine, linear = terms[i]
@@ -204,7 +206,10 @@ def tile_list_checkers_endgame_retrieval_kernel(
             nc.gpsimd.tensor_tensor(cubic[i][:], cubic[i][:], linear[:], ADD)
             if i < LAST:
                 high_terms(i + 1)
-            nc.gpsimd.tensor_tensor(affine[:], cubic[i][:], factor[i % 4][:], MULT)
+            if i < LAST:
+                weigh(i, nc.gpsimd)
+            else:
+                nc.gpsimd.tensor_tensor(affine[:, FIRST_PIECE:], cubic[i][:, FIRST_PIECE:], factor[3][:, FIRST_PIECE:], MULT)
 
         def scatter(i):
             nc.vector.tensor_copy(pages[i][:].indirect(idx3[:]), terms[i][1][:])
@@ -215,46 +220,50 @@ def tile_list_checkers_endgame_retrieval_kernel(
             a, t = divmod(i, 4)
             for half in range(2):
                 if t == 0:
-                    rows = 4 - a
+                    rows = 4 - 2 * a
                     base = (STAGE0, STAGE1)[a] + rows * 4 * KIB * half
                     stage[a, half] = place("stage%d%d" % (a, half), [P, rows, 2 * N], F32, base)
-                nc.sync.dma_start(stage[a, half][:, t, :], pages[i][:, 2 * N * half : 2 * N * (half + 1)])
+                nc.scalar.dma_start(stage[a, half][:, t, :], pages[i][:, 2 * N * half : 2 * N * (half + 1)])
 
         woven = {}
 
-        def weave(a, c, rows, on_scalar):
-            woven[a, c] = place("woven%d%d" % (a, c), [P, N, 4], BF16, (PAGES, STAGE0)[a] + 4 * KIB * c)
-            src = stage[a, c // 2][:, 0:rows, N * (c % 2) : N * (c % 2 + 1)].rearrange("p t (g i) -> p g t i", i=4)
-            dst = woven[a, c][:, :, 0:rows].rearrange("p (g i) t -> p g t i", i=4)
-            if on_scalar:
-                nc.scalar.copy(dst, src)
-            else:
-                nc.gpsimd.tensor_scalar(dst, src, 1.0, 0.0, MULT, ADD)
+        def weave(a, half, c):
+            if c == 0:
+                base = STAGE0 if (a, half) == (1, 0) else PAGES + 8 * KIB * half
+                woven[a, half] = place("woven%d%d" % (a, half), [P, 2 * N, 4], BF16, base)
+            rows = 4 - 2 * a
+            nc.scalar.copy(
+                woven[a, half][:, N * c : N * (c + 1), 0:rows].rearrange("p (g i) t -> p g t i", i=4),
+                stage[a, half][:, :, N * c : N * (c + 1)].rearrange("p t (g i) -> p g t i", i=4),
+            )
 
-        def weave_last(c, on_scalar):
-            src = pages[LAST][:, N * c : N * (c + 1)]
-            dst = woven[1, c][:, :, 3]
-            if on_scalar:
+        def weave_row(t, half, c):
+            src = pages[4 + t][:, N * (2 * half + c) : N * (2 * half + c + 1)]
+            dst = woven[1, half][:, N * c : N * (c + 1), t]
+            if half == 0:
                 nc.scalar.copy(dst, src)
             else:
                 nc.gpsimd.tensor_scalar(dst, src, 1.0, 0.0, MULT, ADD)
 
         codes = {}
 
-        def quantize_page(a, c):
+        def quantize_page(a, c0, c1):
+            half = c0 // 2
             nc.vector.quantize_mx(
-                out=codes[a][:, N * c : N * (c + 1)].bitcast(FP8X4), scales=page_plane[a][:, N * c : N * (c + 1)],
-                in_=woven[a, c][:].rearrange("p c t -> p (c t)"),
+                out=codes[a][:, N * c0 : N * c1].bitcast(FP8X4), scales=page_plane[a][:, N * c0 : N * c1],
+                in_=woven[a, half][:, N * (c0 - 2 * half) : N * (c1 - 2 * half), :].rearrange("p c t -> p (c t)"),
             )
 
         first_product(0)
         first_product(1)
-        first_tile()
-        first_product(2)
+        horner(0)
+        weigh(0, nc.vector)
+        horner(1)
         quantize_w1(1)
+        first_product(2)
         first_product(3)
-        high_terms(1)
-        polynomial(1)
+        high_terms(2)
+        weigh(1, nc.gpsimd)
         scatter(0)
         stage_page(0)
         first_product(4)
@@ -263,26 +272,41 @@ def tile_list_checkers_endgame_retrieval_kernel(
                 polynomial(i + 1)
             if i == LAST:
                 codes[0] = place("page_codes0", [P, T2], U32, AFFINE + 8 * KIB)
-                for c in range(4):
-                    quantize_page(0, c)
-            scatter(i)
-            if i < LAST:
+                for half in range(2):
+                    quantize_page(0, 2 * half, 2 * half + 2)
+                piece = place("first_piece", [P, FIRST_PIECE], F32, PAGES + 8 * KIB - 2 * FIRST_PIECE)
+                nc.vector.tensor_tensor(piece[:], cubic[i][:, :FIRST_PIECE], factor[3][:, :FIRST_PIECE], MULT)
+                nc.vector.tensor_copy(pages[i][:].indirect(idx3[:, : FIRST_PIECE // 16]), piece[:])
+                nc.vector.tensor_copy(pages[i][:].indirect(idx3[:, FIRST_PIECE // 16 :]), terms[i][1][:, FIRST_PIECE:])
+            else:
+                scatter(i)
+            if i < LAST - 1:
                 stage_page(i)
             if i + 4 < ROW_TILES:
                 first_product(i + 4)
+            if i == 3:
+                for half in range(2):
+                    for c in range(2):
+                        weave(0, half, c)
             if i == 5:
-                for c in range(4):
-                    weave(0, c, 4, True)
-        for c in range(4):
-            weave(1, c, 3, N * c < SCALAR_COLUMNS)
+                for c in range(2):
+                    weave(1, 0, c)
+            if i == 6:
+                for c in range(2):
+                    weave_row(2, 0, c)
+        for c in range(2):
+            weave(1, 1, c)
+        for c in range(2):
+            weave_row(2, 1, c)
 
         v2_plane = place("v2_plane", [P, S2], U8, AFFINE + 16 * KIB)
         v2_codes = place("v2_codes", [P, 2 * S2], U32, AFFINE + 16 * KIB + S2)
         nc.vector.tensor_copy(v2_plane[:], tab2_plane[:].indirect(idx2[:]))
         for a in range(2):
             nc.vector.tensor_copy(v2_codes[:, S2 * a : S2 * (a + 1)], tab2_w[:, T2 * a : T2 * (a + 1)].bitcast(U32).indirect(idx2[:]))
-        for c in range(4):
-            weave_last(c, N * c < SCALAR_COLUMNS)
+        for c in range(2):
+            for half in range(2):
+                weave_row(3, half, c)
 
         score = {}
 
@@ -303,7 +327,7 @@ def tile_list_checkers_endgame_retrieval_kernel(
                 second_product(n, 0, c)
         codes[1] = place("page_codes1", [P, T2], U32, STAGE0 + 16 * KIB)
         for c in order:
-            quantize_page(1, c)
+            quantize_page(1, c, c + 1)
             for n in range(2):
                 second_product(n, 1, c)
 

@@ -23,6 +23,7 @@ LIST_HALF = N // 16
 ROW_TILES = H // P
 LAST = ROW_TILES - 1
 KIB = 1024
+SCALAR_COLUMNS = 1280
 FIRST_PIECE = 256
 ON_VECTOR = 2
 
@@ -76,16 +77,16 @@ def tile_list_checkers_endgame_retrieval_kernel(
         page_plane = [keep.tile([P, T2], U8, name="page_plane%d" % a, align_bytes=64) for a in range(2)]
 
         tab_w = place("tab_w", [P, T], I32, STAGE0)
-        w1_raw = [place("w1_raw0", [P, 4, N], F32, STAGE0 + 16 * KIB), place("w1_raw1", [P, 4, N], F32, STAGE1)]
-        tab_rows = place("tab_rows", [P, T], U8, STAGE0 + 24 * KIB)
-        tab_plane = place("tab_plane", [P, T], U8, STAGE0 + 28 * KIB)
+        w1_raw = [place("w1_raw0", [P, 4, N], F32, STAGE0 + 16 * KIB), place("w1_raw1", [P, 4, N], F32, STAGE0 + 24 * KIB)]
+        tab_rows = place("tab_rows", [P, T], U8, STAGE1)
+        tab_plane = place("tab_plane", [P, T], U8, STAGE1 + 4 * KIB)
         w4_raw = place("w4_raw", [P, 2 * H], U8, STAGE1 + 8 * KIB)
         w4_plane_raw = place("w4_plane_raw", [P, H], U8, STAGE1 + 10 * KIB)
         tab2_w = place("tab2_w", [P, 2 * T2], I32, TAB2)
         factor_first = place("factor_first", [P, 1, S], F32, FACTOR)
         factor_rest = place("factor_rest", [P, 3, S], F32, FACTOR + 4 * KIB)
         factor = [factor_first[:, 0, :]] + [factor_rest[:, u, :] for u in range(3)]
-        pages = [place("page%d" % i, [P, T2], F32, PAGES + 8 * KIB * i) for i in range(ROW_TILES)]
+        pages = [place("page%d" % i, [P, T2], F32, PAGES + 8 * KIB * i) for i in range(LAST)]
 
         nc.vector.memset(w4_plane_raw[:].bitcast(I32), 0)
         nc.vector.memset(tab_plane[:].bitcast(I32), 0)
@@ -109,25 +110,27 @@ def tile_list_checkers_endgame_retrieval_kernel(
         nc.sync.dma_start(w4_raw[:].bitcast(I32), w4_words[0].bitcast(I32))
         load_w1(0)
         nc.sync.dma_start(tab_w[:], tab_words[0].rearrange("p t i -> p (t i)").bitcast(I32))
-        nc.sync.dma_start(c2_t[:].rearrange("p (a t) -> p a t", t=4), c2.rearrange("(a p t) -> p a t", a=2, t=4))
-        nc.sync.dma_start(c3_t[:].rearrange("p (a t) -> p a t", t=4), c3.rearrange("(a p t) -> p a t", a=2, t=4))
+        nc.sync.dma_start(idx2[:], offs2)
+        for q in range(4):
+            nc.sync.dma_start(scale_rows(tab2_plane, q, 8), tab2_scales[:, 4 * q : 4 * q + 4, :].bitcast(I32))
         load_factor(factor_first, 0, 1)
-        load_w1(1)
         load_page(0)
         nc.sync.dma_start(idx3[:], offs3)
         load_factor(factor_rest, 1, 4)
-        for i in range(1, ROW_TILES):
+        load_w1(1)
+        for i in range(1, 5):
             load_page(i)
-        nc.sync.dma_start(idx2[:], offs2)
         for a in range(2):
             nc.sync.dma_start(tab2_w[:, T2 * a : T2 * (a + 1)], tab2_words[a].rearrange("p t i -> p (t i)").bitcast(I32))
         nc.sync.dma_start(idx4[:], offs4)
         with nc.allow_non_contiguous_dma(reason="512 gains, one to a partition"):
             nc.sync.dma_start(gain_t[:], gain.rearrange("(c p) -> p c", p=P))
+        for i in range(5, LAST):
+            load_page(i)
         for q in range(4):
             nc.scalar.dma_start(scale_rows(w4_plane_raw, q), w4_scales[0, 4 * q : 4 * q + 4, :].bitcast(I32))
-        for q in range(4):
-            nc.gpsimd.dma_start(scale_rows(tab2_plane, q, 8), tab2_scales[:, 4 * q : 4 * q + 4, :].bitcast(I32))
+        nc.gpsimd.dma_start(c2_t[:].rearrange("p (a t) -> p a t", t=4), c2.rearrange("(a p t) -> p a t", a=2, t=4))
+        nc.gpsimd.dma_start(c3_t[:].rearrange("p (a t) -> p a t", t=4), c3.rearrange("(a p t) -> p a t", a=2, t=4))
 
         for q in range(4):
             nc.vector.tensor_copy(scale_rows(tab_plane, q), scale_rows(tab_rows, q))
@@ -152,6 +155,9 @@ def tile_list_checkers_endgame_retrieval_kernel(
         )
         for h in range(2):
             nc.vector.tensor_copy(v_codes[h][:], tab_w[:].bitcast(U32).indirect(list_half(idx, h)))
+
+        v2_plane = keep.tile([P, S2], U8, name="v2_plane", align_bytes=64)
+        nc.vector.tensor_copy(v2_plane[:], tab2_plane[:].indirect(idx2[:]))
 
         lin = {}
         terms = {}
@@ -204,11 +210,13 @@ def tile_list_checkers_endgame_retrieval_kernel(
         def polynomial(i):
             square, affine, linear = terms[i]
             nc.gpsimd.tensor_tensor(cubic[i][:], cubic[i][:], linear[:], ADD)
-            if i < LAST:
+            if i < LAST - 1:
                 high_terms(i + 1)
             if i < LAST:
                 weigh(i, nc.gpsimd)
-            else:
+            if i == LAST - 1:
+                high_terms(LAST)
+            if i == LAST:
                 nc.gpsimd.tensor_tensor(affine[:, FIRST_PIECE:], cubic[i][:, FIRST_PIECE:], factor[3][:, FIRST_PIECE:], MULT)
 
         def scatter(i):
@@ -218,29 +226,26 @@ def tile_list_checkers_endgame_retrieval_kernel(
 
         def stage_page(i):
             a, t = divmod(i, 4)
-            for half in range(2):
-                if t == 0:
-                    rows = 4 - 2 * a
-                    base = (STAGE0, STAGE1)[a] + rows * 4 * KIB * half
-                    stage[a, half] = place("stage%d%d" % (a, half), [P, rows, 2 * N], F32, base)
-                nc.scalar.dma_start(stage[a, half][:, t, :], pages[i][:, 2 * N * half : 2 * N * (half + 1)])
+            if t == 0:
+                stage[a] = place("stage%d" % a, [P, 4 - 2 * a, T2], F32, (STAGE0, STAGE1)[a])
+            nc.scalar.dma_start(stage[a][:, t, :], pages[i][:])
 
         woven = {}
 
-        def weave(a, half, c):
-            if c == 0:
-                base = STAGE0 if (a, half) == (1, 0) else PAGES + 8 * KIB * half
-                woven[a, half] = place("woven%d%d" % (a, half), [P, 2 * N, 4], BF16, base)
-            rows = 4 - 2 * a
+        def woven_part(a, c0, c1):
+            start = max(s0 for b, s0 in woven if b == a and s0 <= c0)
+            return woven[a, start][:, c0 - start : c1 - start, :]
+
+        def weave(a, c0, c1):
             nc.scalar.copy(
-                woven[a, half][:, N * c : N * (c + 1), 0:rows].rearrange("p (g i) t -> p g t i", i=4),
-                stage[a, half][:, :, N * c : N * (c + 1)].rearrange("p t (g i) -> p g t i", i=4),
+                woven_part(a, c0, c1)[:, :, 0 : 4 - 2 * a].rearrange("p (g i) t -> p g t i", i=4),
+                stage[a][:, :, c0:c1].rearrange("p t (g i) -> p g t i", i=4),
             )
 
-        def weave_row(t, half, c):
-            src = pages[4 + t][:, N * (2 * half + c) : N * (2 * half + c + 1)]
-            dst = woven[1, half][:, N * c : N * (c + 1), t]
-            if half == 0:
+        def weave_row(t, c0, c1):
+            src = pages[4 + t][:, c0:c1]
+            dst = woven_part(1, c0, c1)[:, :, t]
+            if c0 < SCALAR_COLUMNS:
                 nc.scalar.copy(dst, src)
             else:
                 nc.gpsimd.tensor_scalar(dst, src, 1.0, 0.0, MULT, ADD)
@@ -248,10 +253,9 @@ def tile_list_checkers_endgame_retrieval_kernel(
         codes = {}
 
         def quantize_page(a, c0, c1):
-            half = c0 // 2
             nc.vector.quantize_mx(
-                out=codes[a][:, N * c0 : N * c1].bitcast(FP8X4), scales=page_plane[a][:, N * c0 : N * c1],
-                in_=woven[a, half][:, N * (c0 - 2 * half) : N * (c1 - 2 * half), :].rearrange("p c t -> p (c t)"),
+                out=codes[a][:, c0:c1].bitcast(FP8X4), scales=page_plane[a][:, c0:c1],
+                in_=woven_part(a, c0, c1).rearrange("p c t -> p (c t)"),
             )
 
         first_product(0)
@@ -259,12 +263,12 @@ def tile_list_checkers_endgame_retrieval_kernel(
         horner(0)
         weigh(0, nc.vector)
         horner(1)
-        quantize_w1(1)
         first_product(2)
         first_product(3)
         high_terms(2)
         weigh(1, nc.gpsimd)
         scatter(0)
+        quantize_w1(1)
         stage_page(0)
         first_product(4)
         for i in range(1, ROW_TILES):
@@ -273,7 +277,7 @@ def tile_list_checkers_endgame_retrieval_kernel(
             if i == LAST:
                 codes[0] = place("page_codes0", [P, T2], U32, AFFINE + 8 * KIB)
                 for half in range(2):
-                    quantize_page(0, 2 * half, 2 * half + 2)
+                    quantize_page(0, 2 * N * half, 2 * N * (half + 1))
                 piece = place("first_piece", [P, FIRST_PIECE], F32, PAGES + 8 * KIB - 2 * FIRST_PIECE)
                 nc.vector.tensor_tensor(piece[:], cubic[i][:, :FIRST_PIECE], factor[3][:, :FIRST_PIECE], MULT)
                 nc.vector.tensor_copy(pages[i][:].indirect(idx3[:, : FIRST_PIECE // 16]), piece[:])
@@ -284,64 +288,70 @@ def tile_list_checkers_endgame_retrieval_kernel(
                 stage_page(i)
             if i + 4 < ROW_TILES:
                 first_product(i + 4)
+            if i == 4:
+                pages.append(place("page_last", [P, T2], F32, PAGES + 8 * KIB * i))
+                load_page(LAST)
             if i == 3:
                 for half in range(2):
-                    for c in range(2):
-                        weave(0, half, c)
+                    woven[0, 2 * N * half] = place("woven0%d" % half, [P, 2 * N, 4], BF16, PAGES + 8 * KIB * half)
+                for c in range(4):
+                    weave(0, N * c, N * (c + 1))
             if i == 5:
-                for c in range(2):
-                    weave(1, 0, c)
+                woven[1, 0] = place("woven_scalar", [P, SCALAR_COLUMNS, 4], BF16, STAGE0)
+                weave(1, 0, SCALAR_COLUMNS)
             if i == 6:
-                for c in range(2):
-                    weave_row(2, 0, c)
-        for c in range(2):
-            weave(1, 1, c)
-        for c in range(2):
-            weave_row(2, 1, c)
+                weave_row(2, 0, SCALAR_COLUMNS)
+        woven[1, SCALAR_COLUMNS] = place("woven_gpsimd", [P, T2 - SCALAR_COLUMNS, 4], BF16, PAGES + 9 * KIB)
+        weave(1, SCALAR_COLUMNS, T2)
+        weave_row(2, SCALAR_COLUMNS, T2)
 
-        v2_plane = place("v2_plane", [P, S2], U8, AFFINE + 16 * KIB)
-        v2_codes = place("v2_codes", [P, 2 * S2], U32, AFFINE + 16 * KIB + S2)
-        nc.vector.tensor_copy(v2_plane[:], tab2_plane[:].indirect(idx2[:]))
+        v2_codes = place("v2_codes", [P, 2 * S2], U32, AFFINE + 16 * KIB)
         for a in range(2):
             nc.vector.tensor_copy(v2_codes[:, S2 * a : S2 * (a + 1)], tab2_w[:, T2 * a : T2 * (a + 1)].bitcast(U32).indirect(idx2[:]))
-        for c in range(2):
-            for half in range(2):
-                weave_row(3, half, c)
+        weave_row(3, SCALAR_COLUMNS, T2)
+        for c0, c1 in ((0, N), (N, 2 * N), (2 * N, SCALAR_COLUMNS)):
+            weave_row(3, c0, c1)
 
         score = {}
 
         def second_product(n, a, c):
-            if a == 0:
-                score[n, c] = psum.tile([P, N], F32, name="score", tag="bank%d" % (4 * (n % 2) + c))
+            first = a == n // 2
+            if first:
+                score[n, c] = psum.tile([P, N], F32, name="score", tag="bank%d" % (4 * (n % 2) + (c if n < 2 else mirror[c])))
             nc.tensor.matmul_mx(
                 out=score[n, c][:],
                 lhsT=v2_codes[:, S2 * a + P * n : S2 * a + P * (n + 1)].bitcast(FP8X4),
                 lhsT_scale=v2_plane[4 * a : P, P * n : P * (n + 1)],
                 rhs=codes[a][:, N * c : N * (c + 1)].bitcast(FP8X4), rhs_scale=page_plane[a][:, N * c : N * (c + 1)],
-                start=(a == 0), stop=(a == 1),
+                start=first, stop=not first,
             )
 
-        order = (0, 2, 1, 3)
+        order = (0, 1, 3, 2)
+        mirror = dict(zip(order, reversed(order)))
         for n in range(2):
             for c in order:
                 second_product(n, 0, c)
-        codes[1] = place("page_codes1", [P, T2], U32, STAGE0 + 16 * KIB)
+        codes[1] = place("page_codes1", [P, T2], U32, TAB2)
         for c in order:
-            quantize_page(1, c, c + 1)
-            for n in range(2):
-                second_product(n, 1, c)
+            cuts = [N * c] + [SCALAR_COLUMNS] * (N * c < SCALAR_COLUMNS < N * (c + 1)) + [N * (c + 1)]
+            for c0, c1 in reversed(list(zip(cuts, cuts[1:]))):
+                quantize_page(1, c0, c1)
+            second_product(0, 1, c)
+        for c in order:
+            second_product(1, 1, c)
 
         score_sb = {}
         for n in range(S2 // P):
-            score_sb[n] = place("score_sb%d" % n, [P, T2], F32, PAGES + 8 * KIB * (2 + n))
-            for c in order:
-                if (n, c) == (0, 3):
+            score_sb[n] = place("score_sb%d" % n, [P, T2], F32, PAGES + 8 * KIB * (2, 3, 5, 7)[n])
+            for c in order if n < 2 else reversed(order):
+                if n == 0 and c in order[2:]:
                     nc.vector.tensor_copy(score_sb[n][:, N * c : N * (c + 1)], score[n, c][:])
                 else:
                     nc.scalar.copy(score_sb[n][:, N * c : N * (c + 1)], score[n, c][:])
-                if n + 2 < S2 // P:
-                    second_product(n + 2, 0, c)
+            if n + 2 < S2 // P:
+                for c in reversed(order):
                     second_product(n + 2, 1, c)
+                    second_product(n + 2, 0, c)
         for n in range(S2 // P):
             picked = place("picked%d" % n, [P, PQ], F32, FACTOR + 4 * KIB * n)
             result = place("result%d" % n, [P, PQ], F32, SQUARE + 4 * KIB * n)

@@ -25,7 +25,7 @@ LAST = ROW_TILES - 1
 KIB = 1024
 SCALAR_COLUMNS = 1280
 FIRST_PIECE = 256
-ON_VECTOR = 2
+ON_VECTOR = 3
 
 PAGES = 0
 FACTOR = PAGES + 64 * KIB
@@ -83,9 +83,8 @@ def tile_list_checkers_endgame_retrieval_kernel(
         w4_raw = place("w4_raw", [P, 2 * H], U8, STAGE1 + 8 * KIB)
         w4_plane_raw = place("w4_plane_raw", [P, H], U8, STAGE1 + 10 * KIB)
         tab2_w = place("tab2_w", [P, 2 * T2], I32, TAB2)
-        factor_first = place("factor_first", [P, 1, S], F32, FACTOR)
-        factor_rest = place("factor_rest", [P, 3, S], F32, FACTOR + 4 * KIB)
-        factor = [factor_first[:, 0, :]] + [factor_rest[:, u, :] for u in range(3)]
+        factor_pairs = [place("factor%d" % u, [P, 2, S], F32, FACTOR + 8 * KIB * u) for u in range(2)]
+        factor = [factor_pairs[t // 2][:, t % 2, :] for t in range(4)]
         pages = [place("page%d" % i, [P, T2], F32, PAGES + 8 * KIB * i) for i in range(LAST)]
 
         nc.vector.memset(w4_plane_raw[:].bitcast(I32), 0)
@@ -95,30 +94,31 @@ def tile_list_checkers_endgame_retrieval_kernel(
         def load_w1(a):
             nc.sync.dma_start(w1_raw[a][:], w1[:, N * a : N * (a + 1)].rearrange("(p j) c -> p j c", j=4))
 
-        def load_factor(tile, t0, t1):
-            src = wgs.rearrange("(q t) j -> q t j", t=4)[:, t0:t1, :]
+        def load_factors(u):
+            src = wgs.rearrange("(q t) j -> q t j", t=4)[:, 2 * u : 2 * u + 2, :]
             for g in (0, 2, 1, 3):
-                nc.sync.dma_start(tile[32 * g : 32 * (g + 1), :, :], src)
+                nc.sync.dma_start(factor_pairs[u][32 * g : 32 * (g + 1), :, :], src)
 
         def load_page(i):
             a, t = divmod(i, 4)
             nc.sync.dma_start(pages[i][:], page0[N * a : N * (a + 1), :].rearrange("(p t) c -> t p c", t=4)[t])
 
+        nc.sync.dma_start(idx[:], offs)
         for q in range(4):
             nc.sync.dma_start(scale_rows(tab_rows, q), tab_scales[0, 4 * q : 4 * q + 4, :].bitcast(I32))
-        nc.sync.dma_start(idx[:], offs)
+        nc.sync.dma_start(tab_w[:], tab_words[0].rearrange("p t i -> p (t i)").bitcast(I32))
         nc.sync.dma_start(w4_raw[:].bitcast(I32), w4_words[0].bitcast(I32))
         load_w1(0)
-        nc.sync.dma_start(tab_w[:], tab_words[0].rearrange("p t i -> p (t i)").bitcast(I32))
         nc.sync.dma_start(idx2[:], offs2)
         for q in range(4):
             nc.sync.dma_start(scale_rows(tab2_plane, q, 8), tab2_scales[:, 4 * q : 4 * q + 4, :].bitcast(I32))
-        load_factor(factor_first, 0, 1)
+        load_factors(0)
         load_page(0)
         nc.sync.dma_start(idx3[:], offs3)
-        load_factor(factor_rest, 1, 4)
         load_w1(1)
-        for i in range(1, 5):
+        load_page(1)
+        load_factors(1)
+        for i in range(2, 5):
             load_page(i)
         for a in range(2):
             nc.sync.dma_start(tab2_w[:, T2 * a : T2 * (a + 1)], tab2_words[a].rearrange("p t i -> p (t i)").bitcast(I32))
@@ -140,21 +140,23 @@ def tile_list_checkers_endgame_retrieval_kernel(
             w4_raw[:].bitcast(U16).rearrange("p (a m t) -> p a t m", a=2, t=4),
         )
 
-        def quantize_w1(a):
-            grouped = place("w1_grouped%d" % a, [P, 4 * N], BF16, STAGE1 + 12 * KIB + 4 * KIB * a)
+        def quantize_w1(a, t0, t1):
+            grouped = place("w1_grouped%d%d" % (a, t0), [P, (t1 - t0) * N], BF16, STAGE1 + 12 * KIB + KIB * (4 * a + t0))
             nc.scalar.copy(
-                grouped[:].rearrange("p (t m j) -> p m j t", t=4, j=4),
-                w1_raw[a][:].rearrange("p j (m t) -> p m j t", t=4),
+                grouped[:].rearrange("p (t m j) -> p m j t", m=P, j=4),
+                w1_raw[a][:].rearrange("p j (m t) -> p m j t", t=4)[:, :, :, t0:t1],
             )
-            nc.vector.quantize_mx(out=w1_codes[a][:].bitcast(FP8X4), scales=w1_plane[a][:], in_=grouped[:])
+            cols = slice(P * t0, P * t1)
+            nc.vector.quantize_mx(out=w1_codes[a][:, cols].bitcast(FP8X4), scales=w1_plane[a][:, cols], in_=grouped[:])
 
-        quantize_w1(0)
         nc.vector.tensor_copy(
             w4_plane[:].rearrange("p (a t m) -> p a t m", a=2, t=4),
             w4_plane_raw[:].rearrange("p (a m t) -> p a t m", a=2, t=4),
         )
         for h in range(2):
             nc.vector.tensor_copy(v_codes[h][:], tab_w[:].bitcast(U32).indirect(list_half(idx, h)))
+        quantize_w1(0, 0, 2)
+        quantize_w1(0, 2, 4)
 
         v2_plane = keep.tile([P, S2], U8, name="v2_plane", align_bytes=64)
         nc.vector.tensor_copy(v2_plane[:], tab2_plane[:].indirect(idx2[:]))
@@ -261,18 +263,20 @@ def tile_list_checkers_endgame_retrieval_kernel(
         first_product(0)
         first_product(1)
         horner(0)
-        weigh(0, nc.vector)
+        weigh(0, nc.gpsimd)
         horner(1)
         first_product(2)
-        first_product(3)
-        high_terms(2)
         weigh(1, nc.gpsimd)
+        horner(2)
+        first_product(3)
+        high_terms(3)
+        weigh(2, nc.gpsimd)
         scatter(0)
-        quantize_w1(1)
+        quantize_w1(1, 0, 4)
         stage_page(0)
         first_product(4)
         for i in range(1, ROW_TILES):
-            if i + 1 < ROW_TILES:
+            if ON_VECTOR <= i + 1 < ROW_TILES:
                 polynomial(i + 1)
             if i == LAST:
                 codes[0] = place("page_codes0", [P, T2], U32, AFFINE + 8 * KIB)

@@ -113,9 +113,9 @@ def tile_list_checkers_endgame_retrieval_kernel(
         for q in range(4):
             nc.sync.dma_start(scale_rows(tab2_plane, q, 8), tab2_scales[:, 4 * q : 4 * q + 4, :].bitcast(I32))
         load_factors(0)
+        load_w1(1)
         load_page(0)
         nc.sync.dma_start(idx3[:], offs3)
-        load_w1(1)
         load_page(1)
         load_factors(1)
         for i in range(2, 5):
@@ -169,8 +169,8 @@ def tile_list_checkers_endgame_retrieval_kernel(
             affine = place("affine%d" % i, [P, S], F32, AFFINE + 4 * KIB * ((i + 2) % 5))
             square = linear = None
             if i >= ON_VECTOR:
-                square = place("square%d" % i, [P, S], F32, SQUARE + 4 * KIB * (i % 3))
-                linear = place("linear%d" % i, [P, S], F32, LINEAR + 4 * KIB * (i % 4))
+                square = place("square%d" % i, [P, S], F32, STAGE0 + 24 * KIB if i == ON_VECTOR else SQUARE + 4 * KIB * (i % 3))
+                linear = place("linear%d" % i, [P, S], F32, STAGE0 + 28 * KIB if i == ON_VECTOR else LINEAR + 4 * KIB * (i % 4))
             for h in range(2):
                 cols = slice(N * h, N * (h + 1))
                 lin[i, h] = psum.tile([P, N], F32, name="lin", tag="bank%d" % (2 * (i % 3) + h))
@@ -227,10 +227,12 @@ def tile_list_checkers_endgame_retrieval_kernel(
         stage = {}
 
         def stage_page(i):
-            a, t = divmod(i, 4)
-            if t == 0:
-                stage[a] = place("stage%d" % a, [P, 4 - 2 * a, T2], F32, (STAGE0, STAGE1)[a])
-            nc.scalar.dma_start(stage[a][:, t, :], pages[i][:])
+            pair, e = divmod(i, 2)
+            for half in range(2):
+                if e == 0:
+                    base = (STAGE0 + 16 * KIB, STAGE0, STAGE1)[pair] + 8 * KIB * (1 - half)
+                    stage[pair, half] = place("stage%d%d" % (pair, half), [P, 2, 2 * N], F32, base)
+                nc.scalar.dma_start(stage[pair, half][:, e, :], pages[i][:, 2 * N * half : 2 * N * (half + 1)])
 
         woven = {}
 
@@ -238,11 +240,15 @@ def tile_list_checkers_endgame_retrieval_kernel(
             start = max(s0 for b, s0 in woven if b == a and s0 <= c0)
             return woven[a, start][:, c0 - start : c1 - start, :]
 
-        def weave(a, c0, c1):
-            nc.scalar.copy(
-                woven_part(a, c0, c1)[:, :, 0 : 4 - 2 * a].rearrange("p (g i) t -> p g t i", i=4),
-                stage[a][:, :, c0:c1].rearrange("p t (g i) -> p g t i", i=4),
-            )
+        def weave(pair, c0, c1):
+            a, t0 = pair // 2, 2 * (pair % 2)
+            half = c0 // (2 * N)
+            dst = woven_part(a, c0, c1)[:, :, t0 : t0 + 2].rearrange("p (g i) t -> p g t i", i=4)
+            src = stage[pair, half][:, :, c0 - 2 * N * half : c1 - 2 * N * half].rearrange("p t (g i) -> p g t i", i=4)
+            if a == 0 or c0 < SCALAR_COLUMNS:
+                nc.scalar.copy(dst, src)
+            else:
+                nc.gpsimd.tensor_scalar(dst, src, 1.0, 0.0, MULT, ADD)
 
         def weave_row(t, c0, c1):
             src = pages[4 + t][:, c0:c1]
@@ -268,14 +274,15 @@ def tile_list_checkers_endgame_retrieval_kernel(
         first_product(2)
         weigh(1, nc.gpsimd)
         horner(2)
+        quantize_w1(1, 0, 4)
         first_product(3)
         high_terms(3)
-        weigh(2, nc.gpsimd)
         scatter(0)
-        quantize_w1(1, 0, 4)
         stage_page(0)
         first_product(4)
         for i in range(1, ROW_TILES):
+            if i + 1 == ON_VECTOR - 1:
+                weigh(i + 1, nc.gpsimd)
             if ON_VECTOR <= i + 1 < ROW_TILES:
                 polynomial(i + 1)
             if i == LAST:
@@ -295,18 +302,20 @@ def tile_list_checkers_endgame_retrieval_kernel(
             if i == 4:
                 pages.append(place("page_last", [P, T2], F32, PAGES + 8 * KIB * i))
                 load_page(LAST)
-            if i == 3:
+            if i == 1:
                 for half in range(2):
                     woven[0, 2 * N * half] = place("woven0%d" % half, [P, 2 * N, 4], BF16, PAGES + 8 * KIB * half)
-                for c in range(4):
-                    weave(0, N * c, N * (c + 1))
+            if i in (1, 3):
+                for half in range(2):
+                    weave(i // 2, 2 * N * half, 2 * N * (half + 1))
             if i == 5:
-                woven[1, 0] = place("woven_scalar", [P, SCALAR_COLUMNS, 4], BF16, STAGE0)
-                weave(1, 0, SCALAR_COLUMNS)
+                woven[1, 0] = place("woven_scalar", [P, SCALAR_COLUMNS, 4], BF16, STAGE0 + 16 * KIB)
+                weave(2, 0, 2 * N)
+                weave(2, 2 * N, SCALAR_COLUMNS)
             if i == 6:
                 weave_row(2, 0, SCALAR_COLUMNS)
-        woven[1, SCALAR_COLUMNS] = place("woven_gpsimd", [P, T2 - SCALAR_COLUMNS, 4], BF16, PAGES + 9 * KIB)
-        weave(1, SCALAR_COLUMNS, T2)
+        woven[1, SCALAR_COLUMNS] = place("woven_gpsimd", [P, T2 - SCALAR_COLUMNS, 4], BF16, CUBIC + 4 * KIB)
+        weave(2, SCALAR_COLUMNS, T2)
         weave_row(2, SCALAR_COLUMNS, T2)
 
         v2_codes = place("v2_codes", [P, 2 * S2], U32, AFFINE + 16 * KIB)
@@ -359,10 +368,9 @@ def tile_list_checkers_endgame_retrieval_kernel(
         for n in range(S2 // P):
             picked = place("picked%d" % n, [P, PQ], F32, FACTOR + 4 * KIB * n)
             result = place("result%d" % n, [P, PQ], F32, SQUARE + 4 * KIB * n)
-            pieces = 2 if n == S2 // P - 1 else 1
-            width = PQ // pieces
-            for u in range(pieces):
-                cols = slice(width * u, width * (u + 1))
-                nc.vector.tensor_copy(picked[:, cols], score_sb[n][:].indirect(idx4[:, width // 16 * u : width // 16 * (u + 1)]))
+            cuts = (0, 512, 768, PQ) if n == S2 // P - 1 else (0, PQ)
+            for c0, c1 in zip(cuts, cuts[1:]):
+                cols = slice(c0, c1)
+                nc.vector.tensor_copy(picked[:, cols], score_sb[n][:].indirect(idx4[:, c0 // 16 : c1 // 16]))
                 nc.scalar.activation(result[:, cols], picked[:, cols], ACT.Tanh, scale=gain_t[:, n : n + 1])
                 nc.sync.dma_start(out[P * n : P * (n + 1), cols], result[:, cols])

@@ -31,10 +31,10 @@ PAGES = 0
 FACTOR = PAGES + 64 * KIB
 SQUARE = FACTOR + 16 * KIB
 CUBIC = SQUARE + 12 * KIB
-LINEAR = CUBIC + 8 * KIB
-AFFINE = LINEAR + 16 * KIB
+LINEAR = CUBIC + 12 * KIB
+AFFINE = LINEAR + 12 * KIB
 TAB2 = AFFINE + 21 * KIB
-STAGE0 = TAB2 + 16 * KIB
+STAGE0 = TAB2 + 16 * KIB + S2
 STAGE1 = STAGE0 + 32 * KIB
 SMALL = STAGE1 + 24 * KIB
 
@@ -76,7 +76,7 @@ def tile_list_checkers_endgame_retrieval_kernel(
         v_codes = [keep.tile([P, N], U32, name="v_codes%d" % h, align_bytes=64) for h in range(2)]
         page_plane = [keep.tile([P, T2], U8, name="page_plane%d" % a, align_bytes=64) for a in range(2)]
 
-        tab_w = place("tab_w", [P, T], I32, STAGE0)
+        tab_w = place("tab_w", [P, T], I32, STAGE0 - S2)
         w1_raw = [place("w1_raw0", [P, 4, N], F32, STAGE0 + 16 * KIB), place("w1_raw1", [P, 4, N], F32, STAGE0 + 24 * KIB)]
         tab_rows = place("tab_rows", [P, T], U8, STAGE1)
         tab_plane = place("tab_plane", [P, T], U8, STAGE1 + 4 * KIB)
@@ -106,12 +106,12 @@ def tile_list_checkers_endgame_retrieval_kernel(
         nc.sync.dma_start(idx[:], offs)
         for q in range(4):
             nc.sync.dma_start(scale_rows(tab_rows, q), tab_scales[0, 4 * q : 4 * q + 4, :].bitcast(I32))
-        nc.sync.dma_start(tab_w[:], tab_words[0].rearrange("p t i -> p (t i)").bitcast(I32))
         nc.sync.dma_start(w4_raw[:].bitcast(I32), w4_words[0].bitcast(I32))
-        load_w1(0)
         nc.sync.dma_start(idx2[:], offs2)
-        for q in range(4):
-            nc.sync.dma_start(scale_rows(tab2_plane, q, 8), tab2_scales[:, 4 * q : 4 * q + 4, :].bitcast(I32))
+        nc.sync.dma_start(tab_w[:], tab_words[0].rearrange("p t i -> p (t i)").bitcast(I32))
+        load_w1(0)
+        nc.sync.dma_start(c3_t[:].rearrange("p (a t) -> p a t", t=4), c3.rearrange("(a p t) -> p a t", a=2, t=4))
+        nc.sync.dma_start(c2_t[:].rearrange("p (a t) -> p a t", t=4), c2.rearrange("(a p t) -> p a t", a=2, t=4))
         load_factors(0)
         load_w1(1)
         load_page(0)
@@ -128,9 +128,9 @@ def tile_list_checkers_endgame_retrieval_kernel(
         for i in range(5, LAST):
             load_page(i)
         for q in range(4):
+            nc.gpsimd.dma_start(scale_rows(tab2_plane, q, 8), tab2_scales[:, 4 * q : 4 * q + 4, :].bitcast(I32))
+        for q in range(4):
             nc.scalar.dma_start(scale_rows(w4_plane_raw, q), w4_scales[0, 4 * q : 4 * q + 4, :].bitcast(I32))
-        nc.gpsimd.dma_start(c2_t[:].rearrange("p (a t) -> p a t", t=4), c2.rearrange("(a p t) -> p a t", a=2, t=4))
-        nc.gpsimd.dma_start(c3_t[:].rearrange("p (a t) -> p a t", t=4), c3.rearrange("(a p t) -> p a t", a=2, t=4))
 
         for q in range(4):
             nc.vector.tensor_copy(scale_rows(tab_plane, q), scale_rows(tab_rows, q))
@@ -158,7 +158,7 @@ def tile_list_checkers_endgame_retrieval_kernel(
         quantize_w1(0, 0, 2)
         quantize_w1(0, 2, 4)
 
-        v2_plane = keep.tile([P, S2], U8, name="v2_plane", align_bytes=64)
+        v2_plane = place("v2_plane", [P, S2], U8, STAGE0 - S2)
         nc.vector.tensor_copy(v2_plane[:], tab2_plane[:].indirect(idx2[:]))
 
         lin = {}
@@ -170,16 +170,16 @@ def tile_list_checkers_endgame_retrieval_kernel(
             square = linear = None
             if i >= ON_VECTOR:
                 square = place("square%d" % i, [P, S], F32, STAGE0 + 24 * KIB if i == ON_VECTOR else SQUARE + 4 * KIB * (i % 3))
-                linear = place("linear%d" % i, [P, S], F32, STAGE0 + 28 * KIB if i == ON_VECTOR else LINEAR + 4 * KIB * (i % 4))
+                linear = place("linear%d" % i, [P, S], F32, STAGE0 + 28 * KIB if i == ON_VECTOR else LINEAR + 4 * KIB * (i % 3))
             for h in range(2):
                 cols = slice(N * h, N * (h + 1))
                 lin[i, h] = psum.tile([P, N], F32, name="lin", tag="bank%d" % (2 * (i % 3) + h))
                 nc.tensor.matmul_mx(
-                    out=lin[i, h][:], lhsT=w1_codes[a][:, P * t : P * (t + 1)].bitcast(FP8X4), lhsT_scale=w1_plane[a][:, P * t : P * (t + 1)],
+                    out=lin[i, h][:], lhsT=w4_codes[:, 2 * P * i : 2 * P * (i + 1)].bitcast(FP4X4), lhsT_scale=w4_plane[:, P * i : P * (i + 1)],
                     rhs=v_codes[h][:].bitcast(FP8X4), rhs_scale=v_plane[:, cols], start=True, stop=False,
                 )
                 nc.tensor.matmul_mx(
-                    out=lin[i, h][:], lhsT=w4_codes[:, 2 * P * i : 2 * P * (i + 1)].bitcast(FP4X4), lhsT_scale=w4_plane[:, P * i : P * (i + 1)],
+                    out=lin[i, h][:], lhsT=w1_codes[a][:, P * t : P * (t + 1)].bitcast(FP8X4), lhsT_scale=w1_plane[a][:, P * t : P * (t + 1)],
                     rhs=v_codes[h][:].bitcast(FP8X4), rhs_scale=v_plane[:, cols], start=False, stop=True,
                 )
                 nc.scalar.activation(affine[:, cols], lin[i, h][:], ACT.Identity, bias=c2_t[:, i : i + 1], scale=c3_t[:, i : i + 1])
@@ -192,9 +192,12 @@ def tile_list_checkers_endgame_retrieval_kernel(
 
         cubic = {}
 
+        def cubic_tile(i):
+            return place("cubic%d" % i, [P, S], F32, CUBIC + 4 * KIB * (0 if i == 0 else 1 + (i + 1) % 2))
+
         def horner(i):
             affine = terms[i][1]
-            cubic[i] = place("cubic%d" % i, [P, S], F32, CUBIC + 4 * KIB * (i % 2))
+            cubic[i] = cubic_tile(i)
             halves = [slice(N * h, N * (h + 1)) for h in range(2)]
             for h in range(2):
                 nc.vector.tensor_tensor(cubic[i][:, halves[h]], affine[:, halves[h]], lin[i, h][:], MULT)
@@ -206,7 +209,7 @@ def tile_list_checkers_endgame_retrieval_kernel(
 
         def high_terms(i):
             square, affine, linear = terms[i]
-            cubic[i] = place("cubic%d" % i, [P, S], F32, CUBIC + 4 * KIB * (i % 2))
+            cubic[i] = cubic_tile(i)
             nc.gpsimd.tensor_tensor(cubic[i][:], square[:], affine[:], MULT)
 
         def polynomial(i):

@@ -24,7 +24,6 @@ ROW_TILES = H // P
 LAST = ROW_TILES - 1
 KIB = 1024
 SCALAR_COLUMNS = 1280
-FIRST_PIECE = 256
 ON_VECTOR = 3
 
 PAGES = 0
@@ -77,7 +76,8 @@ def tile_list_checkers_endgame_retrieval_kernel(
         page_plane = [keep.tile([P, T2], U8, name="page_plane%d" % a, align_bytes=64) for a in range(2)]
 
         tab_w = place("tab_w", [P, T], I32, STAGE0 - S2)
-        w1_raw = [place("w1_raw0", [P, 4, N], F32, STAGE0 + 16 * KIB), place("w1_raw1", [P, 4, N], F32, STAGE0 + 24 * KIB)]
+        w1_early = [place("w1_early%d" % u, [P, 4, N // 2], F32, STAGE0 + (16 + 4 * u) * KIB) for u in range(2)]
+        w1_late = place("w1_late", [P, 4, N], F32, STAGE0 + 24 * KIB)
         tab_rows = place("tab_rows", [P, T], U8, STAGE1)
         tab_plane = place("tab_plane", [P, T], U8, STAGE1 + 4 * KIB)
         w4_raw = place("w4_raw", [P, 2 * H], U8, STAGE1 + 8 * KIB)
@@ -91,8 +91,8 @@ def tile_list_checkers_endgame_retrieval_kernel(
         nc.vector.memset(tab_plane[:].bitcast(I32), 0)
         nc.gpsimd.memset(tab2_plane[:].bitcast(I32), 0)
 
-        def load_w1(a):
-            nc.sync.dma_start(w1_raw[a][:], w1[:, N * a : N * (a + 1)].rearrange("(p j) c -> p j c", j=4))
+        def load_w1(tile, c0, c1):
+            nc.sync.dma_start(tile[:], w1[:, c0:c1].rearrange("(p j) c -> p j c", j=4))
 
         def load_factors(u):
             src = wgs.rearrange("(q t) j -> q t j", t=4)[:, 2 * u : 2 * u + 2, :]
@@ -109,16 +109,16 @@ def tile_list_checkers_endgame_retrieval_kernel(
         nc.sync.dma_start(w4_raw[:].bitcast(I32), w4_words[0].bitcast(I32))
         nc.sync.dma_start(idx2[:], offs2)
         nc.sync.dma_start(tab_w[:], tab_words[0].rearrange("p t i -> p (t i)").bitcast(I32))
-        load_w1(0)
+        for u in range(2):
+            load_w1(w1_early[u], N // 2 * u, N // 2 * (u + 1))
         nc.sync.dma_start(c3_t[:].rearrange("p (a t) -> p a t", t=4), c3.rearrange("(a p t) -> p a t", a=2, t=4))
         nc.sync.dma_start(c2_t[:].rearrange("p (a t) -> p a t", t=4), c2.rearrange("(a p t) -> p a t", a=2, t=4))
         load_factors(0)
-        load_w1(1)
+        load_w1(w1_late, N, H)
         load_page(0)
         nc.sync.dma_start(idx3[:], offs3)
-        load_page(1)
         load_factors(1)
-        for i in range(2, 5):
+        for i in range(1, 5):
             load_page(i)
         for a in range(2):
             nc.sync.dma_start(tab2_w[:, T2 * a : T2 * (a + 1)], tab2_words[a].rearrange("p t i -> p (t i)").bitcast(I32))
@@ -140,14 +140,17 @@ def tile_list_checkers_endgame_retrieval_kernel(
             w4_raw[:].bitcast(U16).rearrange("p (a m t) -> p a t m", a=2, t=4),
         )
 
-        def quantize_w1(a, t0, t1):
-            grouped = place("w1_grouped%d%d" % (a, t0), [P, (t1 - t0) * N], BF16, STAGE1 + 12 * KIB + KIB * (4 * a + t0))
+        grouped = [place("w1_grouped%d" % a, [P, 4 * N], BF16, STAGE1 + (12 + 4 * a) * KIB) for a in range(2)]
+
+        def group_w1(a, raw, m0, m1, t0, t1):
             nc.scalar.copy(
-                grouped[:].rearrange("p (t m j) -> p m j t", m=P, j=4),
-                w1_raw[a][:].rearrange("p j (m t) -> p m j t", t=4)[:, :, :, t0:t1],
+                grouped[a][:].rearrange("p (t m j) -> p m j t", m=P, j=4)[:, m0:m1, :, t0:t1],
+                raw[:].rearrange("p j (m t) -> p m j t", t=4)[:, :, :, t0:t1],
             )
+
+        def quantize_w1(a, t0, t1):
             cols = slice(P * t0, P * t1)
-            nc.vector.quantize_mx(out=w1_codes[a][:, cols].bitcast(FP8X4), scales=w1_plane[a][:, cols], in_=grouped[:])
+            nc.vector.quantize_mx(out=w1_codes[a][:, cols].bitcast(FP8X4), scales=w1_plane[a][:, cols], in_=grouped[a][:, N * t0 : N * t1])
 
         nc.vector.tensor_copy(
             w4_plane[:].rearrange("p (a t m) -> p a t m", a=2, t=4),
@@ -155,8 +158,10 @@ def tile_list_checkers_endgame_retrieval_kernel(
         )
         for h in range(2):
             nc.vector.tensor_copy(v_codes[h][:], tab_w[:].bitcast(U32).indirect(list_half(idx, h)))
-        quantize_w1(0, 0, 2)
-        quantize_w1(0, 2, 4)
+        group_w1(0, w1_early[0], 0, P // 2, 0, 4)
+        for t0 in (0, 2):
+            group_w1(0, w1_early[1], P // 2, P, t0, t0 + 2)
+            quantize_w1(0, t0, t0 + 2)
 
         v2_plane = place("v2_plane", [P, S2], U8, STAGE0 - S2)
         nc.vector.tensor_copy(v2_plane[:], tab2_plane[:].indirect(idx2[:]))
@@ -166,7 +171,7 @@ def tile_list_checkers_endgame_retrieval_kernel(
 
         def first_product(i):
             a, t = divmod(i, 4)
-            affine = place("affine%d" % i, [P, S], F32, AFFINE + 4 * KIB * ((i + 2) % 5))
+            affine = place("affine%d" % i, [P, S], F32, STAGE1 + 16 * KIB if i == ON_VECTOR else AFFINE + 4 * KIB * ((i + 2) % 5))
             square = linear = None
             if i >= ON_VECTOR:
                 square = place("square%d" % i, [P, S], F32, STAGE0 + 24 * KIB if i == ON_VECTOR else SQUARE + 4 * KIB * (i % 3))
@@ -217,12 +222,9 @@ def tile_list_checkers_endgame_retrieval_kernel(
             nc.gpsimd.tensor_tensor(cubic[i][:], cubic[i][:], linear[:], ADD)
             if i < LAST - 1:
                 high_terms(i + 1)
-            if i < LAST:
-                weigh(i, nc.gpsimd)
+            weigh(i, nc.gpsimd)
             if i == LAST - 1:
                 high_terms(LAST)
-            if i == LAST:
-                nc.gpsimd.tensor_tensor(affine[:, FIRST_PIECE:], cubic[i][:, FIRST_PIECE:], factor[3][:, FIRST_PIECE:], MULT)
 
         def scatter(i):
             nc.vector.tensor_copy(pages[i][:].indirect(idx3[:]), terms[i][1][:])
@@ -277,6 +279,7 @@ def tile_list_checkers_endgame_retrieval_kernel(
         first_product(2)
         weigh(1, nc.gpsimd)
         horner(2)
+        group_w1(1, w1_late, 0, P, 0, 4)
         quantize_w1(1, 0, 4)
         first_product(3)
         high_terms(3)
@@ -292,12 +295,7 @@ def tile_list_checkers_endgame_retrieval_kernel(
                 codes[0] = place("page_codes0", [P, T2], U32, AFFINE + 8 * KIB)
                 for half in range(2):
                     quantize_page(0, 2 * N * half, 2 * N * (half + 1))
-                piece = place("first_piece", [P, FIRST_PIECE], F32, PAGES + 8 * KIB - 2 * FIRST_PIECE)
-                nc.vector.tensor_tensor(piece[:], cubic[i][:, :FIRST_PIECE], factor[3][:, :FIRST_PIECE], MULT)
-                nc.vector.tensor_copy(pages[i][:].indirect(idx3[:, : FIRST_PIECE // 16]), piece[:])
-                nc.vector.tensor_copy(pages[i][:].indirect(idx3[:, FIRST_PIECE // 16 :]), terms[i][1][:, FIRST_PIECE:])
-            else:
-                scatter(i)
+            scatter(i)
             if i < LAST - 1:
                 stage_page(i)
             if i + 4 < ROW_TILES:
@@ -317,13 +315,14 @@ def tile_list_checkers_endgame_retrieval_kernel(
                 weave(2, 2 * N, SCALAR_COLUMNS)
             if i == 6:
                 weave_row(2, 0, SCALAR_COLUMNS)
-        woven[1, SCALAR_COLUMNS] = place("woven_gpsimd", [P, T2 - SCALAR_COLUMNS, 4], BF16, CUBIC + 4 * KIB)
+        woven[1, SCALAR_COLUMNS] = place("woven_gpsimd", [P, T2 - SCALAR_COLUMNS, 4], BF16, PAGES + 8 * KIB)
         weave(2, SCALAR_COLUMNS, T2)
         weave_row(2, SCALAR_COLUMNS, T2)
 
         v2_codes = place("v2_codes", [P, 2 * S2], U32, AFFINE + 16 * KIB)
-        for a in range(2):
-            nc.vector.tensor_copy(v2_codes[:, S2 * a : S2 * (a + 1)], tab2_w[:, T2 * a : T2 * (a + 1)].bitcast(U32).indirect(idx2[:]))
+        for a, j0, j1 in ((0, 0, 2 * P), (1, 0, S2), (0, 2 * P, S2)):
+            window = tab2_w[:, T2 * a : T2 * (a + 1)].bitcast(U32)
+            nc.vector.tensor_copy(v2_codes[:, S2 * a + j0 : S2 * a + j1], window.indirect(idx2[:, j0 // 16 : j1 // 16]))
         weave_row(3, SCALAR_COLUMNS, T2)
         for c0, c1 in ((0, N), (N, 2 * N), (2 * N, SCALAR_COLUMNS)):
             weave_row(3, c0, c1)

@@ -23,6 +23,7 @@ LIST_HALF = N // 16
 ROW_TILES = H // P
 LAST = ROW_TILES - 1
 KIB = 1024
+QUADRANTS = (0, 2, 1, 3)
 SCALAR_COLUMNS = 1280
 ON_VECTOR = 3
 
@@ -96,7 +97,7 @@ def tile_list_checkers_endgame_retrieval_kernel(
 
         def load_factors(u):
             src = wgs.rearrange("(q t) j -> q t j", t=4)[:, 2 * u : 2 * u + 2, :]
-            for g in (0, 2, 1, 3):
+            for g in QUADRANTS:
                 nc.sync.dma_start(factor_pairs[u][32 * g : 32 * (g + 1), :, :], src)
 
         def load_page(i):
@@ -104,15 +105,15 @@ def tile_list_checkers_endgame_retrieval_kernel(
             nc.sync.dma_start(pages[i][:], page0[N * a : N * (a + 1), :].rearrange("(p t) c -> t p c", t=4)[t])
 
         nc.sync.dma_start(idx[:], offs)
-        for q in range(4):
+        for q in QUADRANTS:
             nc.sync.dma_start(scale_rows(tab_rows, q), tab_scales[0, 4 * q : 4 * q + 4, :].bitcast(I32))
-        nc.sync.dma_start(w4_raw[:].bitcast(I32), w4_words[0].bitcast(I32))
-        nc.sync.dma_start(idx2[:], offs2)
-        nc.sync.dma_start(tab_w[:], tab_words[0].rearrange("p t i -> p (t i)").bitcast(I32))
-        for u in range(2):
-            load_w1(w1_early[u], N // 2 * u, N // 2 * (u + 1))
         nc.sync.dma_start(c3_t[:].rearrange("p (a t) -> p a t", t=4), c3.rearrange("(a p t) -> p a t", a=2, t=4))
         nc.sync.dma_start(c2_t[:].rearrange("p (a t) -> p a t", t=4), c2.rearrange("(a p t) -> p a t", a=2, t=4))
+        nc.sync.dma_start(tab_w[:], tab_words[0].rearrange("p t i -> p (t i)").bitcast(I32))
+        nc.sync.dma_start(w4_raw[:].bitcast(I32), w4_words[0].bitcast(I32))
+        for u in range(2):
+            load_w1(w1_early[u], N // 2 * u, N // 2 * (u + 1))
+        nc.sync.dma_start(idx2[:], offs2)
         load_factors(0)
         load_w1(w1_late, N, H)
         load_page(0)
@@ -127,9 +128,9 @@ def tile_list_checkers_endgame_retrieval_kernel(
             nc.sync.dma_start(gain_t[:], gain.rearrange("(c p) -> p c", p=P))
         for i in range(5, LAST):
             load_page(i)
-        for q in range(4):
+        for q in QUADRANTS:
             nc.gpsimd.dma_start(scale_rows(tab2_plane, q, 8), tab2_scales[:, 4 * q : 4 * q + 4, :].bitcast(I32))
-        for q in range(4):
+        for q in QUADRANTS:
             nc.scalar.dma_start(scale_rows(w4_plane_raw, q), w4_scales[0, 4 * q : 4 * q + 4, :].bitcast(I32))
 
         for q in range(4):

@@ -1,6 +1,7 @@
 from contextlib import ExitStack
 
 import concourse.mybir as mybir
+from concourse.masks import make_identity
 
 K, H, T, S, T2, S2, PQ = 512, 1024, 4096, 1024, 2048, 512, 1024
 FLOPS = 2 * (2 * K * H * S) + 2 * H * S2 * T2
@@ -16,6 +17,8 @@ FP4X4 = mybir.dt.float4_e2m1fn_x4
 ACT = mybir.ActivationFunctionType
 MULT = mybir.AluOpType.mult
 ADD = mybir.AluOpType.add
+POW = mybir.AluOpType.pow
+IS_GE = mybir.AluOpType.is_ge
 
 P = 128
 N = 512
@@ -25,7 +28,8 @@ LAST = ROW_TILES - 1
 KIB = 1024
 QUADRANTS = (0, 2, 1, 3)
 SCALAR_COLUMNS = 1280
-ON_VECTOR = 3
+ON_VECTOR = 2
+ON_TENSOR = (2, 4, 6)
 
 PAGES = 0
 FACTOR = PAGES + 64 * KIB
@@ -37,6 +41,21 @@ TAB2 = AFFINE + 21 * KIB
 STAGE0 = TAB2 + 16 * KIB + S2
 STAGE1 = STAGE0 + 32 * KIB
 SMALL = STAGE1 + 24 * KIB
+SHARED = STAGE1 + 16 * KIB
+
+
+def slot(base, k):
+    return base + 4 * KIB * k
+
+
+FIRST_AT = (SHARED, slot(AFFINE, 3), slot(AFFINE, 0), slot(AFFINE, 3), slot(AFFINE, 4), SHARED, slot(CUBIC, 1), slot(AFFINE, 3))
+SQUARE_AT = (None, None, slot(AFFINE, 1), slot(SQUARE, 0), slot(SQUARE, 1), slot(SQUARE, 2), slot(STAGE0, 1), slot(SQUARE, 0))
+LINEAR_AT = (None, None, slot(AFFINE, 2), slot(LINEAR, 0), slot(CUBIC, 0), slot(AFFINE, 1), slot(STAGE0, 0), SMALL)
+TURNED_AT = {2: slot(SQUARE, 2), 4: slot(SQUARE, 1), 6: STAGE0 + 30 * KIB}
+QUADRATIC_AT = {2: slot(LINEAR, 1), 4: slot(CUBIC, 0), 6: slot(LINEAR, 0)}
+OPENING_AT = (slot(CUBIC, 0), slot(CUBIC, 1), slot(CUBIC, 1), AFFINE - 2 * KIB, slot(LINEAR, 1), slot(LINEAR, 2), None, slot(CUBIC, 2))
+BANKS_AT = (0, 1, 2, 1, 0, 2, 1, 1)
+CLOSING_AT = {0: slot(AFFINE, 4), 1: SHARED, 4: slot(AFFINE, 0)}
 
 
 def tile_list_checkers_endgame_retrieval_kernel(
@@ -78,14 +97,13 @@ def tile_list_checkers_endgame_retrieval_kernel(
 
         tab_w = place("tab_w", [P, T], I32, STAGE0 - S2)
         w1_early = [place("w1_early%d" % u, [P, 4, N // 2], F32, STAGE0 + (16 + 4 * u) * KIB) for u in range(2)]
-        w1_late = place("w1_late", [P, 4, N], F32, STAGE0 + 24 * KIB)
+        w1_late = place("w1_late", [P, 4, N], F32, AFFINE + 2 * KIB)
         tab_rows = place("tab_rows", [P, T], U8, STAGE1)
         tab_plane = place("tab_plane", [P, T], U8, STAGE1 + 4 * KIB)
         w4_raw = place("w4_raw", [P, 2 * H], U8, STAGE1 + 8 * KIB)
         w4_plane_raw = place("w4_plane_raw", [P, H], U8, STAGE1 + 10 * KIB)
         tab2_w = place("tab2_w", [P, 2 * T2], I32, TAB2)
-        factor_pairs = [place("factor%d" % u, [P, 2, S], F32, FACTOR + 8 * KIB * u) for u in range(2)]
-        factor = [factor_pairs[t // 2][:, t % 2, :] for t in range(4)]
+        factor = [place("factor%d" % t, [P, S], F32, FACTOR + 4 * KIB * t) for t in range(4)]
         pages = [place("page%d" % i, [P, T2], F32, PAGES + 8 * KIB * i) for i in range(LAST)]
 
         nc.vector.memset(w4_plane_raw[:].bitcast(I32), 0)
@@ -95,10 +113,9 @@ def tile_list_checkers_endgame_retrieval_kernel(
         def load_w1(tile, c0, c1):
             nc.sync.dma_start(tile[:], w1[:, c0:c1].rearrange("(p j) c -> p j c", j=4))
 
-        def load_factors(u):
-            src = wgs.rearrange("(q t) j -> q t j", t=4)[:, 2 * u : 2 * u + 2, :]
+        def load_factor(t):
             for g in QUADRANTS:
-                nc.sync.dma_start(factor_pairs[u][32 * g : 32 * (g + 1), :, :], src)
+                nc.sync.dma_start(factor[t][32 * g : 32 * (g + 1), :], wgs.rearrange("(q t) j -> t q j", t=4)[t])
 
         def load_page(i):
             a, t = divmod(i, 4)
@@ -114,11 +131,13 @@ def tile_list_checkers_endgame_retrieval_kernel(
         for u in range(2):
             load_w1(w1_early[u], N // 2 * u, N // 2 * (u + 1))
         nc.sync.dma_start(idx2[:], offs2)
-        load_factors(0)
         load_w1(w1_late, N, H)
+        load_factor(0)
         load_page(0)
         nc.sync.dma_start(idx3[:], offs3)
-        load_factors(1)
+        load_factor(1)
+        load_factor(2)
+        load_factor(3)
         for i in range(1, 5):
             load_page(i)
         for a in range(2):
@@ -133,15 +152,27 @@ def tile_list_checkers_endgame_retrieval_kernel(
         for q in QUADRANTS:
             nc.scalar.dma_start(scale_rows(w4_plane_raw, q), w4_scales[0, 4 * q : 4 * q + 4, :].bitcast(I32))
 
+
         for q in range(4):
             nc.vector.tensor_copy(scale_rows(tab_plane, q), scale_rows(tab_rows, q))
+        identity = place("identity", [P, P], F32, STAGE1 + 3 * KIB)
+        make_identity(nc, identity[:])
+        exponent, sign, root, slope = [
+            place(name, [P, ROW_TILES], F32, STAGE1 + 2 * KIB + 64 * k) for k, name in enumerate(("exponent", "sign", "root", "slope"))
+        ]
+        nc.gpsimd.memset(exponent[:], 0.5)
+        nc.gpsimd.tensor_scalar(slope[:], c3_t[:], 0.0, 2.0, IS_GE, MULT)
+        nc.gpsimd.tensor_scalar(sign[:], slope[:], 1.0, -1.0, MULT, ADD)
+        nc.gpsimd.tensor_tensor(slope[:], c3_t[:], sign[:], MULT)
+        nc.gpsimd.tensor_tensor(root[:], slope[:], exponent[:], POW)
+        nc.gpsimd.tensor_tensor(slope[:], c2_t[:], sign[:], MULT)
         nc.vector.tensor_copy(v_plane[:], tab_plane[:].indirect(idx[:]))
         nc.vector.tensor_copy(
             w4_codes[:].bitcast(U16).rearrange("p (a t m) -> p a t m", a=2, t=4),
             w4_raw[:].bitcast(U16).rearrange("p (a m t) -> p a t m", a=2, t=4),
         )
 
-        grouped = [place("w1_grouped%d" % a, [P, 4 * N], BF16, STAGE1 + (12 + 4 * a) * KIB) for a in range(2)]
+        grouped = [place("w1_grouped0", [P, 4 * N], BF16, STAGE1 + 12 * KIB)]
 
         def group_w1(a, raw, m0, m1, t0, t1):
             nc.scalar.copy(
@@ -167,78 +198,108 @@ def tile_list_checkers_endgame_retrieval_kernel(
         v2_plane = place("v2_plane", [P, S2], U8, STAGE0 - S2)
         nc.vector.tensor_copy(v2_plane[:], tab2_plane[:].indirect(idx2[:]))
 
-        lin = {}
-        terms = {}
+        lin, values, square, linear, cubic = {}, {}, {}, {}, {}
+
+        def bank(b):
+            return psum.tile([P, N], F32, name="bank", tag="bank%d" % b)
+
+        halves = [slice(N * h, N * (h + 1)) for h in range(2)]
 
         def first_product(i):
             a, t = divmod(i, 4)
-            affine = place("affine%d" % i, [P, S], F32, STAGE1 + 16 * KIB if i == ON_VECTOR else AFFINE + 4 * KIB * ((i + 2) % 5))
-            square = linear = None
-            if i >= ON_VECTOR:
-                square = place("square%d" % i, [P, S], F32, STAGE0 + 24 * KIB if i == ON_VECTOR else SQUARE + 4 * KIB * (i % 3))
-                linear = place("linear%d" % i, [P, S], F32, STAGE0 + 28 * KIB if i == ON_VECTOR else LINEAR + 4 * KIB * (i % 3))
+            col = slice(i, i + 1)
+            values[i] = place("first%d" % i, [P, S], F32, FIRST_AT[i])
             for h in range(2):
-                cols = slice(N * h, N * (h + 1))
-                lin[i, h] = psum.tile([P, N], F32, name="lin", tag="bank%d" % (2 * (i % 3) + h))
+                lin[i, h] = bank(2 * BANKS_AT[i] + h)
                 nc.tensor.matmul_mx(
                     out=lin[i, h][:], lhsT=w4_codes[:, 2 * P * i : 2 * P * (i + 1)].bitcast(FP4X4), lhsT_scale=w4_plane[:, P * i : P * (i + 1)],
-                    rhs=v_codes[h][:].bitcast(FP8X4), rhs_scale=v_plane[:, cols], start=True, stop=False,
+                    rhs=v_codes[h][:].bitcast(FP8X4), rhs_scale=v_plane[:, halves[h]], start=True, stop=False,
                 )
                 nc.tensor.matmul_mx(
                     out=lin[i, h][:], lhsT=w1_codes[a][:, P * t : P * (t + 1)].bitcast(FP8X4), lhsT_scale=w1_plane[a][:, P * t : P * (t + 1)],
-                    rhs=v_codes[h][:].bitcast(FP8X4), rhs_scale=v_plane[:, cols], start=False, stop=True,
+                    rhs=v_codes[h][:].bitcast(FP8X4), rhs_scale=v_plane[:, halves[h]], start=False, stop=True,
                 )
-                nc.scalar.activation(affine[:, cols], lin[i, h][:], ACT.Identity, bias=c2_t[:, i : i + 1], scale=c3_t[:, i : i + 1])
-                if i >= ON_VECTOR:
-                    nc.scalar.activation(square[:, cols], lin[i, h][:], ACT.Square)
-            if i >= ON_VECTOR:
+            if i < ON_VECTOR:
                 for h in range(2):
-                    nc.scalar.copy(linear[:, N * h : N * (h + 1)], lin[i, h][:])
-            terms[i] = (square, affine, linear)
+                    nc.scalar.activation(values[i][:, halves[h]], lin[i, h][:], ACT.Identity, bias=c2_t[:, col], scale=c3_t[:, col])
+                return
+            square[i] = place("square%d" % i, [P, S], F32, SQUARE_AT[i])
+            linear[i] = place("linear%d" % i, [P, S], F32, LINEAR_AT[i])
+            if i in ON_TENSOR:
+                for h in range(2):
+                    nc.scalar.activation(square[i][:, halves[h]], lin[i, h][:], ACT.Square, scale=root[:, col])
+                    nc.scalar.activation(linear[i][:, halves[h]], lin[i, h][:], ACT.Identity, bias=sign[:, col], scale=slope[:, col])
+                for h in range(2):
+                    nc.scalar.activation(values[i][:, halves[h]], lin[i, h][:], ACT.Copy, scale=sign[:, col])
+            else:
+                for h in range(2):
+                    nc.scalar.activation(values[i][:, halves[h]], lin[i, h][:], ACT.Identity, bias=c2_t[:, col], scale=c3_t[:, col])
+                    nc.scalar.activation(square[i][:, halves[h]], lin[i, h][:], ACT.Square)
+                for h in range(2):
+                    nc.scalar.copy(linear[i][:, halves[h]], lin[i, h][:])
 
-        cubic = {}
+        turned, quadratic = {}, {}
 
-        def cubic_tile(i):
-            return place("cubic%d" % i, [P, S], F32, CUBIC + 4 * KIB * (0 if i == 0 else 1 + (i + 1) % 2))
+        def sum_turned(i):
+            turned[i] = place("turned%d" % i, [P, S], F32, TURNED_AT[i])
+            sums = [bank(2 * BANKS_AT[i] + h) for h in range(2)]
+            for b in range(S // P):
+                block = slice(P * b, P * (b + 1))
+                dst = sums[b // 4][:, P * (b % 4) : P * (b % 4 + 1)]
+                nc.tensor.matmul(dst, square[i][:, block], identity[:], start=True, stop=False, is_transpose=True)
+                nc.tensor.matmul(dst, linear[i][:, block], identity[:], start=False, stop=True, is_transpose=True)
+            for h in range(2):
+                nc.scalar.copy(turned[i][:, halves[h]], sums[h][:])
+
+        def turn_back(i):
+            quadratic[i] = place("quadratic%d" % i, [P, S], F32, QUADRATIC_AT[i])
+            backs = [bank(6 + h) for h in range(2)]
+            for b in range(S // P):
+                nc.tensor.transpose(backs[b // 4][:, P * (b % 4) : P * (b % 4 + 1)], turned[i][:, P * b : P * (b + 1)], identity[:])
+            for h in range(2):
+                nc.scalar.copy(quadratic[i][:, halves[h]], backs[h][:])
 
         def horner(i):
-            affine = terms[i][1]
-            cubic[i] = cubic_tile(i)
-            halves = [slice(N * h, N * (h + 1)) for h in range(2)]
+            cubic[i] = place("cubic%d" % i, [P, S], F32, OPENING_AT[i])
             for h in range(2):
-                nc.vector.tensor_tensor(cubic[i][:, halves[h]], affine[:, halves[h]], lin[i, h][:], MULT)
+                nc.vector.tensor_tensor(cubic[i][:, halves[h]], values[i][:, halves[h]], lin[i, h][:], MULT)
             for h in range(2):
                 nc.vector.scalar_tensor_tensor(cubic[i][:, halves[h]], cubic[i][:, halves[h]], 1.0, lin[i, h][:], ADD, MULT)
 
-        def weigh(i, engine):
-            engine.tensor_tensor(terms[i][1][:], cubic[i][:], factor[i % 4], MULT)
+        def opening_product(i):
+            cubic[i] = place("cubic%d" % i, [P, S], F32, OPENING_AT[i]) if OPENING_AT[i] else values[i]
+            other = factor[i % 4] if i in ON_TENSOR else square[i]
+            nc.gpsimd.tensor_tensor(cubic[i][:], values[i][:], other[:], MULT)
 
-        def high_terms(i):
-            square, affine, linear = terms[i]
-            cubic[i] = cubic_tile(i)
-            nc.gpsimd.tensor_tensor(cubic[i][:], square[:], affine[:], MULT)
+        def closing_product(i):
+            if i in CLOSING_AT:
+                values[i] = place("weighed%d" % i, [P, S], F32, CLOSING_AT[i])
+            elif i in ON_TENSOR:
+                values[i] = cubic[i]
+            other = quadratic[i] if i in ON_TENSOR else factor[i % 4]
+            nc.gpsimd.tensor_tensor(values[i][:], cubic[i][:], other[:], MULT)
 
         def polynomial(i):
-            square, affine, linear = terms[i]
-            nc.gpsimd.tensor_tensor(cubic[i][:], cubic[i][:], linear[:], ADD)
-            if i < LAST - 1:
-                high_terms(i + 1)
-            weigh(i, nc.gpsimd)
-            if i == LAST - 1:
-                high_terms(LAST)
+            if i not in ON_TENSOR:
+                nc.gpsimd.tensor_tensor(cubic[i][:], cubic[i][:], linear[i][:], ADD)
+            if i < LAST:
+                opening_product(i + 1)
+            closing_product(i)
 
         def scatter(i):
-            nc.vector.tensor_copy(pages[i][:].indirect(idx3[:]), terms[i][1][:])
+            nc.vector.tensor_copy(pages[i][:].indirect(idx3[:]), values[i][:])
 
         stage = {}
 
+        def stage_first_pass(half):
+            stage[0, half] = place("stage0%d" % half, [P, 4, 2 * N], F32, STAGE0 + 16 * KIB * half)
+            for t in range(4):
+                nc.sync.dma_start(stage[0, half][:, t, :], pages[t][:, 2 * N * half : 2 * N * (half + 1)])
+
         def stage_page(i):
-            pair, e = divmod(i, 2)
-            for half in range(2):
-                if e == 0:
-                    base = (STAGE0 + 16 * KIB, STAGE0, STAGE1)[pair] + 8 * KIB * (1 - half)
-                    stage[pair, half] = place("stage%d%d" % (pair, half), [P, 2, 2 * N], F32, base)
-                nc.scalar.dma_start(stage[pair, half][:, e, :], pages[i][:, 2 * N * half : 2 * N * (half + 1)])
+            if i == 4:
+                stage[1] = place("stage1", [P, 2, T2], F32, STAGE1)
+            nc.sync.dma_start(stage[1][:, i - 4, :], pages[i][:])
 
         woven = {}
 
@@ -246,11 +307,11 @@ def tile_list_checkers_endgame_retrieval_kernel(
             start = max(s0 for b, s0 in woven if b == a and s0 <= c0)
             return woven[a, start][:, c0 - start : c1 - start, :]
 
-        def weave(pair, c0, c1):
-            a, t0 = pair // 2, 2 * (pair % 2)
+        def weave(a, c0, c1):
             half = c0 // (2 * N)
-            dst = woven_part(a, c0, c1)[:, :, t0 : t0 + 2].rearrange("p (g i) t -> p g t i", i=4)
-            src = stage[pair, half][:, :, c0 - 2 * N * half : c1 - 2 * N * half].rearrange("p t (g i) -> p g t i", i=4)
+            dst = woven_part(a, c0, c1)[:, :, 0 : (4, 2)[a]].rearrange("p (g i) t -> p g t i", i=4)
+            src = stage[1][:, :, c0:c1] if a else stage[0, half][:, :, c0 - 2 * N * half : c1 - 2 * N * half]
+            src = src.rearrange("p t (g i) -> p g t i", i=4)
             if a == 0 or c0 < SCALAR_COLUMNS:
                 nc.scalar.copy(dst, src)
             else:
@@ -272,55 +333,61 @@ def tile_list_checkers_endgame_retrieval_kernel(
                 in_=woven_part(a, c0, c1).rearrange("p c t -> p (c t)"),
             )
 
+        def terms(i):
+            if i < ROW_TILES:
+                first_product(i)
+            if i - 1 in ON_TENSOR:
+                turn_back(i - 1)
+            if i in ON_TENSOR:
+                sum_turned(i)
+
         first_product(0)
         first_product(1)
         horner(0)
-        weigh(0, nc.gpsimd)
+        closing_product(0)
         horner(1)
-        first_product(2)
-        weigh(1, nc.gpsimd)
-        horner(2)
+        grouped.append(place("w1_grouped1", [P, 4 * N], BF16, SHARED))
         group_w1(1, w1_late, 0, P, 0, 4)
         quantize_w1(1, 0, 4)
-        first_product(3)
-        high_terms(3)
+        closing_product(1)
+        terms(2)
+        opening_product(2)
+        terms(3)
         scatter(0)
-        stage_page(0)
-        first_product(4)
+        terms(4)
         for i in range(1, ROW_TILES):
-            if i + 1 == ON_VECTOR - 1:
-                weigh(i + 1, nc.gpsimd)
-            if ON_VECTOR <= i + 1 < ROW_TILES:
+            if i < LAST:
                 polynomial(i + 1)
             if i == LAST:
-                codes[0] = place("page_codes0", [P, T2], U32, AFFINE + 8 * KIB)
+                codes[0] = place("page_codes0", [P, T2], U32, slot(CUBIC, 1))
                 for half in range(2):
                     quantize_page(0, 2 * N * half, 2 * N * (half + 1))
             scatter(i)
-            if i < LAST - 1:
+            if i in (4, 5):
                 stage_page(i)
-            if i + 4 < ROW_TILES:
-                first_product(i + 4)
+            if i + 4 <= ROW_TILES:
+                terms(i + 4)
             if i == 4:
                 pages.append(place("page_last", [P, T2], F32, PAGES + 8 * KIB * i))
                 load_page(LAST)
-            if i == 1:
+            if i == 3:
+                for half in range(2):
+                    stage_first_pass(half)
                 for half in range(2):
                     woven[0, 2 * N * half] = place("woven0%d" % half, [P, 2 * N, 4], BF16, PAGES + 8 * KIB * half)
-            if i in (1, 3):
-                for half in range(2):
-                    weave(i // 2, 2 * N * half, 2 * N * (half + 1))
+                for c in range(T2 // N):
+                    weave(0, N * c, N * (c + 1))
             if i == 5:
-                woven[1, 0] = place("woven_scalar", [P, SCALAR_COLUMNS, 4], BF16, STAGE0 + 16 * KIB)
-                weave(2, 0, 2 * N)
-                weave(2, 2 * N, SCALAR_COLUMNS)
+                woven[1, 0] = place("woven_scalar", [P, SCALAR_COLUMNS, 4], BF16, STAGE0)
+                weave(1, 0, 2 * N)
+                weave(1, 2 * N, SCALAR_COLUMNS)
             if i == 6:
                 weave_row(2, 0, SCALAR_COLUMNS)
         woven[1, SCALAR_COLUMNS] = place("woven_gpsimd", [P, T2 - SCALAR_COLUMNS, 4], BF16, PAGES + 8 * KIB)
-        weave(2, SCALAR_COLUMNS, T2)
+        weave(1, SCALAR_COLUMNS, T2)
         weave_row(2, SCALAR_COLUMNS, T2)
 
-        v2_codes = place("v2_codes", [P, 2 * S2], U32, AFFINE + 16 * KIB)
+        v2_codes = place("v2_codes", [P, 2 * S2], U32, slot(AFFINE, 3))
         for a, j0, j1 in ((0, 0, 2 * P), (1, 0, S2), (0, 2 * P, S2)):
             window = tab2_w[:, T2 * a : T2 * (a + 1)].bitcast(U32)
             nc.vector.tensor_copy(v2_codes[:, S2 * a + j0 : S2 * a + j1], window.indirect(idx2[:, j0 // 16 : j1 // 16]))

@@ -29,7 +29,7 @@ KIB = 1024
 QUADRANTS = (0, 2, 1, 3)
 SCALAR_COLUMNS = 1280
 ON_VECTOR = 2
-ON_TENSOR = (2, 4, 6)
+ON_TENSOR = (2, 4, 5, 6)
 
 PAGES = 0
 FACTOR = PAGES + 64 * KIB
@@ -51,8 +51,8 @@ def slot(base, k):
 FIRST_AT = (SHARED, slot(AFFINE, 3), slot(AFFINE, 0), slot(AFFINE, 3), slot(AFFINE, 4), SHARED, slot(CUBIC, 1), slot(AFFINE, 3))
 SQUARE_AT = (None, None, slot(AFFINE, 1), slot(SQUARE, 0), slot(SQUARE, 1), slot(SQUARE, 2), slot(STAGE0, 1), slot(SQUARE, 0))
 LINEAR_AT = (None, None, slot(AFFINE, 2), slot(LINEAR, 0), slot(CUBIC, 0), slot(AFFINE, 1), slot(STAGE0, 0), SMALL)
-TURNED_AT = {2: slot(SQUARE, 2), 4: slot(SQUARE, 1), 6: STAGE0 + 30 * KIB}
-QUADRATIC_AT = {2: slot(LINEAR, 1), 4: slot(CUBIC, 0), 6: slot(LINEAR, 0)}
+TURNED_AT = {2: slot(SQUARE, 2), 4: slot(SQUARE, 1), 5: slot(SQUARE, 2), 6: STAGE0 + 30 * KIB}
+QUADRATIC_AT = {2: slot(LINEAR, 1), 4: slot(CUBIC, 0), 5: slot(AFFINE, 1), 6: slot(LINEAR, 0)}
 OPENING_AT = (slot(CUBIC, 0), slot(CUBIC, 1), slot(CUBIC, 1), AFFINE - 2 * KIB, slot(LINEAR, 1), slot(LINEAR, 2), None, slot(CUBIC, 2))
 BANKS_AT = (0, 1, 2, 1, 0, 2, 1, 1)
 CLOSING_AT = {0: slot(AFFINE, 4), 1: SHARED, 4: slot(AFFINE, 0)}
@@ -137,8 +137,9 @@ def tile_list_checkers_endgame_retrieval_kernel(
         nc.sync.dma_start(idx3[:], offs3)
         load_factor(1)
         load_factor(2)
+        load_page(1)
         load_factor(3)
-        for i in range(1, 5):
+        for i in range(2, 5):
             load_page(i)
         for a in range(2):
             nc.sync.dma_start(tab2_w[:, T2 * a : T2 * (a + 1)], tab2_words[a].rearrange("p t i -> p (t i)").bitcast(I32))
@@ -277,7 +278,8 @@ def tile_list_checkers_endgame_retrieval_kernel(
             elif i in ON_TENSOR:
                 values[i] = cubic[i]
             other = quadratic[i] if i in ON_TENSOR else factor[i % 4]
-            nc.gpsimd.tensor_tensor(values[i][:], cubic[i][:], other[:], MULT)
+            for cols in halves if i == 0 else [slice(0, S)]:
+                nc.gpsimd.tensor_tensor(values[i][:, cols], cubic[i][:, cols], other[:, cols], MULT)
 
         def polynomial(i):
             if i not in ON_TENSOR:

@@ -92,6 +92,8 @@ def tile_list_checkers_endgame_retrieval_kernel(
         w1_codes = [keep.tile([P, N], U32, name="w1_codes%d" % a, align_bytes=64) for a in range(2)]
         w1_plane = [keep.tile([P, N], U8, name="w1_plane%d" % a, align_bytes=64) for a in range(2)]
         v_plane = keep.tile([P, S], U8, name="v_plane", align_bytes=64)
+        v_rows = keep.tile([P, S], U8, name="v_rows", align_bytes=64)
+        v2_plane = keep.tile([P, S2], U8, name="v2_plane", align_bytes=64)
         v_codes = [keep.tile([P, N], U32, name="v_codes%d" % h, align_bytes=64) for h in range(2)]
         page_plane = [keep.tile([P, T2], U8, name="page_plane%d" % a, align_bytes=64) for a in range(2)]
 
@@ -108,7 +110,9 @@ def tile_list_checkers_endgame_retrieval_kernel(
 
         nc.vector.memset(w4_plane_raw[:].bitcast(I32), 0)
         nc.vector.memset(tab_plane[:].bitcast(I32), 0)
+        nc.vector.memset(v_plane[:].bitcast(I32), 0)
         nc.gpsimd.memset(tab2_plane[:].bitcast(I32), 0)
+        nc.gpsimd.memset(v2_plane[:].bitcast(I32), 0)
 
         def load_w1(tile, c0, c1):
             nc.sync.dma_start(tile[:], w1[:, c0:c1].rearrange("(p j) c -> p j c", j=4))
@@ -122,15 +126,15 @@ def tile_list_checkers_endgame_retrieval_kernel(
             nc.sync.dma_start(pages[i][:], page0[N * a : N * (a + 1), :].rearrange("(p t) c -> t p c", t=4)[t])
 
         nc.sync.dma_start(idx[:], offs)
-        for q in QUADRANTS:
-            nc.sync.dma_start(scale_rows(tab_rows, q), tab_scales[0, 4 * q : 4 * q + 4, :].bitcast(I32))
-        nc.sync.dma_start(c3_t[:].rearrange("p (a t) -> p a t", t=4), c3.rearrange("(a p t) -> p a t", a=2, t=4))
-        nc.sync.dma_start(c2_t[:].rearrange("p (a t) -> p a t", t=4), c2.rearrange("(a p t) -> p a t", a=2, t=4))
+        nc.sync.dma_start(tab_rows[0:16, :].bitcast(I32), tab_scales[0].bitcast(I32))
         nc.sync.dma_start(tab_w[:], tab_words[0].rearrange("p t i -> p (t i)").bitcast(I32))
         nc.sync.dma_start(w4_raw[:].bitcast(I32), w4_words[0].bitcast(I32))
         for u in range(2):
             load_w1(w1_early[u], N // 2 * u, N // 2 * (u + 1))
+        nc.sync.dma_start(c3_t[:].rearrange("p (a t) -> p a t", t=4), c3.rearrange("(a p t) -> p a t", a=2, t=4))
+        nc.sync.dma_start(c2_t[:].rearrange("p (a t) -> p a t", t=4), c2.rearrange("(a p t) -> p a t", a=2, t=4))
         nc.sync.dma_start(idx2[:], offs2)
+        nc.sync.dma_start(tab2_plane[0:32, :].bitcast(I32), tab2_scales.rearrange("a q t -> (a q) t").bitcast(I32))
         load_w1(w1_late, N, H)
         load_factor(0)
         load_page(0)
@@ -149,13 +153,10 @@ def tile_list_checkers_endgame_retrieval_kernel(
         for i in range(5, LAST):
             load_page(i)
         for q in QUADRANTS:
-            nc.gpsimd.dma_start(scale_rows(tab2_plane, q, 8), tab2_scales[:, 4 * q : 4 * q + 4, :].bitcast(I32))
-        for q in QUADRANTS:
             nc.scalar.dma_start(scale_rows(w4_plane_raw, q), w4_scales[0, 4 * q : 4 * q + 4, :].bitcast(I32))
 
 
-        for q in range(4):
-            nc.vector.tensor_copy(scale_rows(tab_plane, q), scale_rows(tab_rows, q))
+        nc.vector.tensor_copy(tab_plane[0:16, :].bitcast(I32), tab_rows[0:16, :].bitcast(I32))
         identity = place("identity", [P, P], F32, STAGE1 + 3 * KIB)
         make_identity(nc, identity[:])
         exponent, sign, root, slope = [
@@ -167,7 +168,10 @@ def tile_list_checkers_endgame_retrieval_kernel(
         nc.gpsimd.tensor_tensor(slope[:], c3_t[:], sign[:], MULT)
         nc.gpsimd.tensor_tensor(root[:], slope[:], exponent[:], POW)
         nc.gpsimd.tensor_tensor(slope[:], c2_t[:], sign[:], MULT)
-        nc.vector.tensor_copy(v_plane[:], tab_plane[:].indirect(idx[:]))
+        nc.vector.tensor_copy(v_rows[:], tab_plane[:].indirect(idx[:]))
+        nc.vector.tensor_copy(scale_rows(v_plane, 0), scale_rows(v_rows, 0))
+        for q in (2, 1, 3):
+            nc.scalar.dma_start(scale_rows(v_plane, q), v_rows[4 * q : 4 * q + 4, :].bitcast(I32))
         nc.vector.tensor_copy(
             w4_codes[:].bitcast(U16).rearrange("p (a t m) -> p a t m", a=2, t=4),
             w4_raw[:].bitcast(U16).rearrange("p (a m t) -> p a t m", a=2, t=4),
@@ -196,8 +200,8 @@ def tile_list_checkers_endgame_retrieval_kernel(
             group_w1(0, w1_early[1], P // 2, P, t0, t0 + 2)
             quantize_w1(0, t0, t0 + 2)
 
-        v2_plane = place("v2_plane", [P, S2], U8, STAGE0 - S2)
-        nc.vector.tensor_copy(v2_plane[:], tab2_plane[:].indirect(idx2[:]))
+        v2_rows = place("v2_rows", [P, S2], U8, STAGE0 - S2)
+        nc.vector.tensor_copy(v2_rows[:], tab2_plane[:].indirect(idx2[:]))
 
         lin, values, square, linear, cubic = {}, {}, {}, {}, {}
 
@@ -369,6 +373,11 @@ def tile_list_checkers_endgame_retrieval_kernel(
                 stage_page(i)
             if i + 4 <= ROW_TILES:
                 terms(i + 4)
+            if i == 2:
+                for a in range(2):
+                    for q in QUADRANTS:
+                        rows = 16 * a + 4 * q
+                        nc.sync.dma_start(v2_plane[32 * q + 4 * a : 32 * q + 4 * a + 4, :].bitcast(I32), v2_rows[rows : rows + 4, :].bitcast(I32))
             if i == 4:
                 pages.append(place("page_last", [P, T2], F32, PAGES + 8 * KIB * i))
                 load_page(LAST)

@@ -28,8 +28,6 @@ LAST = ROW_TILES - 1
 KIB = 1024
 QUADRANTS = (0, 2, 1, 3)
 SCALAR_COLUMNS = 1280
-ON_VECTOR = 2
-ON_TENSOR = (2, 4, 5, 6)
 
 PAGES = 0
 FACTOR = PAGES + 64 * KIB
@@ -48,14 +46,12 @@ def slot(base, k):
     return base + 4 * KIB * k
 
 
-FIRST_AT = (SHARED, slot(AFFINE, 3), slot(AFFINE, 0), slot(AFFINE, 3), slot(AFFINE, 4), SHARED, slot(CUBIC, 1), slot(AFFINE, 3))
-SQUARE_AT = (None, None, slot(AFFINE, 1), slot(SQUARE, 0), slot(SQUARE, 1), slot(SQUARE, 2), slot(STAGE0, 1), slot(SQUARE, 0))
-LINEAR_AT = (None, None, slot(AFFINE, 2), slot(LINEAR, 0), slot(CUBIC, 0), slot(AFFINE, 1), slot(STAGE0, 0), SMALL)
-TURNED_AT = {2: slot(SQUARE, 2), 4: slot(SQUARE, 1), 5: slot(SQUARE, 2), 6: STAGE0 + 30 * KIB}
-QUADRATIC_AT = {2: slot(LINEAR, 1), 4: slot(CUBIC, 0), 5: slot(AFFINE, 1), 6: slot(LINEAR, 0)}
-OPENING_AT = (slot(CUBIC, 0), slot(CUBIC, 1), slot(CUBIC, 1), AFFINE - 2 * KIB, slot(LINEAR, 1), slot(LINEAR, 2), None, slot(CUBIC, 2))
-BANKS_AT = (0, 1, 2, 1, 0, 2, 1, 1)
-CLOSING_AT = {0: slot(AFFINE, 4), 1: SHARED, 4: slot(AFFINE, 0)}
+LINEAR_AT = {2: slot(CUBIC, 2), 3: slot(SQUARE, 0), 4: slot(AFFINE, 4), 5: slot(AFFINE, 3), 6: slot(LINEAR, 1), 7: slot(AFFINE, 4)}
+SQUARE_AT = {2: slot(SQUARE, 2), 3: slot(AFFINE, 1), 4: slot(SQUARE, 1), 5: slot(SQUARE, 2), 6: slot(STAGE0, 1), 7: slot(SQUARE, 0)}
+AFFINE_AT = {2: slot(LINEAR, 2), 3: slot(AFFINE, 2), 4: slot(CUBIC, 0), 5: slot(CUBIC, 1), 6: slot(LINEAR, 0), 7: slot(CUBIC, 2)}
+TURNED_AT = {2: slot(AFFINE, 0), 6: STAGE0 + 30 * KIB}
+BANKS_AT = (0, 1, 2, 1, 3, 0, 2, 1)
+BACK_AT = {2: 3, 3: 0, 4: 2, 5: 1, 6: 3, 7: 0}
 
 
 def tile_list_checkers_endgame_retrieval_kernel(
@@ -108,7 +104,7 @@ def tile_list_checkers_endgame_retrieval_kernel(
         factor = [place("factor%d" % t, [P, S], F32, FACTOR + 4 * KIB * t) for t in range(4)]
         pages = [place("page%d" % i, [P, T2], F32, PAGES + 8 * KIB * i) for i in range(LAST)]
 
-        nc.vector.memset(w4_plane_raw[:].bitcast(I32), 0)
+        nc.gpsimd.memset(w4_plane_raw[:].bitcast(I32), 0)
         nc.vector.memset(tab_plane[:].bitcast(I32), 0)
         nc.vector.memset(v_plane[:].bitcast(I32), 0)
         nc.gpsimd.memset(tab2_plane[:].bitcast(I32), 0)
@@ -128,6 +124,8 @@ def tile_list_checkers_endgame_retrieval_kernel(
         nc.sync.dma_start(idx[:], offs)
         nc.sync.dma_start(tab_rows[0:16, :].bitcast(I32), tab_scales[0].bitcast(I32))
         nc.sync.dma_start(tab_w[:], tab_words[0].rearrange("p t i -> p (t i)").bitcast(I32))
+        for q in QUADRANTS:
+            nc.sync.dma_start(scale_rows(w4_plane_raw, q), w4_scales[0, 4 * q : 4 * q + 4, :].bitcast(I32))
         nc.sync.dma_start(w4_raw[:].bitcast(I32), w4_words[0].bitcast(I32))
         for u in range(2):
             load_w1(w1_early[u], N // 2 * u, N // 2 * (u + 1))
@@ -135,13 +133,13 @@ def tile_list_checkers_endgame_retrieval_kernel(
         nc.sync.dma_start(c2_t[:].rearrange("p (a t) -> p a t", t=4), c2.rearrange("(a p t) -> p a t", a=2, t=4))
         nc.sync.dma_start(idx2[:], offs2)
         nc.sync.dma_start(tab2_plane[0:32, :].bitcast(I32), tab2_scales.rearrange("a q t -> (a q) t").bitcast(I32))
-        load_w1(w1_late, N, H)
         load_factor(0)
         load_page(0)
         nc.sync.dma_start(idx3[:], offs3)
         load_factor(1)
-        load_factor(2)
+        load_w1(w1_late, N, H)
         load_page(1)
+        load_factor(2)
         load_factor(3)
         for i in range(2, 5):
             load_page(i)
@@ -152,16 +150,12 @@ def tile_list_checkers_endgame_retrieval_kernel(
             nc.sync.dma_start(gain_t[:], gain.rearrange("(c p) -> p c", p=P))
         for i in range(5, LAST):
             load_page(i)
-        for q in QUADRANTS:
-            nc.scalar.dma_start(scale_rows(w4_plane_raw, q), w4_scales[0, 4 * q : 4 * q + 4, :].bitcast(I32))
 
 
         nc.vector.tensor_copy(tab_plane[0:16, :].bitcast(I32), tab_rows[0:16, :].bitcast(I32))
-        identity = place("identity", [P, P], F32, STAGE1 + 3 * KIB)
+        identity = keep.tile([P, P], F32, name="identity")
         make_identity(nc, identity[:])
-        exponent, sign, root, slope = [
-            place(name, [P, ROW_TILES], F32, STAGE1 + 2 * KIB + 64 * k) for k, name in enumerate(("exponent", "sign", "root", "slope"))
-        ]
+        exponent, sign, root, slope = [keep.tile([P, ROW_TILES], F32, name=name) for name in ("exponent", "sign", "root", "slope")]
         nc.gpsimd.memset(exponent[:], 0.5)
         nc.gpsimd.tensor_scalar(slope[:], c3_t[:], 0.0, 2.0, IS_GE, MULT)
         nc.gpsimd.tensor_scalar(sign[:], slope[:], 1.0, -1.0, MULT, ADD)
@@ -203,17 +197,18 @@ def tile_list_checkers_endgame_retrieval_kernel(
         v2_rows = place("v2_rows", [P, S2], U8, STAGE0 - S2)
         nc.vector.tensor_copy(v2_rows[:], tab2_plane[:].indirect(idx2[:]))
 
-        lin, values, square, linear, cubic = {}, {}, {}, {}, {}
+        lin, values, square, linear, affine, turned, quadratic = {}, {}, {}, {}, {}, {}, {}
 
         def bank(b):
             return psum.tile([P, N], F32, name="bank", tag="bank%d" % b)
 
         halves = [slice(N * h, N * (h + 1)) for h in range(2)]
 
+        def term(name, i, offset):
+            return place("%s%d" % (name, i), [P, S], F32, offset)
+
         def first_product(i):
             a, t = divmod(i, 4)
-            col = slice(i, i + 1)
-            values[i] = place("first%d" % i, [P, S], F32, FIRST_AT[i])
             for h in range(2):
                 lin[i, h] = bank(2 * BANKS_AT[i] + h)
                 nc.tensor.matmul_mx(
@@ -224,73 +219,50 @@ def tile_list_checkers_endgame_retrieval_kernel(
                     out=lin[i, h][:], lhsT=w1_codes[a][:, P * t : P * (t + 1)].bitcast(FP8X4), lhsT_scale=w1_plane[a][:, P * t : P * (t + 1)],
                     rhs=v_codes[h][:].bitcast(FP8X4), rhs_scale=v_plane[:, halves[h]], start=False, stop=True,
                 )
-            if i < ON_VECTOR:
-                for h in range(2):
-                    nc.scalar.activation(values[i][:, halves[h]], lin[i, h][:], ACT.Identity, bias=c2_t[:, col], scale=c3_t[:, col])
-                return
-            square[i] = place("square%d" % i, [P, S], F32, SQUARE_AT[i])
-            linear[i] = place("linear%d" % i, [P, S], F32, LINEAR_AT[i])
-            if i in ON_TENSOR:
-                for h in range(2):
-                    nc.scalar.activation(square[i][:, halves[h]], lin[i, h][:], ACT.Square, scale=root[:, col])
-                    nc.scalar.activation(linear[i][:, halves[h]], lin[i, h][:], ACT.Identity, bias=sign[:, col], scale=slope[:, col])
-                for h in range(2):
-                    nc.scalar.activation(values[i][:, halves[h]], lin[i, h][:], ACT.Copy, scale=sign[:, col])
-            else:
-                for h in range(2):
-                    nc.scalar.activation(values[i][:, halves[h]], lin[i, h][:], ACT.Identity, bias=c2_t[:, col], scale=c3_t[:, col])
-                    nc.scalar.activation(square[i][:, halves[h]], lin[i, h][:], ACT.Square)
-                for h in range(2):
-                    nc.scalar.copy(linear[i][:, halves[h]], lin[i, h][:])
 
-        turned, quadratic = {}, {}
+        def inner_affine(i, offset):
+            affine[i] = term("affine", i, offset)
+            for h in range(2):
+                nc.scalar.activation(affine[i][:, halves[h]], lin[i, h][:], ACT.Identity, bias=c2_t[:, i : i + 1], scale=c3_t[:, i : i + 1])
+
+        def times_lin(i, offset):
+            product = term("inner", i, offset)
+            for h in range(2):
+                nc.vector.tensor_tensor(product[:, halves[h]], affine[i][:, halves[h]], lin[i, h][:], MULT)
+            return product
+
+        def summands(i):
+            col = slice(i, i + 1)
+            square[i], affine[i], linear[i] = term("square", i, SQUARE_AT[i]), term("affine", i, AFFINE_AT[i]), term("linear", i, LINEAR_AT[i])
+            for h in range(2):
+                nc.scalar.activation(square[i][:, halves[h]], lin[i, h][:], ACT.Square, scale=root[:, col])
+                nc.scalar.activation(affine[i][:, halves[h]], lin[i, h][:], ACT.Identity, bias=sign[:, col], scale=slope[:, col])
+            for h in range(2):
+                nc.scalar.activation(linear[i][:, halves[h]], lin[i, h][:], ACT.Copy, scale=sign[:, col])
 
         def sum_turned(i):
-            turned[i] = place("turned%d" % i, [P, S], F32, TURNED_AT[i])
+            turned[i] = term("turned", i, TURNED_AT.get(i, SQUARE_AT[i]))
             sums = [bank(2 * BANKS_AT[i] + h) for h in range(2)]
             for b in range(S // P):
                 block = slice(P * b, P * (b + 1))
                 dst = sums[b // 4][:, P * (b % 4) : P * (b % 4 + 1)]
                 nc.tensor.matmul(dst, square[i][:, block], identity[:], start=True, stop=False, is_transpose=True)
-                nc.tensor.matmul(dst, linear[i][:, block], identity[:], start=False, stop=True, is_transpose=True)
+                nc.tensor.matmul(dst, affine[i][:, block], identity[:], start=False, stop=True, is_transpose=True)
             for h in range(2):
                 nc.scalar.copy(turned[i][:, halves[h]], sums[h][:])
 
         def turn_back(i):
-            quadratic[i] = place("quadratic%d" % i, [P, S], F32, QUADRATIC_AT[i])
-            backs = [bank(6 + h) for h in range(2)]
+            quadratic[i] = term("quadratic", i, AFFINE_AT[i])
+            backs = [bank(2 * BACK_AT[i] + h) for h in range(2)]
             for b in range(S // P):
                 nc.tensor.transpose(backs[b // 4][:, P * (b % 4) : P * (b % 4 + 1)], turned[i][:, P * b : P * (b + 1)], identity[:])
             for h in range(2):
                 nc.scalar.copy(quadratic[i][:, halves[h]], backs[h][:])
 
-        def horner(i):
-            cubic[i] = place("cubic%d" % i, [P, S], F32, OPENING_AT[i])
-            for h in range(2):
-                nc.vector.tensor_tensor(cubic[i][:, halves[h]], values[i][:, halves[h]], lin[i, h][:], MULT)
-            for h in range(2):
-                nc.vector.scalar_tensor_tensor(cubic[i][:, halves[h]], cubic[i][:, halves[h]], 1.0, lin[i, h][:], ADD, MULT)
-
-        def opening_product(i):
-            cubic[i] = place("cubic%d" % i, [P, S], F32, OPENING_AT[i]) if OPENING_AT[i] else values[i]
-            other = factor[i % 4] if i in ON_TENSOR else square[i]
-            nc.gpsimd.tensor_tensor(cubic[i][:], values[i][:], other[:], MULT)
-
-        def closing_product(i):
-            if i in CLOSING_AT:
-                values[i] = place("weighed%d" % i, [P, S], F32, CLOSING_AT[i])
-            elif i in ON_TENSOR:
-                values[i] = cubic[i]
-            other = quadratic[i] if i in ON_TENSOR else factor[i % 4]
-            for cols in halves if i == 0 else [slice(0, S)]:
-                nc.gpsimd.tensor_tensor(values[i][:, cols], cubic[i][:, cols], other[:, cols], MULT)
-
-        def polynomial(i):
-            if i not in ON_TENSOR:
-                nc.gpsimd.tensor_tensor(cubic[i][:], cubic[i][:], linear[i][:], ADD)
-            if i < LAST:
-                opening_product(i + 1)
-            closing_product(i)
+        def products(i):
+            values[i] = linear[i] if i == 1 else term("values", i, AFFINE_AT.get(i - 1, SHARED))
+            nc.gpsimd.tensor_tensor(values[i][:], linear[i][:], factor[i % 4][:], MULT)
+            nc.gpsimd.tensor_tensor(values[i][:], values[i][:], quadratic[i][:], MULT)
 
         def scatter(i):
             nc.vector.tensor_copy(pages[i][:].indirect(idx3[:]), values[i][:])
@@ -318,8 +290,11 @@ def tile_list_checkers_endgame_retrieval_kernel(
             dst = woven_part(a, c0, c1)[:, :, 0 : (4, 2)[a]].rearrange("p (g i) t -> p g t i", i=4)
             src = stage[1][:, :, c0:c1] if a else stage[0, half][:, :, c0 - 2 * N * half : c1 - 2 * N * half]
             src = src.rearrange("p t (g i) -> p g t i", i=4)
-            if a == 0 or c0 < SCALAR_COLUMNS:
+            if c0 < (3 * N, SCALAR_COLUMNS)[a]:
                 nc.scalar.copy(dst, src)
+            elif a == 0:
+                rows = stage[0, half][:, :, c0 - 2 * N * half : c1 - 2 * N * half]
+                nc.gpsimd.tensor_scalar(woven_part(a, c0, c1), rows.rearrange("p t c -> p c t"), 1.0, 0.0, MULT, ADD)
             else:
                 nc.gpsimd.tensor_scalar(dst, src, 1.0, 0.0, MULT, ADD)
 
@@ -340,39 +315,51 @@ def tile_list_checkers_endgame_retrieval_kernel(
             )
 
         def terms(i):
-            if i < ROW_TILES:
-                first_product(i)
-            if i - 1 in ON_TENSOR:
-                turn_back(i - 1)
-            if i in ON_TENSOR:
-                sum_turned(i)
+            first_product(i)
+            summands(i)
+            sum_turned(i)
+            turn_back(i)
 
         first_product(0)
+        inner_affine(0, slot(AFFINE, 4))
         first_product(1)
-        horner(0)
-        closing_product(0)
-        horner(1)
+        inner_affine(1, slot(AFFINE, 3))
+        cubic = times_lin(0, slot(CUBIC, 0))
+        for h in range(2):
+            nc.vector.scalar_tensor_tensor(cubic[:, halves[h]], cubic[:, halves[h]], 1.0, lin[0, h][:], ADD, MULT)
+        for h in range(2):
+            nc.gpsimd.tensor_tensor(affine[0][:, halves[h]], cubic[:, halves[h]], factor[0][:, halves[h]], MULT)
+        inner = times_lin(1, slot(CUBIC, 1))
+        linear[1] = term("linear", 1, slot(LINEAR, 0))
+        for h in range(2):
+            nc.scalar.copy(linear[1][:, halves[h]], lin[1, h][:])
+        quadratic[1] = term("quadratic", 1, slot(AFFINE, 3))
+        nc.scalar.activation(quadratic[1][:], inner[:], ACT.Identity, bias=1.0)
+        for h in range(2):
+            nc.vector.tensor_copy(pages[0][:].indirect(list_half(idx3, h)), affine[0][:, halves[h]])
+        products(1)
         grouped.append(place("w1_grouped1", [P, 4 * N], BF16, SHARED))
         group_w1(1, w1_late, 0, P, 0, 4)
         quantize_w1(1, 0, 4)
-        closing_product(1)
         terms(2)
-        opening_product(2)
         terms(3)
-        scatter(0)
-        terms(4)
         for i in range(1, ROW_TILES):
             if i < LAST:
-                polynomial(i + 1)
+                products(i + 1)
+            if i == LAST - 1:
+                weave(0, 3 * N, T2)
             if i == LAST:
                 codes[0] = place("page_codes0", [P, T2], U32, slot(CUBIC, 1))
-                for half in range(2):
-                    quantize_page(0, 2 * N * half, 2 * N * (half + 1))
+                for c0, c1 in ((0, 2 * N), (2 * N, 3 * N), (3 * N, T2)):
+                    quantize_page(0, c0, c1)
             scatter(i)
+            if i == 4:
+                for half in range(2):
+                    stage_first_pass(half)
             if i in (4, 5):
                 stage_page(i)
-            if i + 4 <= ROW_TILES:
-                terms(i + 4)
+            if i + 3 < ROW_TILES:
+                terms(i + 3)
             if i == 2:
                 for a in range(2):
                     for q in QUADRANTS:
@@ -381,12 +368,10 @@ def tile_list_checkers_endgame_retrieval_kernel(
             if i == 4:
                 pages.append(place("page_last", [P, T2], F32, PAGES + 8 * KIB * i))
                 load_page(LAST)
-            if i == 3:
-                for half in range(2):
-                    stage_first_pass(half)
-                for half in range(2):
-                    woven[0, 2 * N * half] = place("woven0%d" % half, [P, 2 * N, 4], BF16, PAGES + 8 * KIB * half)
-                for c in range(T2 // N):
+            if i == 4:
+                for c0, c1 in ((0, 2 * N), (2 * N, 3 * N), (3 * N, T2)):
+                    woven[0, c0] = place("woven0%d" % c0, [P, c1 - c0, 4], BF16, PAGES + 8 * c0)
+                for c in range(3):
                     weave(0, N * c, N * (c + 1))
             if i == 5:
                 woven[1, 0] = place("woven_scalar", [P, SCALAR_COLUMNS, 4], BF16, STAGE0)
@@ -398,7 +383,7 @@ def tile_list_checkers_endgame_retrieval_kernel(
         weave(1, SCALAR_COLUMNS, T2)
         weave_row(2, SCALAR_COLUMNS, T2)
 
-        v2_codes = place("v2_codes", [P, 2 * S2], U32, slot(AFFINE, 3))
+        v2_codes = place("v2_codes", [P, 2 * S2], U32, AFFINE_AT[LAST - 1])
         for a, j0, j1 in ((0, 0, 2 * P), (1, 0, S2), (0, 2 * P, S2)):
             window = tab2_w[:, T2 * a : T2 * (a + 1)].bitcast(U32)
             nc.vector.tensor_copy(v2_codes[:, S2 * a + j0 : S2 * a + j1], window.indirect(idx2[:, j0 // 16 : j1 // 16]))
@@ -451,7 +436,10 @@ def tile_list_checkers_endgame_retrieval_kernel(
             result = place("result%d" % n, [P, PQ], F32, SQUARE + 4 * KIB * n)
             cuts = (0, 512, 768, PQ) if n == S2 // P - 1 else (0, PQ)
             for c0, c1 in zip(cuts, cuts[1:]):
+                nc.vector.tensor_copy(picked[:, c0:c1], score_sb[n][:].indirect(idx4[:, c0 // 16 : c1 // 16]))
+            if n == S2 // P - 2:
+                cuts = (0, 512, PQ)
+            for c0, c1 in zip(cuts, cuts[1:]):
                 cols = slice(c0, c1)
-                nc.vector.tensor_copy(picked[:, cols], score_sb[n][:].indirect(idx4[:, c0 // 16 : c1 // 16]))
                 nc.scalar.activation(result[:, cols], picked[:, cols], ACT.Tanh, scale=gain_t[:, n : n + 1])
                 nc.sync.dma_start(out[P * n : P * (n + 1), cols], result[:, cols])

@@ -82,11 +82,10 @@ def tile_list_checkers_endgame_retrieval_kernel(
         c2_t = keep.tile([P, ROW_TILES], F32, name="c2_t")
         c3_t = keep.tile([P, ROW_TILES], F32, name="c3_t")
         gain_t = keep.tile([P, S2 // P], F32, name="gain_t")
-        tab2_plane = keep.tile([P, T2], U8, name="tab2_plane", align_bytes=64)
         w4_codes = keep.tile([P, 2 * H], U8, name="w4_codes", align_bytes=64)
         w4_plane = keep.tile([P, H], U8, name="w4_plane", align_bytes=64)
         w1_codes = [keep.tile([P, N], U32, name="w1_codes%d" % a, align_bytes=64) for a in range(2)]
-        w1_plane = [keep.tile([P, N], U8, name="w1_plane%d" % a, align_bytes=64) for a in range(2)]
+        w1_plane = {}
         v_plane = keep.tile([P, S], U8, name="v_plane", align_bytes=64)
         v_rows = keep.tile([P, S], U8, name="v_rows", align_bytes=64)
         v2_plane = keep.tile([P, S2], U8, name="v2_plane", align_bytes=64)
@@ -100,6 +99,7 @@ def tile_list_checkers_endgame_retrieval_kernel(
         tab_plane = place("tab_plane", [P, T], U8, STAGE1 + 4 * KIB)
         w4_raw = place("w4_raw", [P, 2 * H], U8, STAGE1 + 8 * KIB)
         w4_plane_raw = place("w4_plane_raw", [P, H], U8, STAGE1 + 10 * KIB)
+        tab2_plane = place("tab2_plane", [P, T2], U8, SMALL)
         tab2_w = place("tab2_w", [P, 2 * T2], I32, TAB2)
         factor = [place("factor%d" % t, [P, S], F32, FACTOR + 4 * KIB * t) for t in range(4)]
         pages = [place("page%d" % i, [P, T2], F32, PAGES + 8 * KIB * i) for i in range(LAST)]
@@ -129,10 +129,15 @@ def tile_list_checkers_endgame_retrieval_kernel(
         nc.sync.dma_start(w4_raw[:].bitcast(I32), w4_words[0].bitcast(I32))
         for u in range(2):
             load_w1(w1_early[u], N // 2 * u, N // 2 * (u + 1))
+        nc.sync.dma_start(idx2[:], offs2)
+        nc.vector.tensor_copy(tab_plane[0:16, :].bitcast(I32), tab_rows[0:16, :].bitcast(I32))
+        nc.vector.tensor_copy(v_rows[:], tab_plane[:].indirect(idx[:]))
+        nc.vector.tensor_copy(scale_rows(v_plane, 0), scale_rows(v_rows, 0))
+        for q in (2, 1, 3):
+            nc.sync.dma_start(scale_rows(v_plane, q), v_rows[4 * q : 4 * q + 4, :].bitcast(I32))
+        nc.sync.dma_start(tab2_plane[0:32, :].bitcast(I32), tab2_scales.rearrange("a q t -> (a q) t").bitcast(I32))
         nc.sync.dma_start(c3_t[:].rearrange("p (a t) -> p a t", t=4), c3.rearrange("(a p t) -> p a t", a=2, t=4))
         nc.sync.dma_start(c2_t[:].rearrange("p (a t) -> p a t", t=4), c2.rearrange("(a p t) -> p a t", a=2, t=4))
-        nc.sync.dma_start(idx2[:], offs2)
-        nc.sync.dma_start(tab2_plane[0:32, :].bitcast(I32), tab2_scales.rearrange("a q t -> (a q) t").bitcast(I32))
         load_factor(0)
         load_page(0)
         nc.sync.dma_start(idx3[:], offs3)
@@ -152,7 +157,6 @@ def tile_list_checkers_endgame_retrieval_kernel(
             load_page(i)
 
 
-        nc.vector.tensor_copy(tab_plane[0:16, :].bitcast(I32), tab_rows[0:16, :].bitcast(I32))
         identity = keep.tile([P, P], F32, name="identity")
         make_identity(nc, identity[:])
         exponent, sign, root, slope = [keep.tile([P, ROW_TILES], F32, name=name) for name in ("exponent", "sign", "root", "slope")]
@@ -162,10 +166,6 @@ def tile_list_checkers_endgame_retrieval_kernel(
         nc.gpsimd.tensor_tensor(slope[:], c3_t[:], sign[:], MULT)
         nc.gpsimd.tensor_tensor(root[:], slope[:], exponent[:], POW)
         nc.gpsimd.tensor_tensor(slope[:], c2_t[:], sign[:], MULT)
-        nc.vector.tensor_copy(v_rows[:], tab_plane[:].indirect(idx[:]))
-        nc.vector.tensor_copy(scale_rows(v_plane, 0), scale_rows(v_rows, 0))
-        for q in (2, 1, 3):
-            nc.scalar.dma_start(scale_rows(v_plane, q), v_rows[4 * q : 4 * q + 4, :].bitcast(I32))
         nc.vector.tensor_copy(
             w4_codes[:].bitcast(U16).rearrange("p (a t m) -> p a t m", a=2, t=4),
             w4_raw[:].bitcast(U16).rearrange("p (a m t) -> p a t m", a=2, t=4),
@@ -181,7 +181,11 @@ def tile_list_checkers_endgame_retrieval_kernel(
 
         def quantize_w1(a, t0, t1):
             cols = slice(P * t0, P * t1)
-            nc.vector.quantize_mx(out=w1_codes[a][:, cols].bitcast(FP8X4), scales=w1_plane[a][:, cols], in_=grouped[a][:, N * t0 : N * t1])
+            shape, name = [P, P * (t1 - t0)], "w1_plane%d%d" % (a, t0)
+            plane = place(name, shape, U8, SMALL) if t0 else keep.tile(shape, U8, name=name, align_bytes=64)
+            for t in range(t0, t1):
+                w1_plane[4 * a + t] = plane[:, P * (t - t0) : P * (t - t0 + 1)]
+            nc.vector.quantize_mx(out=w1_codes[a][:, cols].bitcast(FP8X4), scales=plane[:], in_=grouped[a][:, N * t0 : N * t1])
 
         nc.vector.tensor_copy(
             w4_plane[:].rearrange("p (a t m) -> p a t m", a=2, t=4),
@@ -192,10 +196,12 @@ def tile_list_checkers_endgame_retrieval_kernel(
         group_w1(0, w1_early[0], 0, P // 2, 0, 4)
         for t0 in (0, 2):
             group_w1(0, w1_early[1], P // 2, P, t0, t0 + 2)
-            quantize_w1(0, t0, t0 + 2)
+        quantize_w1(0, 0, 2)
 
         v2_rows = place("v2_rows", [P, S2], U8, STAGE0 - S2)
         nc.vector.tensor_copy(v2_rows[:], tab2_plane[:].indirect(idx2[:]))
+
+        quantize_w1(0, 2, 4)
 
         lin, values, square, linear, affine, turned, quadratic = {}, {}, {}, {}, {}, {}, {}
 
@@ -216,7 +222,7 @@ def tile_list_checkers_endgame_retrieval_kernel(
                     rhs=v_codes[h][:].bitcast(FP8X4), rhs_scale=v_plane[:, halves[h]], start=True, stop=False,
                 )
                 nc.tensor.matmul_mx(
-                    out=lin[i, h][:], lhsT=w1_codes[a][:, P * t : P * (t + 1)].bitcast(FP8X4), lhsT_scale=w1_plane[a][:, P * t : P * (t + 1)],
+                    out=lin[i, h][:], lhsT=w1_codes[a][:, P * t : P * (t + 1)].bitcast(FP8X4), lhsT_scale=w1_plane[i],
                     rhs=v_codes[h][:].bitcast(FP8X4), rhs_scale=v_plane[:, halves[h]], start=False, stop=True,
                 )
 
@@ -287,16 +293,12 @@ def tile_list_checkers_endgame_retrieval_kernel(
 
         def weave(a, c0, c1):
             half = c0 // (2 * N)
-            dst = woven_part(a, c0, c1)[:, :, 0 : (4, 2)[a]].rearrange("p (g i) t -> p g t i", i=4)
+            dst = woven_part(a, c0, c1)[:, :, 0 : (4, 2)[a]]
             src = stage[1][:, :, c0:c1] if a else stage[0, half][:, :, c0 - 2 * N * half : c1 - 2 * N * half]
-            src = src.rearrange("p t (g i) -> p g t i", i=4)
             if c0 < (3 * N, SCALAR_COLUMNS)[a]:
-                nc.scalar.copy(dst, src)
-            elif a == 0:
-                rows = stage[0, half][:, :, c0 - 2 * N * half : c1 - 2 * N * half]
-                nc.gpsimd.tensor_scalar(woven_part(a, c0, c1), rows.rearrange("p t c -> p c t"), 1.0, 0.0, MULT, ADD)
+                nc.scalar.copy(dst.rearrange("p (g i) t -> p g t i", i=4), src.rearrange("p t (g i) -> p g t i", i=4))
             else:
-                nc.gpsimd.tensor_scalar(dst, src, 1.0, 0.0, MULT, ADD)
+                nc.gpsimd.tensor_scalar(dst, src.rearrange("p t c -> p c t"), 1.0, 0.0, MULT, ADD)
 
         def weave_row(t, c0, c1):
             src = pages[4 + t][:, c0:c1]
@@ -415,8 +417,11 @@ def tile_list_checkers_endgame_retrieval_kernel(
             cuts = [N * c] + [SCALAR_COLUMNS] * (N * c < SCALAR_COLUMNS < N * (c + 1)) + [N * (c + 1)]
             for c0, c1 in reversed(list(zip(cuts, cuts[1:]))):
                 quantize_page(1, c0, c1)
+            if c == order[-1]:
+                for early in order[:2]:
+                    second_product(1, 1, early)
             second_product(0, 1, c)
-        for c in order:
+        for c in order[2:]:
             second_product(1, 1, c)
 
         score_sb = {}

@@ -47,9 +47,10 @@ def slot(base, k):
 
 
 LINEAR_AT = {2: slot(CUBIC, 2), 3: slot(SQUARE, 0), 4: slot(AFFINE, 4), 5: slot(AFFINE, 3), 6: slot(LINEAR, 1), 7: slot(AFFINE, 4)}
-SQUARE_AT = {2: slot(SQUARE, 2), 3: slot(AFFINE, 1), 4: slot(SQUARE, 1), 5: slot(SQUARE, 2), 6: slot(STAGE0, 1), 7: slot(SQUARE, 0)}
+SQUARE_AT = {2: slot(SQUARE, 2), 3: slot(AFFINE, 1), 4: slot(SQUARE, 1), 5: slot(STAGE0, 1), 6: slot(SQUARE, 2), 7: slot(SQUARE, 0)}
 AFFINE_AT = {2: slot(LINEAR, 2), 3: slot(AFFINE, 2), 4: slot(CUBIC, 0), 5: slot(CUBIC, 1), 6: slot(LINEAR, 0), 7: slot(CUBIC, 2)}
-TURNED_AT = {2: slot(AFFINE, 0), 6: STAGE0 + 30 * KIB}
+TURNED_AT = {2: slot(AFFINE, 0), 5: STAGE0 + 30 * KIB}
+SCORE_TILES = (0, 2, 1, 3)
 BANKS_AT = (0, 1, 2, 1, 3, 0, 2, 1)
 BACK_AT = {2: 3, 3: 0, 4: 2, 5: 1, 6: 3, 7: 0}
 
@@ -316,6 +317,15 @@ def tile_list_checkers_endgame_retrieval_kernel(
                 in_=woven_part(a, c0, c1).rearrange("p c t -> p (c t)"),
             )
 
+        v2_codes = {}
+
+        def gather_candidates(a, j0, j1, offset):
+            words = place("v2_codes%d%d" % (a, j0), [P, j1 - j0], U32, offset)
+            window = tab2_w[:, T2 * a : T2 * (a + 1)].bitcast(U32)
+            nc.vector.tensor_copy(words[:], window.indirect(idx2[:, j0 // 16 : j1 // 16]))
+            for j in range(j0, j1, P):
+                v2_codes[a, j // P] = words[:, j - j0 : j - j0 + P]
+
         def terms(i):
             first_product(i)
             summands(i)
@@ -350,6 +360,7 @@ def tile_list_checkers_endgame_retrieval_kernel(
                 products(i + 1)
             if i == LAST - 1:
                 weave(0, 3 * N, T2)
+                gather_candidates(0, 0, 2 * P, slot(SQUARE, 1))
             if i == LAST:
                 codes[0] = place("page_codes0", [P, T2], U32, slot(CUBIC, 1))
                 for c0, c1 in ((0, 2 * N), (2 * N, 3 * N), (3 * N, T2)):
@@ -373,8 +384,8 @@ def tile_list_checkers_endgame_retrieval_kernel(
             if i == 4:
                 for c0, c1 in ((0, 2 * N), (2 * N, 3 * N), (3 * N, T2)):
                     woven[0, c0] = place("woven0%d" % c0, [P, c1 - c0, 4], BF16, PAGES + 8 * c0)
-                for c in range(3):
-                    weave(0, N * c, N * (c + 1))
+                for c0 in range(0, 3 * N, N // 2):
+                    weave(0, c0, c0 + N // 2)
             if i == 5:
                 woven[1, 0] = place("woven_scalar", [P, SCALAR_COLUMNS, 4], BF16, STAGE0)
                 weave(1, 0, 2 * N)
@@ -385,10 +396,8 @@ def tile_list_checkers_endgame_retrieval_kernel(
         weave(1, SCALAR_COLUMNS, T2)
         weave_row(2, SCALAR_COLUMNS, T2)
 
-        v2_codes = place("v2_codes", [P, 2 * S2], U32, AFFINE_AT[LAST - 1])
-        for a, j0, j1 in ((0, 0, 2 * P), (1, 0, S2), (0, 2 * P, S2)):
-            window = tab2_w[:, T2 * a : T2 * (a + 1)].bitcast(U32)
-            nc.vector.tensor_copy(v2_codes[:, S2 * a + j0 : S2 * a + j1], window.indirect(idx2[:, j0 // 16 : j1 // 16]))
+        gather_candidates(0, 2 * P, S2, AFFINE_AT[LAST - 1])
+        gather_candidates(1, 0, S2, AFFINE_AT[LAST - 1] + KIB)
         weave_row(3, SCALAR_COLUMNS, T2)
         for c0, c1 in ((0, N), (N, 2 * N), (2 * N, SCALAR_COLUMNS)):
             weave_row(3, c0, c1)
@@ -401,8 +410,8 @@ def tile_list_checkers_endgame_retrieval_kernel(
                 score[n, c] = psum.tile([P, N], F32, name="score", tag="bank%d" % (4 * (n % 2) + (c if n < 2 else mirror[c])))
             nc.tensor.matmul_mx(
                 out=score[n, c][:],
-                lhsT=v2_codes[:, S2 * a + P * n : S2 * a + P * (n + 1)].bitcast(FP8X4),
-                lhsT_scale=v2_plane[4 * a : P, P * n : P * (n + 1)],
+                lhsT=v2_codes[a, SCORE_TILES[n]].bitcast(FP8X4),
+                lhsT_scale=v2_plane[4 * a : P, P * SCORE_TILES[n] : P * (SCORE_TILES[n] + 1)],
                 rhs=codes[a][:, N * c : N * (c + 1)].bitcast(FP8X4), rhs_scale=page_plane[a][:, N * c : N * (c + 1)],
                 start=first, stop=not first,
             )
@@ -446,5 +455,5 @@ def tile_list_checkers_endgame_retrieval_kernel(
                 cuts = (0, 512, PQ)
             for c0, c1 in zip(cuts, cuts[1:]):
                 cols = slice(c0, c1)
-                nc.scalar.activation(result[:, cols], picked[:, cols], ACT.Tanh, scale=gain_t[:, n : n + 1])
-                nc.sync.dma_start(out[P * n : P * (n + 1), cols], result[:, cols])
+                nc.scalar.activation(result[:, cols], picked[:, cols], ACT.Tanh, scale=gain_t[:, SCORE_TILES[n] : SCORE_TILES[n] + 1])
+                nc.sync.dma_start(out[P * SCORE_TILES[n] : P * (SCORE_TILES[n] + 1), cols], result[:, cols])

@@ -167,10 +167,16 @@ def tile_list_checkers_endgame_retrieval_kernel(
         nc.gpsimd.tensor_tensor(slope[:], c3_t[:], sign[:], MULT)
         nc.gpsimd.tensor_tensor(root[:], slope[:], exponent[:], POW)
         nc.gpsimd.tensor_tensor(slope[:], c2_t[:], sign[:], MULT)
-        nc.vector.tensor_copy(
-            w4_codes[:].bitcast(U16).rearrange("p (a t m) -> p a t m", a=2, t=4),
-            w4_raw[:].bitcast(U16).rearrange("p (a m t) -> p a t m", a=2, t=4),
-        )
+
+        def deal_w4(a):
+            nc.vector.tensor_copy(
+                w4_plane[:, N * a : N * (a + 1)].rearrange("p (t m) -> p t m", t=4),
+                w4_plane_raw[:, N * a : N * (a + 1)].rearrange("p (m t) -> p t m", t=4),
+            )
+            nc.vector.tensor_copy(
+                w4_codes[:].bitcast(U16)[:, N * a : N * (a + 1)].rearrange("p (t m) -> p t m", t=4),
+                w4_raw[:].bitcast(U16)[:, N * a : N * (a + 1)].rearrange("p (m t) -> p t m", t=4),
+            )
 
         grouped = [place("w1_grouped0", [P, 4 * N], BF16, STAGE1 + 12 * KIB)]
 
@@ -188,12 +194,9 @@ def tile_list_checkers_endgame_retrieval_kernel(
                 w1_plane[4 * a + t] = plane[:, P * (t - t0) : P * (t - t0 + 1)]
             nc.vector.quantize_mx(out=w1_codes[a][:, cols].bitcast(FP8X4), scales=plane[:], in_=grouped[a][:, N * t0 : N * t1])
 
-        nc.vector.tensor_copy(
-            w4_plane[:].rearrange("p (a t m) -> p a t m", a=2, t=4),
-            w4_plane_raw[:].rearrange("p (a m t) -> p a t m", a=2, t=4),
-        )
         for h in range(2):
             nc.vector.tensor_copy(v_codes[h][:], tab_w[:].bitcast(U32).indirect(list_half(idx, h)))
+            deal_w4(h)
         group_w1(0, w1_early[0], 0, P // 2, 0, 4)
         for t0 in (0, 2):
             group_w1(0, w1_early[1], P // 2, P, t0, t0 + 2)

@@ -214,6 +214,13 @@ def tile_list_checkers_endgame_retrieval_kernel(
 
         halves = [slice(N * h, N * (h + 1)) for h in range(2)]
 
+        warm = bank(7)
+        for k in range(3):
+            nc.tensor.matmul_mx(
+                out=warm[:], lhsT=w4_raw[:, 0 : 2 * P].bitcast(FP4X4), lhsT_scale=w4_plane_raw[:, 0:P],
+                rhs=v_codes[0][:].bitcast(FP8X4), rhs_scale=v_rows[:, 0:N], start=True, stop=True,
+            )
+
         def term(name, i, offset):
             return place("%s%d" % (name, i), [P, S], F32, offset)
 

@@ -27,7 +27,10 @@ ROW_TILES = H // P
 LAST = ROW_TILES - 1
 KIB = 1024
 QUADRANTS = (0, 2, 1, 3)
-SCALAR_COLUMNS = 1280
+FIRST_SPLIT = 1536
+PAIR_SPLIT = 512
+LAST_SPLIT = 1536
+WEAVE_PIECE = 256
 
 PAGES = 0
 FACTOR = PAGES + 64 * KIB
@@ -50,7 +53,7 @@ LINEAR_AT = {2: slot(CUBIC, 2), 3: slot(SQUARE, 0), 4: slot(AFFINE, 4), 5: slot(
 SQUARE_AT = {2: slot(SQUARE, 2), 3: slot(AFFINE, 1), 4: slot(SQUARE, 1), 5: slot(STAGE0, 1), 6: slot(SQUARE, 2), 7: slot(SQUARE, 0)}
 AFFINE_AT = {2: slot(LINEAR, 2), 3: slot(AFFINE, 2), 4: slot(CUBIC, 0), 5: slot(CUBIC, 1), 6: slot(LINEAR, 0), 7: slot(CUBIC, 2)}
 TURNED_AT = {2: slot(AFFINE, 0), 5: STAGE0 + 30 * KIB}
-SCORE_TILES = (0, 2, 1, 3)
+WOVEN_AT = (PAGES, PAGES + 4 * KIB, PAGES + 8 * KIB, AFFINE_AT[LAST])
 BANKS_AT = (0, 1, 2, 1, 3, 0, 2, 1)
 BACK_AT = {2: 3, 3: 0, 4: 2, 5: 1, 6: 3, 7: 0}
 
@@ -103,7 +106,7 @@ def tile_list_checkers_endgame_retrieval_kernel(
         tab2_plane = place("tab2_plane", [P, T2], U8, SMALL)
         tab2_w = place("tab2_w", [P, 2 * T2], I32, TAB2)
         factor = [place("factor%d" % t, [P, S], F32, FACTOR + 4 * KIB * t) for t in range(4)]
-        pages = [place("page%d" % i, [P, T2], F32, PAGES + 8 * KIB * i) for i in range(LAST)]
+        pages = [place("page%d" % i, [P, T2], F32, PAGES + 8 * KIB * i) for i in range(ROW_TILES)]
 
         nc.gpsimd.memset(w4_plane_raw[:].bitcast(I32), 0)
         nc.vector.memset(tab_plane[:].bitcast(I32), 0)
@@ -154,7 +157,7 @@ def tile_list_checkers_endgame_retrieval_kernel(
         nc.sync.dma_start(idx4[:], offs4)
         with nc.allow_non_contiguous_dma(reason="512 gains, one to a partition"):
             nc.sync.dma_start(gain_t[:], gain.rearrange("(c p) -> p c", p=P))
-        for i in range(5, LAST):
+        for i in range(5, ROW_TILES):
             load_page(i)
 
 
@@ -296,36 +299,26 @@ def tile_list_checkers_endgame_retrieval_kernel(
                 stage[1] = place("stage1", [P, 2, T2], F32, STAGE1)
             nc.sync.dma_start(stage[1][:, i - 4, :], pages[i][:])
 
-        woven = {}
+        woven, codes = {}, {}
 
-        def woven_part(a, c0, c1):
-            start = max(s0 for b, s0 in woven if b == a and s0 <= c0)
-            return woven[a, start][:, c0 - start : c1 - start, :]
-
-        def weave(a, c0, c1):
-            half = c0 // (2 * N)
-            dst = woven_part(a, c0, c1)[:, :, 0 : (4, 2)[a]]
-            src = stage[1][:, :, c0:c1] if a else stage[0, half][:, :, c0 - 2 * N * half : c1 - 2 * N * half]
-            if c0 < (3 * N, SCALAR_COLUMNS)[a]:
-                nc.scalar.copy(dst.rearrange("p (g i) t -> p g t i", i=4), src.rearrange("p t (g i) -> p g t i", i=4))
-            else:
-                nc.gpsimd.tensor_scalar(dst, src.rearrange("p t c -> p c t"), 1.0, 0.0, MULT, ADD)
-
-        def weave_row(t, c0, c1):
-            src = pages[4 + t][:, c0:c1]
-            dst = woven_part(1, c0, c1)[:, :, t]
-            if c0 < SCALAR_COLUMNS:
+        def round_into(engine, dst, src):
+            if engine == "scalar":
                 nc.scalar.copy(dst, src)
             else:
                 nc.gpsimd.tensor_scalar(dst, src, 1.0, 0.0, MULT, ADD)
 
-        codes = {}
+        def weave_rows(engine, dst, src):
+            if engine == "scalar":
+                round_into(engine, dst.rearrange("p (g i) t -> p g t i", i=4), src.rearrange("p t (g i) -> p g t i", i=4))
+            else:
+                round_into(engine, dst, src.rearrange("p t c -> p c t"))
 
-        def quantize_page(a, c0, c1):
-            nc.vector.quantize_mx(
-                out=codes[a][:, c0:c1].bitcast(FP8X4), scales=page_plane[a][:, c0:c1],
-                in_=woven_part(a, c0, c1).rearrange("p c t -> p (c t)"),
-            )
+        def weave_first_pass(engine, c0, c1):
+            half, c = c0 // (2 * N), c0 // N
+            weave_rows(engine, woven[0, c][:, c0 - N * c : c1 - N * c, :], stage[0, half][:, :, c0 - 2 * N * half : c1 - 2 * N * half])
+
+        def weave_row(engine, t, c0, c1):
+            round_into(engine, woven[1][:, c0:c1, t], pages[4 + t][:, c0:c1])
 
         v2_codes = {}
 
@@ -368,13 +361,6 @@ def tile_list_checkers_endgame_retrieval_kernel(
         for i in range(1, ROW_TILES):
             if i < LAST:
                 products(i + 1)
-            if i == LAST - 1:
-                weave(0, 3 * N, T2)
-                gather_candidates(0, 0, 2 * P, slot(SQUARE, 1))
-            if i == LAST:
-                codes[0] = place("page_codes0", [P, T2], U32, slot(CUBIC, 1))
-                for c0, c1 in ((0, 2 * N), (2 * N, 3 * N), (3 * N, T2)):
-                    quantize_page(0, c0, c1)
             scatter(i)
             if i == 4:
                 for half in range(2):
@@ -388,64 +374,59 @@ def tile_list_checkers_endgame_retrieval_kernel(
                     for q in QUADRANTS:
                         rows = 16 * a + 4 * q
                         nc.sync.dma_start(v2_plane[32 * q + 4 * a : 32 * q + 4 * a + 4, :].bitcast(I32), v2_rows[rows : rows + 4, :].bitcast(I32))
-            if i == 4:
-                pages.append(place("page_last", [P, T2], F32, PAGES + 8 * KIB * i))
-                load_page(LAST)
-            if i == 4:
-                for c0, c1 in ((0, 2 * N), (2 * N, 3 * N), (3 * N, T2)):
-                    woven[0, c0] = place("woven0%d" % c0, [P, c1 - c0, 4], BF16, PAGES + 8 * c0)
-                for c0 in range(0, 3 * N, N // 2):
-                    weave(0, c0, c0 + N // 2)
-            if i == 5:
-                woven[1, 0] = place("woven_scalar", [P, SCALAR_COLUMNS, 4], BF16, STAGE0)
-                weave(1, 0, 2 * N)
-                weave(1, 2 * N, SCALAR_COLUMNS)
-            if i == 6:
-                weave_row(2, 0, SCALAR_COLUMNS)
-        woven[1, SCALAR_COLUMNS] = place("woven_gpsimd", [P, T2 - SCALAR_COLUMNS, 4], BF16, PAGES + 8 * KIB)
-        weave(1, SCALAR_COLUMNS, T2)
-        weave_row(2, SCALAR_COLUMNS, T2)
 
-        gather_candidates(0, 2 * P, S2, AFFINE_AT[LAST - 1])
-        gather_candidates(1, 0, S2, AFFINE_AT[LAST - 1] + KIB)
-        weave_row(3, SCALAR_COLUMNS, T2)
-        for c0, c1 in ((0, N), (N, 2 * N), (2 * N, SCALAR_COLUMNS)):
-            weave_row(3, c0, c1)
+        for c in range(4):
+            woven[0, c] = place("woven0%d" % c, [P, N, 4], BF16, WOVEN_AT[c])
+        weave_first_pass("gpsimd", FIRST_SPLIT, T2)
+        for c0 in range(0, FIRST_SPLIT, WEAVE_PIECE):
+            weave_first_pass("scalar", c0, c0 + WEAVE_PIECE)
+        woven[1] = place("woven1", [P, T2, 4], BF16, PAGES + 32 * KIB)
+        for engine, cols in (("scalar", slice(0, PAIR_SPLIT)), ("gpsimd", slice(PAIR_SPLIT, T2))):
+            weave_rows(engine, woven[1][:, cols, 0:2], stage[1][:, :, cols])
+        weave_row("scalar", 2, 0, LAST_SPLIT)
+        weave_row("gpsimd", 2, LAST_SPLIT, T2)
+
+        gather_candidates(0, 0, S2, AFFINE_AT[LAST - 1])
+        gather_candidates(1, 0, S2, AFFINE_AT[LAST - 1] + 2 * KIB)
+        warm = bank(7)
+        for k in range(3):
+            nc.tensor.matmul_mx(
+                out=warm[:], lhsT=v2_codes[0, 0].bitcast(FP8X4), lhsT_scale=v2_plane[:, 0:P],
+                rhs=v_codes[0][:].bitcast(FP8X4), rhs_scale=v_plane[:, halves[0]], start=True, stop=True,
+            )
+        weave_row("gpsimd", 3, LAST_SPLIT, T2)
+        for c0, c1 in ((0, N), (N, 2 * N), (2 * N, LAST_SPLIT)):
+            weave_row("scalar", 3, c0, c1)
 
         score = {}
+        order = (0, 3, 1, 2)
+        mirror = dict(zip(order, reversed(order)))
 
         def second_product(n, a, c):
-            first = a == n // 2
-            if first:
-                score[n, c] = psum.tile([P, N], F32, name="score", tag="bank%d" % (4 * (n % 2) + (c if n < 2 else mirror[c])))
+            if a == 0:
+                score[n, c] = bank(4 * (n % 2) + (c if n < 2 else mirror[c]))
             nc.tensor.matmul_mx(
-                out=score[n, c][:],
-                lhsT=v2_codes[a, SCORE_TILES[n]].bitcast(FP8X4),
-                lhsT_scale=v2_plane[4 * a : P, P * SCORE_TILES[n] : P * (SCORE_TILES[n] + 1)],
-                rhs=codes[a][:, N * c : N * (c + 1)].bitcast(FP8X4), rhs_scale=page_plane[a][:, N * c : N * (c + 1)],
-                start=first, stop=not first,
+                out=score[n, c][:], lhsT=v2_codes[a, n].bitcast(FP8X4), lhsT_scale=v2_plane[4 * a : P, P * n : P * (n + 1)],
+                rhs=codes[a, c][:].bitcast(FP8X4), rhs_scale=page_plane[a][:, N * c : N * (c + 1)], start=a == 0, stop=a == 1,
             )
 
-        order = (0, 1, 3, 2)
-        mirror = dict(zip(order, reversed(order)))
-        for n in range(2):
-            for c in order:
-                second_product(n, 0, c)
-        codes[1] = place("page_codes1", [P, T2], U32, TAB2)
+        def quantize_page(a, c, rows, c0, c1):
+            nc.vector.quantize_mx(
+                out=codes[a, c][:, c0 - N * c : c1 - N * c].bitcast(FP8X4), scales=page_plane[a][:, c0:c1], in_=rows.rearrange("p c t -> p (c t)")
+            )
+
         for c in order:
-            cuts = [N * c] + [SCALAR_COLUMNS] * (N * c < SCALAR_COLUMNS < N * (c + 1)) + [N * (c + 1)]
-            for c0, c1 in reversed(list(zip(cuts, cuts[1:]))):
-                quantize_page(1, c0, c1)
-            if c == order[-1]:
-                for early in order[:2]:
-                    second_product(1, 1, early)
-            second_product(0, 1, c)
-        for c in order[2:]:
-            second_product(1, 1, c)
+            codes[0, c] = place("page_codes0%d" % c, [P, N], U32, TAB2 + 2 * KIB * c)
+            quantize_page(0, c, woven[0, c][:], N * c, N * (c + 1))
+            codes[1, c] = place("page_codes1%d" % c, [P, N], U32, WOVEN_AT[c])
+            quantize_page(1, c, woven[1][:, N * c : N * (c + 1), :], N * c, N * (c + 1))
+            for n in range(2):
+                for a in range(2):
+                    second_product(n, a, c)
 
         score_sb = {}
         for n in range(S2 // P):
-            score_sb[n] = place("score_sb%d" % n, [P, T2], F32, PAGES + 8 * KIB * (2, 3, 5, 7)[n])
+            score_sb[n] = place("score_sb%d" % n, [P, T2], F32, STAGE0 + 8 * KIB * n)
             for c in order if n < 2 else reversed(order):
                 if n == 0 and c in order[2:]:
                     nc.vector.tensor_copy(score_sb[n][:, N * c : N * (c + 1)], score[n, c][:])
@@ -453,8 +434,8 @@ def tile_list_checkers_endgame_retrieval_kernel(
                     nc.scalar.copy(score_sb[n][:, N * c : N * (c + 1)], score[n, c][:])
             if n + 2 < S2 // P:
                 for c in reversed(order):
-                    second_product(n + 2, 1, c)
                     second_product(n + 2, 0, c)
+                    second_product(n + 2, 1, c)
         for n in range(S2 // P):
             picked = place("picked%d" % n, [P, PQ], F32, FACTOR + 4 * KIB * n)
             result = place("result%d" % n, [P, PQ], F32, SQUARE + 4 * KIB * n)
@@ -465,5 +446,5 @@ def tile_list_checkers_endgame_retrieval_kernel(
                 cuts = (0, 512, PQ)
             for c0, c1 in zip(cuts, cuts[1:]):
                 cols = slice(c0, c1)
-                nc.scalar.activation(result[:, cols], picked[:, cols], ACT.Tanh, scale=gain_t[:, SCORE_TILES[n] : SCORE_TILES[n] + 1])
-                nc.sync.dma_start(out[P * SCORE_TILES[n] : P * (SCORE_TILES[n] + 1), cols], result[:, cols])
+                nc.scalar.activation(result[:, cols], picked[:, cols], ACT.Tanh, scale=gain_t[:, n : n + 1])
+                nc.sync.dma_start(out[P * n : P * (n + 1), cols], result[:, cols])

from contextlib import ExitStack

import concourse.mybir as mybir
from concourse.masks import make_identity

K, H, T, S, T2, S2, PQ = 512, 1024, 4096, 1024, 2048, 512, 1024
FLOPS = 2 * (2 * K * H * S) + 2 * H * S2 * T2

F32 = mybir.dt.float32
BF16 = mybir.dt.bfloat16
I32 = mybir.dt.int32
U32 = mybir.dt.uint32
U16 = mybir.dt.uint16
U8 = mybir.dt.uint8
FP8X4 = mybir.dt.float8_e4m3fn_x4
FP4X4 = mybir.dt.float4_e2m1fn_x4
ACT = mybir.ActivationFunctionType
MULT = mybir.AluOpType.mult
ADD = mybir.AluOpType.add
POW = mybir.AluOpType.pow
IS_GE = mybir.AluOpType.is_ge

P = 128
N = 512
LIST_HALF = N // 16
ROW_TILES = H // P
LAST = ROW_TILES - 1
KIB = 1024
QUADRANTS = (0, 2, 1, 3)
FIRST_SPLIT = 1536
PAIR_SPLIT = 512
LAST_SPLIT = 1536
WEAVE_PIECE = 256

PAGES = 0
FACTOR = PAGES + 64 * KIB
SQUARE = FACTOR + 16 * KIB
CUBIC = SQUARE + 12 * KIB
LINEAR = CUBIC + 12 * KIB
AFFINE = LINEAR + 12 * KIB
TAB2 = AFFINE + 21 * KIB
STAGE0 = TAB2 + 16 * KIB + S2
STAGE1 = STAGE0 + 32 * KIB
SMALL = STAGE1 + 24 * KIB
SHARED = STAGE1 + 16 * KIB


def slot(base, k):
    return base + 4 * KIB * k


LINEAR_AT = {2: slot(CUBIC, 2), 3: slot(SQUARE, 0), 4: slot(AFFINE, 4), 5: slot(AFFINE, 3), 6: slot(LINEAR, 1), 7: slot(AFFINE, 4)}
SQUARE_AT = {2: slot(SQUARE, 2), 3: slot(AFFINE, 1), 4: slot(SQUARE, 1), 5: slot(STAGE0, 1), 6: slot(SQUARE, 2), 7: slot(SQUARE, 0)}
AFFINE_AT = {2: slot(LINEAR, 2), 3: slot(AFFINE, 2), 4: slot(CUBIC, 0), 5: slot(CUBIC, 1), 6: slot(LINEAR, 0), 7: slot(CUBIC, 2)}
TURNED_AT = {2: slot(AFFINE, 0), 5: STAGE0 + 30 * KIB}
WOVEN_AT = (PAGES, PAGES + 4 * KIB, PAGES + 8 * KIB, AFFINE_AT[LAST])
BANKS_AT = (0, 1, 2, 1, 3, 0, 2, 1)
BACK_AT = {2: 3, 3: 0, 4: 2, 5: 1, 6: 3, 7: 0}


def tile_list_checkers_endgame_retrieval_kernel(
    tc, tab_words, tab_scales, tab2_words, tab2_scales, w4_words, w4_scales, w1, c2, c3, page0, wgs, gain,
    offs, offs2, offs3, offs4, out,
):
    nc = tc.nc
    with ExitStack() as ctx:
        lists = ctx.enter_context(tc.tile_pool(name="lists", bufs=1))
        keep = ctx.enter_context(tc.tile_pool(name="keep", bufs=1))
        arena = ctx.enter_context(tc.tile_pool(name="arena", bufs=1))
        psum = ctx.enter_context(tc.psum_pool(name="psum", bufs=1))

        def place(name, shape, dtype, offset):
            return arena.tile(shape, dtype, name=name, offset=offset, align_bytes=64)

        idx = lists.tile([P, S // 16], U16, name="idx")
        idx2 = lists.tile([P, S2 // 16], U16, name="idx2")
        idx3 = lists.tile([P, S // 16], U16, name="idx3")
        idx4 = lists.tile([P, PQ // 16], U16, name="idx4")

        def list_half(tile, h):
            return tile[:, LIST_HALF * h : LIST_HALF * (h + 1)]

        def scale_rows(tile, q, count=4):
            return tile[32 * q : 32 * q + count, :].bitcast(I32)

        c2_t = keep.tile([P, ROW_TILES], F32, name="c2_t")
        c3_t = keep.tile([P, ROW_TILES], F32, name="c3_t")
        gain_t = keep.tile([P, S2 // P], F32, name="gain_t")
        w4_codes = keep.tile([P, 2 * H], U8, name="w4_codes", align_bytes=64)
        w4_plane = keep.tile([P, H], U8, name="w4_plane", align_bytes=64)
        w1_codes = [keep.tile([P, N], U32, name="w1_codes%d" % a, align_bytes=64) for a in range(2)]
        w1_plane = {}
        v_plane = keep.tile([P, S], U8, name="v_plane", align_bytes=64)
        v_rows = keep.tile([P, S], U8, name="v_rows", align_bytes=64)
        v2_plane = keep.tile([P, S2], U8, name="v2_plane", align_bytes=64)
        v_codes = [keep.tile([P, N], U32, name="v_codes%d" % h, align_bytes=64) for h in range(2)]
        page_plane = [keep.tile([P, T2], U8, name="page_plane%d" % a, align_bytes=64) for a in range(2)]

        tab_w = place("tab_w", [P, T], I32, STAGE0 - S2)
        w1_early = [place("w1_early%d" % u, [P, 4, N // 2], F32, STAGE0 + (16 + 4 * u) * KIB) for u in range(2)]
        w1_late = place("w1_late", [P, 4, N], F32, AFFINE + 2 * KIB)
        tab_rows = place("tab_rows", [P, T], U8, STAGE1)
        tab_plane = place("tab_plane", [P, T], U8, STAGE1 + 4 * KIB)
        w4_raw = place("w4_raw", [P, 2 * H], U8, STAGE1 + 8 * KIB)
        w4_plane_raw = place("w4_plane_raw", [P, H], U8, STAGE1 + 10 * KIB)
        tab2_plane = place("tab2_plane", [P, T2], U8, SMALL)
        tab2_w = place("tab2_w", [P, 2 * T2], I32, TAB2)
        factor = [place("factor%d" % t, [P, S], F32, FACTOR + 4 * KIB * t) for t in range(4)]
        pages = [place("page%d" % i, [P, T2], F32, PAGES + 8 * KIB * i) for i in range(ROW_TILES)]

        nc.gpsimd.memset(w4_plane_raw[:].bitcast(I32), 0)
        nc.vector.memset(tab_plane[:].bitcast(I32), 0)
        nc.vector.memset(v_plane[:].bitcast(I32), 0)
        nc.gpsimd.memset(tab2_plane[:].bitcast(I32), 0)
        nc.gpsimd.memset(v2_plane[:].bitcast(I32), 0)

        def load_w1(tile, c0, c1):
            nc.sync.dma_start(tile[:], w1[:, c0:c1].rearrange("(p j) c -> p j c", j=4))

        def load_factor(t):
            for g in QUADRANTS:
                nc.sync.dma_start(factor[t][32 * g : 32 * (g + 1), :], wgs.rearrange("(q t) j -> t q j", t=4)[t])

        def load_page(i):
            a, t = divmod(i, 4)
            nc.sync.dma_start(pages[i][:], page0[N * a : N * (a + 1), :].rearrange("(p t) c -> t p c", t=4)[t])

        nc.sync.dma_start(idx[:], offs)
        nc.sync.dma_start(tab_rows[0:16, :].bitcast(I32), tab_scales[0].bitcast(I32))
        nc.sync.dma_start(tab_w[:], tab_words[0].rearrange("p t i -> p (t i)").bitcast(I32))
        for q in QUADRANTS:
            nc.sync.dma_start(scale_rows(w4_plane_raw, q), w4_scales[0, 4 * q : 4 * q + 4, :].bitcast(I32))
        nc.sync.dma_start(w4_raw[:].bitcast(I32), w4_words[0].bitcast(I32))
        for u in range(2):
            load_w1(w1_early[u], N // 2 * u, N // 2 * (u + 1))
        nc.sync.dma_start(idx2[:], offs2)
        nc.vector.tensor_copy(tab_plane[0:16, :].bitcast(I32), tab_rows[0:16, :].bitcast(I32))
        nc.vector.tensor_copy(v_rows[:], tab_plane[:].indirect(idx[:]))
        nc.vector.tensor_copy(scale_rows(v_plane, 0), scale_rows(v_rows, 0))
        for q in (2, 1, 3):
            nc.sync.dma_start(scale_rows(v_plane, q), v_rows[4 * q : 4 * q + 4, :].bitcast(I32))
        nc.sync.dma_start(tab2_plane[0:32, :].bitcast(I32), tab2_scales.rearrange("a q t -> (a q) t").bitcast(I32))
        nc.sync.dma_start(c3_t[:].rearrange("p (a t) -> p a t", t=4), c3.rearrange("(a p t) -> p a t", a=2, t=4))
        nc.sync.dma_start(c2_t[:].rearrange("p (a t) -> p a t", t=4), c2.rearrange("(a p t) -> p a t", a=2, t=4))
        load_factor(0)
        load_page(0)
        nc.sync.dma_start(idx3[:], offs3)
        load_factor(1)
        load_w1(w1_late, N, H)
        load_page(1)
        load_factor(2)
        load_factor(3)
        for i in range(2, 5):
            load_page(i)
        for a in range(2):
            nc.sync.dma_start(tab2_w[:, T2 * a : T2 * (a + 1)], tab2_words[a].rearrange("p t i -> p (t i)").bitcast(I32))
        nc.sync.dma_start(idx4[:], offs4)
        with nc.allow_non_contiguous_dma(reason="512 gains, one to a partition"):
            nc.sync.dma_start(gain_t[:], gain.rearrange("(c p) -> p c", p=P))
        for i in range(5, ROW_TILES):
            load_page(i)


        identity = keep.tile([P, P], F32, name="identity")
        make_identity(nc, identity[:])
        exponent, sign, root, slope = [keep.tile([P, ROW_TILES], F32, name=name) for name in ("exponent", "sign", "root", "slope")]
        nc.gpsimd.memset(exponent[:], 0.5)
        nc.gpsimd.tensor_scalar(slope[:], c3_t[:], 0.0, 2.0, IS_GE, MULT)
        nc.gpsimd.tensor_scalar(sign[:], slope[:], 1.0, -1.0, MULT, ADD)
        nc.gpsimd.tensor_tensor(slope[:], c3_t[:], sign[:], MULT)
        nc.gpsimd.tensor_tensor(root[:], slope[:], exponent[:], POW)
        nc.gpsimd.tensor_tensor(slope[:], c2_t[:], sign[:], MULT)

        def deal_w4(a):
            nc.vector.tensor_copy(
                w4_plane[:, N * a : N * (a + 1)].rearrange("p (t m) -> p t m", t=4),
                w4_plane_raw[:, N * a : N * (a + 1)].rearrange("p (m t) -> p t m", t=4),
            )
            nc.vector.tensor_copy(
                w4_codes[:].bitcast(U16)[:, N * a : N * (a + 1)].rearrange("p (t m) -> p t m", t=4),
                w4_raw[:].bitcast(U16)[:, N * a : N * (a + 1)].rearrange("p (m t) -> p t m", t=4),
            )

        grouped = [place("w1_grouped0", [P, 4 * N], BF16, STAGE1 + 12 * KIB)]

        def group_w1(a, raw, m0, m1, t0, t1):
            nc.scalar.copy(
                grouped[a][:].rearrange("p (t m j) -> p m j t", m=P, j=4)[:, m0:m1, :, t0:t1],
                raw[:].rearrange("p j (m t) -> p m j t", t=4)[:, :, :, t0:t1],
            )

        def quantize_w1(a, t0, t1):
            cols = slice(P * t0, P * t1)
            shape, name = [P, P * (t1 - t0)], "w1_plane%d%d" % (a, t0)
            plane = place(name, shape, U8, SMALL) if t0 else keep.tile(shape, U8, name=name, align_bytes=64)
            for t in range(t0, t1):
                w1_plane[4 * a + t] = plane[:, P * (t - t0) : P * (t - t0 + 1)]
            nc.vector.quantize_mx(out=w1_codes[a][:, cols].bitcast(FP8X4), scales=plane[:], in_=grouped[a][:, N * t0 : N * t1])

        for h in range(2):
            nc.vector.tensor_copy(v_codes[h][:], tab_w[:].bitcast(U32).indirect(list_half(idx, h)))
            deal_w4(h)
        group_w1(0, w1_early[0], 0, P // 2, 0, 4)
        for t0 in (0, 2):
            group_w1(0, w1_early[1], P // 2, P, t0, t0 + 2)
        quantize_w1(0, 0, 2)

        v2_rows = place("v2_rows", [P, S2], U8, STAGE0 - S2)
        nc.vector.tensor_copy(v2_rows[:], tab2_plane[:].indirect(idx2[:]))

        quantize_w1(0, 2, 4)

        lin, values, square, linear, affine, turned, quadratic = {}, {}, {}, {}, {}, {}, {}

        def bank(b):
            return psum.tile([P, N], F32, name="bank", tag="bank%d" % b)

        halves = [slice(N * h, N * (h + 1)) for h in range(2)]

        warm = bank(7)
        for k in range(3):
            nc.tensor.matmul_mx(
                out=warm[:], lhsT=w4_raw[:, 0 : 2 * P].bitcast(FP4X4), lhsT_scale=w4_plane_raw[:, 0:P],
                rhs=v_codes[0][:].bitcast(FP8X4), rhs_scale=v_rows[:, 0:N], start=True, stop=True,
            )

        def term(name, i, offset):
            return place("%s%d" % (name, i), [P, S], F32, offset)

        def first_product(i):
            a, t = divmod(i, 4)
            for h in range(2):
                lin[i, h] = bank(2 * BANKS_AT[i] + h)
                nc.tensor.matmul_mx(
                    out=lin[i, h][:], lhsT=w4_codes[:, 2 * P * i : 2 * P * (i + 1)].bitcast(FP4X4), lhsT_scale=w4_plane[:, P * i : P * (i + 1)],
                    rhs=v_codes[h][:].bitcast(FP8X4), rhs_scale=v_plane[:, halves[h]], start=True, stop=False,
                )
                nc.tensor.matmul_mx(
                    out=lin[i, h][:], lhsT=w1_codes[a][:, P * t : P * (t + 1)].bitcast(FP8X4), lhsT_scale=w1_plane[i],
                    rhs=v_codes[h][:].bitcast(FP8X4), rhs_scale=v_plane[:, halves[h]], start=False, stop=True,
                )

        def inner_affine(i, offset):
            affine[i] = term("affine", i, offset)
            for h in range(2):
                nc.scalar.activation(affine[i][:, halves[h]], lin[i, h][:], ACT.Identity, bias=c2_t[:, i : i + 1], scale=c3_t[:, i : i + 1])

        def times_lin(i, offset):
            product = term("inner", i, offset)
            for h in range(2):
                nc.vector.tensor_tensor(product[:, halves[h]], affine[i][:, halves[h]], lin[i, h][:], MULT)
            return product

        def summands(i):
            col = slice(i, i + 1)
            square[i], affine[i], linear[i] = term("square", i, SQUARE_AT[i]), term("affine", i, AFFINE_AT[i]), term("linear", i, LINEAR_AT[i])
            for h in range(2):
                nc.scalar.activation(square[i][:, halves[h]], lin[i, h][:], ACT.Square, scale=root[:, col])
                nc.scalar.activation(affine[i][:, halves[h]], lin[i, h][:], ACT.Identity, bias=sign[:, col], scale=slope[:, col])
            for h in range(2):
                nc.scalar.activation(linear[i][:, halves[h]], lin[i, h][:], ACT.Copy, scale=sign[:, col])

        def sum_turned(i):
            turned[i] = term("turned", i, TURNED_AT.get(i, SQUARE_AT[i]))
            sums = [bank(2 * BANKS_AT[i] + h) for h in range(2)]
            for b in range(S // P):
                block = slice(P * b, P * (b + 1))
                dst = sums[b // 4][:, P * (b % 4) : P * (b % 4 + 1)]
                nc.tensor.matmul(dst, square[i][:, block], identity[:], start=True, stop=False, is_transpose=True)
                nc.tensor.matmul(dst, affine[i][:, block], identity[:], start=False, stop=True, is_transpose=True)
            for h in range(2):
                nc.scalar.copy(turned[i][:, halves[h]], sums[h][:])

        def turn_back(i):
            quadratic[i] = term("quadratic", i, AFFINE_AT[i])
            backs = [bank(2 * BACK_AT[i] + h) for h in range(2)]
            for b in range(S // P):
                nc.tensor.transpose(backs[b // 4][:, P * (b % 4) : P * (b % 4 + 1)], turned[i][:, P * b : P * (b + 1)], identity[:])
            for h in range(2):
                nc.scalar.copy(quadratic[i][:, halves[h]], backs[h][:])

        def products(i):
            values[i] = linear[i] if i == 1 else term("values", i, AFFINE_AT.get(i - 1, SHARED))
            nc.gpsimd.tensor_tensor(values[i][:], linear[i][:], factor[i % 4][:], MULT)
            nc.gpsimd.tensor_tensor(values[i][:], values[i][:], quadratic[i][:], MULT)

        def scatter(i):
            nc.vector.tensor_copy(pages[i][:].indirect(idx3[:]), values[i][:])

        stage = {}

        def stage_first_pass(half):
            stage[0, half] = place("stage0%d" % half, [P, 4, 2 * N], F32, STAGE0 + 16 * KIB * half)
            for t in range(4):
                nc.sync.dma_start(stage[0, half][:, t, :], pages[t][:, 2 * N * half : 2 * N * (half + 1)])

        def stage_page(i):
            if i == 4:
                stage[1] = place("stage1", [P, 2, T2], F32, STAGE1)
            nc.sync.dma_start(stage[1][:, i - 4, :], pages[i][:])

        woven, codes = {}, {}

        def round_into(engine, dst, src):
            if engine == "scalar":
                nc.scalar.copy(dst, src)
            else:
                nc.gpsimd.tensor_scalar(dst, src, 1.0, 0.0, MULT, ADD)

        def weave_rows(engine, dst, src):
            if engine == "scalar":
                round_into(engine, dst.rearrange("p (g i) t -> p g t i", i=4), src.rearrange("p t (g i) -> p g t i", i=4))
            else:
                round_into(engine, dst, src.rearrange("p t c -> p c t"))

        def weave_first_pass(engine, c0, c1):
            half, c = c0 // (2 * N), c0 // N
            weave_rows(engine, woven[0, c][:, c0 - N * c : c1 - N * c, :], stage[0, half][:, :, c0 - 2 * N * half : c1 - 2 * N * half])

        def weave_row(engine, t, c0, c1):
            round_into(engine, woven[1][:, c0:c1, t], pages[4 + t][:, c0:c1])

        v2_codes = {}

        def gather_candidates(a, j0, j1, offset):
            words = place("v2_codes%d%d" % (a, j0), [P, j1 - j0], U32, offset)
            window = tab2_w[:, T2 * a : T2 * (a + 1)].bitcast(U32)
            nc.vector.tensor_copy(words[:], window.indirect(idx2[:, j0 // 16 : j1 // 16]))
            for j in range(j0, j1, P):
                v2_codes[a, j // P] = words[:, j - j0 : j - j0 + P]

        def terms(i):
            first_product(i)
            summands(i)
            sum_turned(i)
            turn_back(i)

        first_product(0)
        inner_affine(0, slot(AFFINE, 4))
        first_product(1)
        inner_affine(1, slot(AFFINE, 3))
        cubic = times_lin(0, slot(CUBIC, 0))
        for h in range(2):
            nc.vector.scalar_tensor_tensor(cubic[:, halves[h]], cubic[:, halves[h]], 1.0, lin[0, h][:], ADD, MULT)
        for h in range(2):
            nc.gpsimd.tensor_tensor(affine[0][:, halves[h]], cubic[:, halves[h]], factor[0][:, halves[h]], MULT)
        inner = times_lin(1, slot(CUBIC, 1))
        linear[1] = term("linear", 1, slot(LINEAR, 0))
        for h in range(2):
            nc.scalar.copy(linear[1][:, halves[h]], lin[1, h][:])
        quadratic[1] = term("quadratic", 1, slot(AFFINE, 3))
        nc.scalar.activation(quadratic[1][:], inner[:], ACT.Identity, bias=1.0)
        for h in range(2):
            nc.vector.tensor_copy(pages[0][:].indirect(list_half(idx3, h)), affine[0][:, halves[h]])
        products(1)
        grouped.append(place("w1_grouped1", [P, 4 * N], BF16, SHARED))
        group_w1(1, w1_late, 0, P, 0, 4)
        quantize_w1(1, 0, 4)
        terms(2)
        terms(3)
        for i in range(1, ROW_TILES):
            if i < LAST:
                products(i + 1)
            scatter(i)
            if i == 4:
                for half in range(2):
                    stage_first_pass(half)
            if i in (4, 5):
                stage_page(i)
            if i + 3 < ROW_TILES:
                terms(i + 3)
            if i == 2:
                for a in range(2):
                    for q in QUADRANTS:
                        rows = 16 * a + 4 * q
                        nc.sync.dma_start(v2_plane[32 * q + 4 * a : 32 * q + 4 * a + 4, :].bitcast(I32), v2_rows[rows : rows + 4, :].bitcast(I32))

        for c in range(4):
            woven[0, c] = place("woven0%d" % c, [P, N, 4], BF16, WOVEN_AT[c])
        weave_first_pass("gpsimd", FIRST_SPLIT, T2)
        for c0 in range(0, FIRST_SPLIT, WEAVE_PIECE):
            weave_first_pass("scalar", c0, c0 + WEAVE_PIECE)
        woven[1] = place("woven1", [P, T2, 4], BF16, PAGES + 32 * KIB)
        for engine, cols in (("scalar", slice(0, PAIR_SPLIT)), ("gpsimd", slice(PAIR_SPLIT, T2))):
            weave_rows(engine, woven[1][:, cols, 0:2], stage[1][:, :, cols])
        weave_row("scalar", 2, 0, LAST_SPLIT)
        weave_row("gpsimd", 2, LAST_SPLIT, T2)

        gather_candidates(0, 0, S2, AFFINE_AT[LAST - 1])
        gather_candidates(1, 0, S2, AFFINE_AT[LAST - 1] + 2 * KIB)
        warm = bank(7)
        for k in range(3):
            nc.tensor.matmul_mx(
                out=warm[:], lhsT=v2_codes[0, 0].bitcast(FP8X4), lhsT_scale=v2_plane[:, 0:P],
                rhs=v_codes[0][:].bitcast(FP8X4), rhs_scale=v_plane[:, halves[0]], start=True, stop=True,
            )
        weave_row("gpsimd", 3, LAST_SPLIT, T2)
        for c0, c1 in ((0, N), (N, 2 * N), (2 * N, LAST_SPLIT)):
            weave_row("scalar", 3, c0, c1)

        score = {}
        order = (0, 3, 1, 2)
        mirror = dict(zip(order, reversed(order)))

        def second_product(n, a, c):
            if a == 0:
                score[n, c] = bank(4 * (n % 2) + (c if n < 2 else mirror[c]))
            nc.tensor.matmul_mx(
                out=score[n, c][:], lhsT=v2_codes[a, n].bitcast(FP8X4), lhsT_scale=v2_plane[4 * a : P, P * n : P * (n + 1)],
                rhs=codes[a, c][:].bitcast(FP8X4), rhs_scale=page_plane[a][:, N * c : N * (c + 1)], start=a == 0, stop=a == 1,
            )

        def quantize_page(a, c, rows, c0, c1):
            nc.vector.quantize_mx(
                out=codes[a, c][:, c0 - N * c : c1 - N * c].bitcast(FP8X4), scales=page_plane[a][:, c0:c1], in_=rows.rearrange("p c t -> p (c t)")
            )

        for c in order:
            codes[0, c] = place("page_codes0%d" % c, [P, N], U32, TAB2 + 2 * KIB * c)
            quantize_page(0, c, woven[0, c][:], N * c, N * (c + 1))
            codes[1, c] = place("page_codes1%d" % c, [P, N], U32, WOVEN_AT[c])
            quantize_page(1, c, woven[1][:, N * c : N * (c + 1), :], N * c, N * (c + 1))
            for n in range(2):
                for a in range(2):
                    second_product(n, a, c)

        score_sb = {}
        for n in range(S2 // P):
            score_sb[n] = place("score_sb%d" % n, [P, T2], F32, STAGE0 + 8 * KIB * n)
            for c in order if n < 2 else reversed(order):
                if n == 0 and c in order[2:]:
                    nc.vector.tensor_copy(score_sb[n][:, N * c : N * (c + 1)], score[n, c][:])
                else:
                    nc.scalar.copy(score_sb[n][:, N * c : N * (c + 1)], score[n, c][:])
            if n + 2 < S2 // P:
                for c in reversed(order):
                    second_product(n + 2, 0, c)
                    second_product(n + 2, 1, c)
        for n in range(S2 // P):
            picked = place("picked%d" % n, [P, PQ], F32, FACTOR + 4 * KIB * n)
            result = place("result%d" % n, [P, PQ], F32, SQUARE + 4 * KIB * n)
            cuts = (0, 512, 768, PQ) if n == S2 // P - 1 else (0, PQ)
            for c0, c1 in zip(cuts, cuts[1:]):
                nc.vector.tensor_copy(picked[:, c0:c1], score_sb[n][:].indirect(idx4[:, c0 // 16 : c1 // 16]))
            if n == S2 // P - 2:
                cuts = (0, 512, PQ)
            for c0, c1 in zip(cuts, cuts[1:]):
                cols = slice(c0, c1)
                nc.scalar.activation(result[:, cols], picked[:, cols], ACT.Tanh, scale=gain_t[:, n : n + 1])
                nc.sync.dma_start(out[P * n : P * (n + 1), cols], result[:, cols])
